import numpy as np, ml_dtypes
CORES = [40,64,80,88,96,104,120,144]
N = 8
BF = ml_dtypes.bfloat16
def gentries(a):
    return np.ascontiguousarray(a.reshape(8, 16, -1).transpose(0, 2, 1)).reshape(8, -1)
def gtable(e):
    e = np.asarray(e); return np.ascontiguousarray(e.reshape(8, -1, 16).transpose(0, 2, 1)).reshape(128, -1).astype(np.int32)
W, S, U, H, C, R, TH, SH = 4096, 1024, 256, 2, 8, 3, 260, 8
B, LC = W // C, 3
def two(rng, lo, hi, shape):
    return np.where(rng.random(shape) < 0.5, lo, hi)
def pack(mu, fr, a, mix, s):
    return {"mu": np.ascontiguousarray(mu.reshape(N, 128, W)).astype(np.float32).astype(BF),
            "fr": np.ascontiguousarray(fr.reshape(N, 128, R * U)).astype(np.float32).astype(BF),
            "a0": np.ascontiguousarray(a.transpose(0, 1, 3, 2, 4)).reshape(N, 128, 16 * C).astype(np.float32).astype(BF),
            "mix": np.ascontiguousarray(mix.transpose(0, 1, 3, 2)).reshape(N, 128, S).astype(np.int32),
            "s0": np.stack([gtable(v) for v in s])}
def frames(rng, mu, mix, s):
    ri = np.arange(N)[:, None, None, None]; gi = np.arange(8)[None, :, None, None]
    st = (s[..., None] + (np.arange(R) * (H - 1)) // 2 + rng.integers(0, H, (N, 8, U, R))) & (S - 1)
    w = mix[ri, gi, st, rng.integers(0, 16, st.shape)]
    x = mu[ri, gi, :, w]
    x = np.where(rng.random((N, 8, U, R, 1)) < 0.5, np.clip(x + rng.integers(-3, 4, x.shape), -8, 7), rng.integers(-8, 8, x.shape))
    return np.ascontiguousarray(x.transpose(0, 1, 4, 3, 2))
def parts(rng):
    mu = rng.integers(-8, 8, (N, 8, 16, W))
    a = 64 * np.eye(16, dtype=np.int64) + rng.integers(-6, 7, (N, 8, C, 16, 16))
    wgt = np.exp2(rng.integers(0, 6, (8, C))); wgt[0] = 1.0; wgt[0, int(rng.integers(0, C))] = 32.0; wgt[1] = 1.0
    cum = np.add.accumulate(wgt, axis=1)
    v = rng.random((N, 8, S * 16, 1)) * cum[None, :, None, C - 1:]
    cl = np.minimum(np.add.reduce((v >= cum[None, :, None, :]).astype(np.int64), axis=-1), C - 1)
    mix = (cl * B + rng.integers(0, B, cl.shape)).reshape(N, 8, S, 16)
    s = rng.integers(0, S, (N, 8, U))
    return mu, a, mix, s
def setup_inputs(rng):
    mu, a, mix, s = parts(rng)
    return pack(mu, frames(rng, mu, mix, s), a, mix, s)
def setup_inputs_spread(rng):
    mu, a, mix, s = parts(rng)
    sz = np.array([1.0, 1.0, 0.5, 0.25, 0.125, 0.0])
    mu = np.floor(mu * rng.choice(sz, (N, 8, 1, W))).astype(np.int64)
    a = np.eye(16, dtype=np.int64) * rng.integers(16, 128, (N, 8, C, 1, 16)) + rng.integers(-127, 128, a.shape) * (rng.random(a.shape) < 0.0625)
    a = np.clip(a, -127, 127)
    mix[:, ::2] = np.minimum((W * rng.random((N, 4, S, 16)) ** 3).astype(np.int64), W - 1)
    s[:, 1::2] = np.minimum((S * rng.random((N, 4, U)) ** 4).astype(np.int64), S - 1)
    x = frames(rng, mu, mix, s)
    x = np.floor(x * rng.choice(sz, (N, 8, 1, R, U))).astype(np.int64)
    return pack(mu, x, a, mix, s)
def setup_inputs_ends(rng):
    mu = two(rng, -8, 7, (N, 8, 16, W)); x = two(rng, -8, 7, (N, 8, 16, R, U)); a = two(rng, -127, 127, (N, 8, C, 16, 16))
    kind = rng.integers(0, 3, (N, 8, S, 1))
    mix = np.where(kind == 0, 0, np.where(kind == 1, W - 1, two(rng, 0, W - 1, (N, 8, S, 16))))
    s = two(rng, 0, S - 1, (N, 8, U))
    mix[:, 7] = W - 1; mu[:, 7, :, W - 1] = -8; a[:, 7, C - 1] = 127; x[:, 7, :, 0::2] = 7; x[:, 7, :, 1::2] = -8
    mu[:, 6, :, 0] = -8; mu[:, 6, :, W - 1] = -8; a[:, 6, 0] = 127; a[:, 6, C - 1] = 127; x[:, 6] = two(rng, -8, 7, (N, 1, R, U))
    mix[:, 4] = W - 1; mu[:, 4, :, W - 1] = -8; a[:, 4, C - 1] = -127; x[:, 4] = -8
    return pack(mu, x, a, mix, s)
def setup_inputs_corners(rng):
    mu, a, mix, s = parts(rng); eye = 64 * np.eye(16, dtype=np.int64); low = (np.arange(16) < 8)[:, None]; slot = np.arange(16)[None, None, :]
    s[:, 2] = ((np.arange(N) & 1) * (S - 1))[:, None]
    mix[:, 3] = rng.choice(np.array([0, B - 1, B, W - 1]), (N, S, 1)); a[:, 3] = two(rng, -127, 127, (N, C, 16, 16))
    mix[:, 4] = rng.choice(np.concatenate([np.arange(C) * B, np.arange(C) * B + B - 1]), (N, S, 16))
    a[:, 5] = 0
    mu[:, 6] = rng.integers(-1, 2, (N, 16, W))
    s[:, 7] = rng.choice(np.array([0, 1, 2, 3, S - 2, S - 1]), (N, U))
    q = np.arange(W)[None, :] & 3
    mu[:, 0] = np.where(q == 0, 6, np.where(q == 1, -7, np.where(q == 2, np.where(low, 6, -8), np.where(low, -7, 7))))
    a[:, 0] = eye; ty = ((np.arange(S) // (H - 1)) & 1)[None, :, None]
    k = rng.integers(0, 16, (N, S, 1)); k[:, ::8] = 15; k[:, 3::8] = 0
    mix[:, 0] = 4 * rng.integers(0, W // 4, (N, S, 16)) + ty + 2 * (slot < k)
    s[:, 0] = (H - 1) * rng.integers(0, S // (H - 1), (N, U)); s[:, 0, :16] = S - (H - 1); s[:, 0, 16:32] = 0
    ft = rng.integers(0, 16, (N, 1, W))
    mu[:, 1] = -8 + ((np.arange(16)[None, :, None] == ft) & ((np.arange(W) & 1) == 1)[None, None, :]).astype(np.int64)
    a[:, 1] = eye; k = np.where(rng.random((N, S, 1)) < 0.5, rng.integers(1, 16, (N, S, 1)), 16)
    mix[:, 1] = 2 * rng.integers(0, W // 2, (N, S, 16)) + (slot < k)
    x = frames(rng, mu, mix, s)
    x[:, 6] = rng.integers(-1, 2, (N, 16, R, U)); x[:, 1] = -8
    cur = s[:, 0].copy(); u4 = (np.arange(U) & 3)[None, :]
    for t in range(R):
        mv = np.where(u4 == 0, 1, np.where(u4 == 1, 0, rng.integers(0, 2, (N, U))))
        x[:, 0, :, t] = np.where((((cur // (H - 1)) + mv) & 1) == 0, 7, -8)[:, None, :]
        cur = (cur + mv * (H - 1)) & (S - 1)
    return pack(mu, x, a, mix, s)
def setup_inputs_crowd(rng):
    mu, a, mix, s = parts(rng); T = N * U
    mix = ((np.arange(S) >> 4) & (C - 1))[None, None, :, None] * B + rng.integers(0, B, (N, 8, S, 16))
    kinds = [(1, TH - 1), (2, TH - 2), (3, TH - 3), (0, TH), (1, TH - 2)]
    for g in range(8):
        n = np.zeros((C // 2, 2), np.int64)
        if g == 0: n[C // 2 - 1, 1] = T
        elif g == 1: n[0, 0] = T - 1; n[C // 2 - 1, 1] = 1
        elif g == 2: n[0] = (TH, TH - 1); n[C // 2 - 1, 1] = T - 2 * TH + 1
        elif g in (3, 4):
            v = TH - 1 if g == 3 else TH; b = 2 * int(rng.integers(0, C // 4))
            h = v // 2 + int(rng.integers(-(v // 4), v // 4 + 1)); i = int(rng.integers(1, h)); j = int(rng.integers(1, v - h))
            n[b] = (i, h - i); n[b + 1] = (j, v - h - j)
            n[(b + C // 4) % (C // 2) + int(rng.integers(0, 2)), int(rng.integers(0, 2))] = T - v
        else:
            p = rng.permutation(C // 2)
            for i in range(3):
                v = kinds[(g + i) % 5]; n[p[i]] = v if rng.random() < 0.5 else v[::-1]
            n[p[3], int(rng.integers(0, 2))] = T - int(np.add.reduce(n.reshape(-1)))
        cl = rng.permutation(np.repeat(np.arange(C), n.reshape(-1))).reshape(N, U)
        s[:, g] = 16 * (cl + C * rng.integers(0, S // (16 * C), (N, U))) + rng.integers(0, 16 - R * (H - 1), (N, U))
    return pack(mu, frames(rng, mu, mix, s), a, mix, s)
def setup_inputs_tally(rng):
    mu, a, mix, s = parts(rng); T = N * U
    mix = ((np.arange(S) >> 4) & (C - 1))[None, None, :, None] * B + rng.integers(0, B, (N, 8, S, 16))
    for g in range(8):
        n = np.zeros(C, np.int64)
        if g in (0, 1, 2, 3, 7):
            q = N - 1 if g == 7 else int(rng.integers(0, N))
            c = C - 1 if g == 7 else 2 * int(rng.integers(0, C // 2)) + (1, 0, 0, 1)[g]
            m = TH - U - 1 if g == 3 else TH - U
            v = rng.choice(np.array([i for i in range(C) if i != c and (g != 3 or i != (c ^ 1))]), (N - 1) * U)
            v[:m] = c
            if g == 3: v[m] = c ^ 1
            v = rng.permutation(v).reshape(N - 1, U)
            cl = np.concatenate([v[:q], np.full((1, U), c, np.int64), v[q:]], axis=0)
        elif g == 4:
            o = 4 * int(rng.integers(0, C // 4)); p = (o + 4) % C; b = o + 2 * int(rng.integers(0, 2)); k = T - 2 * TH + 2
            n[b + int(rng.integers(0, 2))] = TH - 1; n[b ^ 2] = k // 2; n[(b ^ 2) + 1] = k - k // 2
            i = int(rng.integers(1, TH // 3)); j = int(rng.integers(1, TH // 3))
            n[p:p + 4] = rng.permutation(np.array([0, i, j, TH - 1 - i - j]))
            cl = rng.permutation(np.repeat(np.arange(C), n)).reshape(N, U)
        elif g == 5:
            p = rng.permutation(C // 2); k = TH // 15 + 1; left = T - 45 * k
            for i in range(3): n[2 * p[i]] = 7 * k; n[2 * p[i] + 1] = 8 * k
            n[2 * p[3]] = 7 * left // 15; n[2 * p[3] + 1] = left - 7 * left // 15
            cl = rng.permutation(np.repeat(np.arange(C), n)).reshape(N, U)
        else: cl = rng.integers(0, C, (N, U))
        s[:, g] = 16 * (cl + C * rng.integers(0, S // (16 * C), (N, U))) + rng.integers(0, 16 - R * (H - 1), (N, U))
    odd = ((np.arange(W) // B) & 1) == 1
    mu[:, 5] = np.where(odd[None, None, :], two(rng, 6, 7, (N, 16, W)), two(rng, -8, -7, (N, 16, W)))
    a[:, 5] = np.where((np.arange(C) & 1) == 1, -127, 127)[None, :, None, None]
    mu[:, 6, :14] = rng.integers(-8, -3, (N, 14, W)); a[:, 6, :, :14] = 127
    x = frames(rng, mu, mix, s)
    x[:, 5] = two(rng, 6, 7, (N, 16, R, U))
    x[:, 6, :14] = np.where(rng.random((N, 1, R, U)) < 0.5, 7, x[:, 6, :14])
    return pack(mu, x, a, mix, s)
def check_inputs(d):
    bad = []
    for k, lo, hi in (("mu", -8, 7), ("fr", -8, 7), ("a0", -127, 127), ("mix", 0, W - 1), ("s0", 0, S - 1)):
        v = np.asarray(d[k]).astype(np.float64)
        if not (np.min(v) >= lo and np.max(v) <= hi): bad.append("range of " + k)
        elif np.any(v != np.floor(v)): bad.append("whole numbers in " + k)
    return bad
def reference(mu, fr, a0, mix, s0):
    mi = mu.astype(np.float32).astype(np.int32).reshape(N, 8, 16, W)
    mf = np.ascontiguousarray(mi.reshape(N, 8, 16, C, B).transpose(0, 1, 3, 2, 4)).astype(np.float64)
    x = fr.astype(np.float32).astype(np.int32).reshape(N, 8, 16, R, U)
    a = a0.astype(np.float32).astype(np.int64).reshape(N, 8, 16, C, 16).transpose(0, 1, 3, 2, 4)
    lst = mix.astype(np.int64).reshape(N, 8, 16, S)
    s = np.stack([gentries(v) for v in s0]).astype(np.int64)
    yw = np.zeros((N, 8, R, U), np.float32)
    gi = np.arange(8)[:, None, None, None]; si = np.arange(16)[None, None, :, None]
    for t in range(R):
        z = np.matmul(a.astype(np.float64), mf).astype(np.int64)
        M = np.clip((z + 32) >> 6, -8, 7).astype(np.int32).transpose(0, 1, 3, 2, 4).reshape(N, 8, 16, W)
        G = np.zeros((8, C, 16, 16), np.int64); n = np.zeros((8, C), np.int64); new = []
        for r in range(N):
            st = (s[r][:, None, :] + np.arange(H)[None, :, None]) & (S - 1)
            cand = lst[r][gi, si, st[:, :, None, :]].reshape(8, 16 * H, U)
            mc = np.take_along_axis(M[r], cand.reshape(8, 1, 16 * H * U), 2).reshape(8, 16, 16 * H, U)
            xt = x[r, :, :, t]
            score = np.add.reduce(mc * (2 * xt[:, :, None, :] - mc), axis=1)
            k = np.argmax(score, axis=1)
            w = np.take_along_axis(cand, k[:, None, :], 1)[:, 0]
            e = xt - np.take_along_axis(M[r], w[:, None, :], 2)
            v = np.take_along_axis(mi[r], w[:, None, :], 2)
            hit = (w >> 9)[:, None, :] == np.arange(C)[None, :, None]
            left = (hit[:, :, None, :] * e[:, None]).astype(np.float64)
            G = G + np.matmul(left, v.transpose(0, 2, 1)[:, None].astype(np.float64)).astype(np.int64)
            n = n + np.add.reduce(hit.astype(np.int64), axis=2)
            yw[r, :, t] = w
            new.append((s[r] + (k >> 4)) & (S - 1))
        s = np.stack(new)
        took = np.zeros((8, C), bool); D = np.zeros_like(G)
        for l in range(LC + 1):
            gs = np.repeat(np.add.reduce(G.reshape(8, C >> l, 1 << l, 16, 16), axis=2), 1 << l, axis=1)
            ns = np.repeat(np.add.reduce(n.reshape(8, C >> l, 1 << l), axis=2), 1 << l, axis=1)
            now = (ns >= TH) & ~took
            D = np.where(now[:, :, None, None], gs, D); took = took | now
        a = np.clip(a + np.clip(D >> SH, -2, 2)[None], -127, 127)
    ya = np.ascontiguousarray(a.transpose(0, 1, 3, 2, 4)).reshape(N, 128, 16 * C)
    return {"ya": ya.astype(np.float32), "ys": s.astype(np.float32), "yw": yw.reshape(N, 8, R * U)}

@@ -1,0 +1,577 @@
+from concourse.bass import DstId, RemoteDMATransfer
+from concourse.mybir import AluOpType as A
+from concourse.mybir import ActivationFunctionType as F
+
+R = 3
+PW = 34
+QX = 12
+BF, F32, I32, U16 = "bfloat16", "float32", "int32", "uint16"
+
+SCRATCH = {}
+
+
+def _sb(dtype, **kw):
+    for k, v in kw.items():
+        SCRATCH[k] = ("sbuf", [128] + (v if isinstance(v, list) else [v]), dtype)
+
+
+_sb(BF, MU=4096, MT=4096, FR=768, X192=768, A0=128, TA=128, XR=256 * QX + 2048, D=8192, SQ=[2 * QX, 16, 16], SQY=2048, HI=512, LO=512,
+    THI=[16, 2, 16], TLO=[16, 2, 16], ATS=128, BD=1024, NE=256, MW=256, EW0=1024, EW1=1024, ET0=1024, ET1=1024,
+    PT=256, FN=256, RN=4 * PW, NR=32, DL0=128, DL1=128, DL2=128,
+    ONES=128, ID=128, NID=128, ID64=128, PERM=128, P00=128, P01=128, P10=128, P11=128, SW=144, J64=16, OH=16, KN=128,
+    ZB=512, OC=128, M3=128, M192=128, TBX=32 * QX, TBY=256, L1B=128, L2B=128)
+_sb(F32, MIXF=1032, CF=16, DD=128, PD=128, KC=128, R16=16, N1=128, N2=128, N3=128, BI=8, BN=8, U8=16, U8R=16,
+    SP=32 * QX, SS=8 * PW, RX1=32 * QX, RX2=32 * QX, RY=256, H64=16, SCF=16, HS=16, SF=16,
+    OUT=64, OUTT=64, NCOL=4, LB=8 * PW, LBS=8 * PW, C260=16, THR=128, UU=128, DS=128,
+    LF0=128, LF1=128, LF2=128, LF3=128, SB0=128, SB1=128, SB2=128, YA=128)
+_sb(I32, MIX=1032, S0=16, PI=1, CI=8, LOI=512, KI=32, HL=32, CL=16, SI=16, SJ=16)
+_sb(U16, LS1=32, LS2=32, CAND=640, XL=128, W16=16, SC16=16, CL16=16)
+for _t in range(R):
+    _sb(U16, **{"P%d" % _t: 4 * PW, "LD%d" % _t: 4 * PW, "LH%d" % _t: 4 * PW, "HB%d" % _t: 2 * PW})
+for _n in ("Z0", "Z1", "Z2", "Z3", "KX1", "KX2", "KY"):
+    SCRATCH[_n] = ("psum", [128, 512], F32)
+SCRATCH["ZT"] = ("psum", [128, 1024], BF)
+
+SEMAPHORES = ["qv", "qs", "qp", "qg", "sent", "d_s0", "d_fr0", "d_fr1", "d_a0", "d_mix", "d_mixw", "d_mu0", "d_mu1", "d_mu2", "d_mu3",
+              "d_o0", "d_o1", "d_ya"]
+SEMAPHORES += ["%s%d" % (n, t) for t in range(R) for n in ("rd", "rh", "ag", "hin")]
+
+
+def _mask(engines):
+    m = 0
+    for e in engines:
+        m |= 1 << e
+    return m
+
+
+def _layout(T, topo):
+    cores = list(T.cores)
+    first = [c for c in cores if c == cores[0] or topo.may_write(cores[0], c)]
+    second = [c for c in cores if c not in first]
+    planes = {}
+    for mine, other in ((first, second), (second, first)):
+        for c in mine:
+            helpers = [h for h in topo.cores_of(c) if h != c and topo.die(h) == topo.die(c)
+                       and all(topo.may_write(h, o) for o in other)]
+            planes[c] = (mine, other, helpers[:2])
+    return planes
+
+
+def _dst(topo, dst, src):
+    rid, pid = topo.addr(dst, src)
+    return DstId(rid=rid, pnc=pid)
+
+
+def helper_program(g, core, owner, T, topo, planes):
+    mine, other, helpers = planes[owner]
+    h, k = helpers.index(core), mine.index(owner)
+    n_in = len(topo.engines(owner, core)) // 2
+    total = 0
+    for t in range(R):
+        g.wait_ge(T.sem["hin%d" % t], n_in)
+        tr = []
+        for i in range(2):
+            dst = other[2 * h + i]
+            eng = topo.engines(core, dst)
+            half = len(eng) // 2
+            tr.append(RemoteDMATransfer(dst_ids=[_dst(topo, dst, core)], dma_engine_mask=_mask(eng[i * half:(i + 1) * half]),
+                                        remote_sem=T.sem["rh%d" % t], src=T["HB%d" % t][:, i * PW:(i + 1) * PW],
+                                        dst=T["LH%d" % t][:, k * PW:(k + 1) * PW]))
+            total += half
+        g.remote_dma_fused(tr, local_sem=T.sem.sent)
+    g.wait_ge(T.sem.sent, total)
+
+
+def _emit(ops, g, T):
+    queue = {"v": g.vector, "s": g.scalar, "p": g.tensor, "g": g, "y": g.sync}
+    wr, rd, bank, known, count = {}, {}, {}, {e: {} for e in queue}, {}
+    marked = set()
+    for o in ops:
+        e = o["e"]
+        if e == "ext":
+            ev = (o["sem"], o["n"], {o["sem"]: o["n"]})
+            for k in o["w"]:
+                wr[k], rd[k] = ev, []
+            continue
+        deps = []
+        for k in o["r"]:
+            if k in wr:
+                deps.append(wr[k])
+        for k in o["w"]:
+            deps += rd.get(k, [])
+            if k in wr:
+                deps.append(wr[k])
+        for k in o["b"]:
+            deps += [ev for e2, ev in bank.get(k, {}).items() if e2 != e]
+        need = {}
+        for ev in deps:
+            if known[e].get(ev[0], 0) < ev[1] and (ev[0] not in need or need[ev[0]][1] < ev[1]):
+                need[ev[0]] = ev
+        waits = []
+        for ev in need.values():
+            if not any(z is not ev and z[2].get(ev[0], 0) >= ev[1] for z in need.values()):
+                waits.append((ev[0], ev[1]))
+        for ev in need.values():
+            for k, v in ev[2].items():
+                if known[e].get(k, 0) < v:
+                    known[e][k] = v
+        for w in waits:
+            marked.add(w)
+        o["waits"] = waits
+        key = o["sem"] if o["sem"] else e
+        count[key] = count.get(key, 0) + (16 if o["sem"] else 1)
+        val = o["n"] if o["n"] else count[key]
+        clock = dict(known[e])
+        clock[key] = val
+        ev = (key, val, clock)
+        o["ev"] = (key, count[key])
+        for k in o["r"]:
+            rd.setdefault(k, []).append(ev)
+        for k in o["w"]:
+            wr[k], rd[k] = ev, []
+        for k in o["b"]:
+            bank.setdefault(k, {})[e] = ev
+    number = {}
+    for e in queue:
+        for i, w in enumerate(sorted(w for w in marked if w[0] == e)):
+            number[w] = i + 1
+    for o in ops:
+        if o["e"] == "ext":
+            continue
+        q = queue[o["e"]]
+        for w in o["waits"]:
+            if w in number:
+                q.wait_ge(T.sem["q" + w[0]], number[w])
+            else:
+                q.wait_ge(T.sem[w[0]], w[1])
+        ins = o["f"]()
+        if o["sem"]:
+            ins.then_inc(T.sem[o["sem"]], 16)
+        elif o["ev"] in number:
+            ins.then_inc(T.sem["q" + o["e"]], 1)
+
+
+def rank_program(g, core, T, topo):
+    planes = _layout(T, topo)
+    if T.rank_of(core) is None:
+        for c in planes:
+            if core in planes[c][2]:
+                helper_program(g, core, c, T, topo, planes)
+        return
+    mine, other, helpers = planes[core]
+    me = mine.index(core)
+    V, S, P = g.vector, g.scalar, g.tensor
+    ops = []
+    sent = [0]
+
+    def op(e, f, r=(), w=(), b=(), sem=None, n=0):
+        ops.append({"e": e, "f": f, "r": list(r), "w": list(w), "b": list(b), "sem": sem, "n": n})
+
+    def ext(sem, n, w):
+        ops.append({"e": "ext", "sem": sem, "n": n, "w": list(w)})
+
+    def ts(out, in0, s1, s2, o0, o1, r, w, b=()):
+        if o1 is None:
+            op("v", lambda: V.tensor_scalar(out, in0, s1, None, o0), r, w, b)
+        else:
+            op("v", lambda: V.tensor_scalar(out, in0, s1, s2, o0, o1), r, w, b)
+
+    def tt(out, in0, in1, o, r, w, b=()):
+        op("v", lambda: V.tensor_tensor(out, in0, in1, o), r, w, b)
+
+    def cp(out, in_, r, w, b=()):
+        op("v", lambda: V.tensor_copy(out, in_), r, w, b)
+
+    def ms(out, c, w):
+        op("v", lambda: V.memset(out, c), (), w)
+
+    def scan(out, d0, d1, o0, o1, r, w, b=()):
+        op("v", lambda: V.tensor_tensor_scan(out, d0, d1, 0.0, o0, o1), r, w, b)
+
+    def act(out, in_, func, r, w, b=(), **kw):
+        op("s", lambda: S.activation(out, in_, func, **kw), r, w, b)
+
+    def mm(bank, out, lhsT, rhs, start, stop, r):
+        op("p", lambda: P.matmul(out, lhsT, rhs, start, stop), r, (), [bank])
+
+    def iota(out, pat, cm, w, fl=True):
+        if fl:
+            op("g", lambda: g.iota(out, pat, 0, cm, allow_small_or_imprecise_dtypes=True), (), w)
+        else:
+            op("g", lambda: g.iota(out, pat, 0, cm), (), w)
+
+    def dma(e, out, in_, sem, r=(), w=(), n=0):
+        q = g.sync if e == "y" else g.scalar
+        op(e, lambda: q.dma_start(out, in_), r, w, (), sem, n)
+
+    MTK = ["MT%d" % c for c in range(8)]
+    XRK = ["XR%d" % i for i in range(16)]
+    BDK = ["BD%d" % i for i in range(8)]
+    PM = [[T.P00, T.P01], [T.P10, T.P11]]
+    MUK = ["MU%d" % i for i in range(4)]
+    SCL = [1, 2, 4, 5, 7]
+    NX = 16 * QX
+    XO, YO = 16 * NX, 32 * NX
+    CYK = ["CY%d" % i for i in range(8)]
+
+    dma("s", T.S0[:], T.s0[:], "d_s0", w=["S0"])
+    dma("y", T.MIX[:, 0:1024], T.mix[:], "d_mix", w=["MIX"])
+    dma("s", T.A0[:], T.a0[:], "d_a0", w=["A0"])
+    dma("s", T.FR[:, 0:256], T.fr[:, 0:256], "d_fr0", w=["FR0"])
+    dma("s", T.MIX[:, 1024:1028], T.mix[:, 0:4], "d_mixw", w=["MIXW"])
+    for i in range(4):
+        dma("y", T.MU[:, 1024 * i:1024 * i + 1024], T.mu[:, 1024 * i:1024 * i + 1024], "d_mu%d" % i, w=[MUK[i]])
+    dma("y", T.FR[:, 256:768], T.fr[:, 256:768], "d_fr1", w=["FR1", "FR2"])
+
+    iota(T.PI[:], [[0, 1]], 1, ["PI"], False)
+    iota(T.DD[:], [[-1, 128]], 1, ["DD"])
+    iota(T.R16[:], [[1, 16]], 0, ["R16"])
+    op("g", lambda: g.iota(T.LOI[:, 0:128], [[1, 16], [0, 2], [16, 16 - QX]], NX, 0), (), ["LOI"])
+    iota(T.TBX[0:64, :], [[-16, 2], [0, QX], [-1, 16]], 0, ["TBX"])
+    for k in range(2):
+        iota(T.TBY[0:64, 128 * k:128 * k + 128], [[-16, 2], [0, 16 - QX], [-1, 16]], 0, ["TBY%d" % k])
+    iota(T.U8R[:], [[0, 2], [128, 8]], 0, ["U8R"])
+    iota(T.KC[:], [[0, 16], [1, 8]], 0, ["KC"])
+    for l, buf in ((1, T.N1), (2, T.N2), (3, T.N3)):
+        iota(buf[:], [[1, 128 >> l], [0, 1 << l]], 0, ["N%d" % l])
+    iota(T.PD[:], [[-1, 8], [-8, 16]], 1, ["PD"])
+
+    ms(T.ONES[:], 1.0, ["ONES"])
+    ms(T.ZB[0:32, :], 192.0 / 32, ["ZBa"])
+    ms(T.ZB[32:64, :], 1.0 / 128 / 32, ["ZBb"])
+    ms(T.SW[:], 0.0, ["SW"])
+    ms(T.SP[:], 0.0, ["SP"])
+    ms(T.EW0[:], 0.0, ["EW0"])
+    ms(T.EW1[:], 0.0, ["EW1"])
+    ms(T.RN[:], 0.0, ["RN0", "RN1"])
+    ms(T.SP[:, 0::16], -float(1 << 25), ["SP"])
+    for i, sh in enumerate((1, 2, 3, 4)):
+        ts(T.CI[:, i:i + 1], T.PI[:], sh, None, A.arith_shift_right, None, ["PI"], ["CI%d" % i])
+    ts(T.CI[:, 4:5], T.PI[:], 15, None, A.bitwise_and, None, ["PI"], ["CI4"])
+    ts(T.CI[:, 5:6], T.PI[:], 4, 1, A.arith_shift_right, A.bitwise_and, ["PI"], ["CI5"])
+    cp(T.CF[:, 0:6], T.CI[:, 0:6], ["CI%d" % i for i in range(6)], ["CF"])
+    gcol, icol, par1, par0, i8 = T.CF[:, 3:4], T.CF[:, 4:5], T.CF[:, 5:6], T.CF[:, 6:7], T.CF[:, 7:8]
+    ts(par0, par1, -1.0, 1.0, A.mult, A.add, ["CF"], ["par0"])
+    ts(i8, icol, 8.0, None, A.mult, None, ["CF"], ["i8"])
+    ts(T.BI[:], T.R16[:, 0:8], gcol, None, A.is_equal, None, ["R16", "CF"], ["BI"])
+    for g2 in range(2):
+        for c2 in range(2):
+            ts(PM[g2][c2][:], T.DD[:], 16.0 * (c2 - g2), par1 if c2 else par0, A.is_equal, A.mult,
+               ["DD", "CF", "par0"], ["PM%d%d" % (g2, c2)])
+
+    def bias_banks(names=("Z2", "Z3")):
+        for z in names:
+            mm(z, T[z][:], T.ONES[0:64, :], T.ZB[0:64, :], True, False, ["ONES", "ZBa", "ZBb"])
+
+    def expand():
+        for gp in range(8):
+            out = T.BD[:, 128 * gp:128 * gp + 128]
+            if gp < 5:
+                ts(out, T.ATS[:], T.BI[:, gp:gp + 1], None, A.mult, None, ["ATS", "BI"], [BDK[gp]])
+            else:
+                act(out, T.ATS[:], F.Identity, ["ATS", "BI"], [BDK[gp]], scale=T.BI[:, gp:gp + 1])
+
+    def xrep(t, which, eng):
+        src = T.FR[:, 256 * t:256 * t + NX]
+        for i in which:
+            if eng == "v":
+                ts(T.XR[:, i:XO:16], src, 192.0, None, A.add, None, ["FR%d" % t], [XRK[i]])
+            else:
+                act(T.XR[:, i:XO:16], src, F.Identity, ["FR%d" % t], [XRK[i]], bias=192.0)
+
+    def xrep_late(t):
+        act(T.XR[:, XO:XO + 2048], T.FR[:, 256 * t:256 * t + 256].indirect(T.XL[:]), F.Identity, ["FR%d" % t, "XL"], ["XY"], bias=192.0)
+
+    def x192(t):
+        act(T.X192[:, 256 * t:256 * t + 256], T.FR[:, 256 * t:256 * t + 256], F.Identity, ["FR%d" % t], ["X192_%d" % t], bias=192.0)
+
+    def lists(src, key):
+        for h in range(2):
+            ts(T.LS2[:, h::2], src[:, 0:16], float(h), None, A.add, None, [key], ["LS2%d" % h])
+        for h in range(2):
+            ts(T.LS1[:, h * QX:h * QX + QX], src[:, 0:QX], float(h), None, A.add, None, [key], ["LS1a%d" % h])
+            o = 2 * QX + h * (16 - QX)
+            ts(T.LS1[:, o:o + 16 - QX], src[:, QX:16], float(h), None, A.add, None, [key], ["LS1b%d" % h])
+
+    def candidates():
+        l2 = ["LS20", "LS21"]
+        act(T.HI[:], T.MIXF[:, 0:1028].indirect(T.LS2[:]), F.Identity, ["MIXF"] + l2, ["HI"],
+            scale=1.0 / 64, bias=127.5 + 1.0 / 128)
+        ts(T.LOI[:], T.MIX[:, 0:1028].indirect(T.LS2[:]), 63, None, A.bitwise_and, None, ["MIX", "MIXW"] + l2, ["LOI"])
+        cp(T.LO[:], T.LOI[:], ["LOI"], ["LO"])
+        op("v", lambda: V.transpose(T.THI[:], T.HI[:]), ["HI"], ["THI"])
+        op("v", lambda: V.transpose(T.TLO[:], T.LO[:]), ["LO"], ["TLO"])
+
+    def candidate_list():
+        cp(T.CAND[:, 0:512], T.MIX[:, 0:1028].indirect(T.LS1[:]), ["MIX", "MIXW", "LS1a0", "LS1a1", "LS1b0", "LS1b1"], ["CAND"])
+
+    def late_list():
+        for c in range(8):
+            o = 2 * NX + 16 * c
+            cp(T.CAND[:, 512 + c::8], T.CAND[:, o:o + 16], ["CAND"], [CYK[c]])
+
+    def key_start():
+        mm("KX1", T.KX1[:, 0:2 * NX], T.ONES[0:64, :], T.TBX[0:64, :], True, False, ["ONES", "TBX"])
+        mm("KX2", T.KX2[:, 0:2 * NX], T.ONES[0:64, :], T.TBX[0:64, :], True, False, ["ONES", "TBX"])
+        mm("KY", T.KY[:, 0:256], T.ONES[0:64, :], T.TBY[0:64, :], True, False, ["ONES", "TBY0", "TBY1"])
+        for k, (src, name) in enumerate(((T.THI, "THI"), (T.TLO, "TLO"))):
+            kx = "KX%d" % (k + 1)
+            for h in range(2):
+                for g2 in range(2):
+                    r = [name, "PM%d%d" % (g2, h)]
+                    mm(kx, T[kx][:, h * NX:h * NX + NX], PM[g2][h][:], src[:, 0:QX, g2, :], False, False, r)
+                    o = 128 * k + 64 * h
+                    mm("KY", T.KY[:, o:o + 64], PM[g2][h][:], src[:, QX:16, g2, :], False, False, r)
+
+    bias_banks()
+    op("v", lambda: V.transpose(T.TA[:], T.A0[:]), ["A0"], ["TA"])
+    for c in range(8):
+        for g2 in range(2):
+            o = 32 * (c // 2) + 16 * g2
+            mm("Z1", T.Z1[:, c:128:8], PM[g2][c % 2][:], T.TA[:, o:o + 16], g2 == 0, g2 == 1, ["TA", "PM%d%d" % (g2, c % 2)])
+    cp(T.SF[:], T.S0[:], ["S0"], ["SF"])
+    lists(T.S0, "S0")
+    ts(T.ATS[:], T.Z1[:, 0:128], 1.0 / 64, None, A.mult, None, [], ["ATS"], ["Z1"])
+    ts(T.SW[:, 15:143:16], T.BI[:], -2048.0, None, A.mult, None, ["BI"], ["SW"])
+    cp(T.XL[:], T.LOI[:, 0:128], ["LOI"], ["XL"])
+    expand()
+    x192(0)
+    xrep_late(0)
+    xrep(0, range(0, 16), "v")
+    ts(T.ID[:], T.DD[:], 0.0, None, A.is_equal, None, ["DD"], ["ID"])
+    ts(T.NID[:], T.DD[:], 0.0, -1.0, A.is_equal, A.mult, ["DD"], ["NID"])
+    ts(T.BN[:], T.BI[:], -1.0, None, A.mult, None, ["BI"], ["BN"])
+    ts(T.OH[:], T.R16[:], icol, None, A.is_equal, None, ["R16", "CF"], ["OH"])
+    ts(T.U8[:], T.U8R[:], i8, None, A.add, None, ["U8R", "i8"], ["U8"])
+    ts(T.KN[:], T.KC[:], icol, None, A.is_equal, None, ["KC", "CF"], ["KN"])
+    cp(T.MIXF[:, 0:1028], T.MIX[:, 0:1028], ["MIX", "MIXW"], ["MIXF"])
+    candidates()
+    candidate_list()
+    late_list()
+    key_start()
+
+    def owner_constants():
+        ts(T.ID64[:], T.DD[:], 0.0, 1.0 / 64, A.is_equal, A.mult, ["DD"], ["ID64"])
+        ts(T.LF0[:], T.DD[:], 0.0, 1.0 / 256, A.is_equal, A.mult, ["DD"], ["LF0"])
+        for l in (1, 2, 3):
+            ts(T["LF%d" % l][:], T["N%d" % l][:], T.CF[:, l - 1:l], 1.0 / 256, A.is_equal, A.mult, ["N%d" % l, "CF"], ["LF%d" % l])
+        for l in (1, 2):
+            ts(T["L%dB" % l][:], T["N%d" % l][:], T.CF[:, l - 1:l], None, A.is_equal, None, ["N%d" % l, "CF"], ["L%dB" % l])
+        ms(T.OC[0:64, :], 0.0, ["OCa", "OCb"])
+        ms(T.M3[0:64, :], -3.0 / 64, ["M3"])
+        ms(T.SS[:], 1.0, ["SS"])
+        ms(T.C260[:], 260.0, ["C260"])
+        for i, v in enumerate((-1.0e6, -260.0, 0.0, 130.0)):
+            ms(T.THR[:, i::4], v, ["THR%d" % i])
+        for l in range(3):
+            tt(T["SB%d" % l][:], T["LF%d" % (l + 1)][:], T["LF%d" % l][:], A.subtract, ["LF%d" % l, "LF%d" % (l + 1)], ["SB%d" % l])
+        ms(T.OC[0:32, 3:128:4], 192.0 / 32, ["OCa"])
+        ms(T.OC[32:64, 3:128:4], -255.0 / 512 / 32, ["OCb"])
+        ms(T.SS[:, 0::8], 0.0, ["SS"])
+
+    own_s = [(0, "Z0"), (2, "Z1"), (4, "Z3")]
+    chunks = [(0, 2), (2, 4), (4, 6), (6, 8)] + [(c, c + 4) for c in range(8, 2 * QX, 4)]
+    zbank = {0: "Z2", 3: "Z3", 6: "Z2", 1: "Z0", 2: "Z1", 4: "Z0", 5: "Z1", 7: "Z0"}
+
+    def qof(c):
+        return c % QX if c < 2 * QX else QX + (c - 2 * QX) % (16 - QX)
+
+    for t in range(R):
+        last = t == R - 1
+        vplan = {0: [("d", 0)], 3: [("d", 3), ("c", 1), ("c", 2)], 6: [("d", 6), ("c", 4)], 7: [("c", 5), ("c", 7)]}
+        for c in (1, 0, 2, 3, 4, 5, 6, 7):
+            z = zbank[c]
+            if c == 4:
+                bias_banks([zbank[6]])
+            mm(z, T[z][:], T.BD[:, c::8], T.MU[:, 512 * c:512 * c + 512], c in SCL, True, BDK + ["MU%d" % (c // 2)])
+            if c in SCL:
+                act(T.MT[:, 512 * c:512 * c + 512], T[z][:], F.Identity, [], [MTK[c]], [z], bias=192.0 + 1.0 / 128)
+            for kind, d in vplan.get(c, []):
+                dst = T.MT[:, 512 * d:512 * d + 512]
+                if kind == "d":
+                    zd = zbank[d]
+                    ts(dst, T[zd][:], 184.0, 199.0, A.max, A.min, [], [MTK[d]], [zd])
+                else:
+                    ts(dst, dst, 184.0, 199.0, A.max, A.min, [MTK[d]], [MTK[d]])
+        for c0, z in own_s:
+            mc = T.D[:, 256 * c0:256 * c0 + 512]
+            act(mc, T.MT[:, 0:4096].indirect(T.CAND[:, 16 * c0:16 * c0 + 32]), F.Identity, MTK + ["CAND"], ["D%d" % c0])
+            mm(z, T[z][:], T.NID[:], T.XR[:, 256 * c0:256 * c0 + 512], True, False, ["NID"] + XRK)
+            mm(z, T[z][:], T.ID[:], mc, False, True, ["ID", "D%d" % c0])
+        for c0, c1 in chunks:
+            q0 = qof(c0)
+            if c0 in dict(own_s):
+                z = dict(own_s)[c0]
+                act(T.SQ[:, c0:c1], T[z][:], F.Square, [], ["SQ%d" % c0], [z])
+            else:
+                tt(T.D[:, 256 * c0:256 * c1], T.MT[:, 0:4096].indirect(T.CAND[:, 16 * c0:16 * c1]),
+                   T.XR[:, 256 * q0:256 * (q0 + c1 - c0)], A.subtract, MTK + XRK + ["CAND"], ["D%d" % c0])
+                act(T.SQ[:, c0:c1], T.D[:, 256 * c0:256 * c1], F.Square, ["D%d" % c0], ["SQ%d" % c0])
+            if c1 % 4:
+                continue
+            b0 = c1 - 4
+            r = ["SW", "SQ%d" % b0, "SQ%d" % c0]
+            for k in range(2):
+                name = "KX%d" % (k + 1)
+                for j in range(16):
+                    mm(name, T[name][:, 16 * b0:16 * c1], T.SW[:, 15 - j:143 - j], T.SQ[:, b0:c1, j, :], False,
+                       c1 == 2 * QX and j == 15, r)
+        for j0, j1 in ((0, 8), (8, 12), (12, 14), (14, 16)):
+            a, b = 128 * j0, 128 * j1
+            if j0 == 12:
+                for k, rx in enumerate((T.RX1, T.RX2)):
+                    kx = "KX%d" % (k + 1)
+                    scan(rx[:], T.SP[:], T[kx][:, 0:2 * NX], A.add, A.max, ["SP"], ["RX%d" % k], [kx])
+            tt(T.D[:, YO + a:YO + b], T.MT[:, 0:4096].indirect(T.CAND[:, 512 + 8 * j0:512 + 8 * j1]),
+               T.XR[:, XO + a:XO + b], A.subtract, MTK + CYK + ["XY"], ["DY%d" % j0])
+            act(T.SQY[:, a:b], T.D[:, YO + a:YO + b], F.Square, ["DY%d" % j0], ["SY%d" % j0])
+            for j in range(j0, j1):
+                for k in range(2):
+                    mm("KY", T.KY[:, 128 * k:128 * k + 128], T.SW[:, 15 - j:143 - j], T.SQY[:, 128 * j:128 * j + 128], False,
+                       j == 15 and k == 1, ["SW", "SY%d" % j0])
+        for k, rx in enumerate((T.RX1, T.RX2)):
+            tt(T.KI[:, 16 * k:16 * k + QX], rx[:, 15:NX:16], rx[:, NX + 15:2 * NX:16], A.max, ["RX%d" % k], ["KIa%d" % k])
+        tt(T.HS[:, 0:QX], T.RX1[:, NX + 15:2 * NX:16], T.RX1[:, 15:NX:16], A.is_gt, ["RX0"], ["HSa"])
+        scan(T.RY[:], T.SP[:, 0:256], T.KY[:, 0:256], A.add, A.max, ["SP"], ["RY"], ["KY"])
+        for k in range(2):
+            o = 128 * k
+            tt(T.KI[:, 16 * k + QX:16 * k + 16], T.RY[:, o + 15:o + 64:16], T.RY[:, o + 79:o + 128:16], A.max, ["RY"], ["KIb%d" % k])
+        ts(T.HL[:], T.KI[:], 63, None, A.bitwise_and, None, ["KIa0", "KIa1", "KIb0", "KIb1"], ["HL"])
+        ts(T.H64[:], T.HL[:, 0:16], 64.0, None, A.mult, None, ["HL"], ["H64"])
+        ts(T.CL[:], T.HL[:, 0:16], 3, None, A.arith_shift_right, None, ["HL"], ["CL"])
+        wf = T.OUT[:, 16 * t:16 * t + 16]
+        tt(wf, T.H64[:], T.HL[:, 16:32], A.add, ["H64", "HL"], ["OUT%d" % t])
+        tt(T.SCF[:], T.CL[:], T.U8[:], A.add, ["CL", "U8"], ["SCF"])
+        cp(T.W16[:], wf, ["OUT%d" % t], ["W16"])
+        cp(T.CL16[:], T.CL[:], ["CL"], ["CL16"])
+        cp(T.SC16[:], T.SCF[:], ["SCF"], ["SC16"])
+        xs = T.X192[:, 256 * t:256 * t + 256]
+        tt(T.NE[:], T.MT[:, 0:4096].indirect(T.W16[:]), xs, A.subtract, MTK + ["W16", "X192_%d" % t], ["NE"])
+        act(T.MW[:], T.MU[:, 0:4096].indirect(T.W16[:]), F.Identity, MUK + ["W16"], ["MW"])
+        masked, plain = ((T.MW, "MW"), (T.NE, "NE")) if last else ((T.NE, "NE"), (T.MW, "MW"))
+        for h in range(2):
+            cp(T["EW%d" % h][:, 0:1024].indirect(T.SC16[:, 8 * h:8 * h + 8]), masked[0][:, 128 * h:128 * h + 128],
+               [masked[1], "SC16"], ["EW%d" % h])
+        act(T.FN[:], T.OH[:, 0:16].indirect(T.CL16[:]), F.Identity, ["OH", "CL16"], ["FN", "NCOL"], accum_out=T.NCOL[:, 0:1])
+        for s in range(2):
+            act(T.RN[:, 32 + s::PW], T.BN[:, s::2], F.Identity, ["BN", "NCOL"], ["RN%d" % s], scale=T.NCOL[:, 0:1])
+        for h in range(2):
+            mm("KY", T.KY[:, 128 * h:128 * h + 128], plain[0][:, 128 * h:128 * h + 128], T.ID[:], True, True, [plain[1], "ID"])
+        act(T.PT[:], T.KY[:, 0:256], F.Copy, [], ["PT"], ["KY"])
+        for hb in range(2):
+            z = "Z%d" % (1 + hb)
+            for c in range(8):
+                mm(z, T[z][:, c::8], T.EW0[:, c::8], T.ID[:, 64 * hb:64 * hb + 64], True, True, ["EW0", "ID"])
+            act(T.ET0[:, 512 * hb:512 * hb + 512], T[z][:], F.Copy, [], ["ET0%d" % hb], [z])
+        for c in range(8):
+            op("p", lambda c=c: P.transpose(T.ZT[:, 128 * c:128 * c + 128], T.EW1[:, c::8], T.ID[:]), ["EW1", "ID"], (), ["ZT"])
+        for c in range(8):
+            cp(T.ET1[:, c::8], T.ZT[:, 128 * c:128 * c + 128], [], ["ET1c%d" % c], ["ZT"])
+        mm("Z0", T.Z0[:, 0:4 * PW], T.KN[:], T.RN[:], True, False, ["KN", "RN0", "RN1"])
+        for h in range(2):
+            for hb in range(2):
+                for gp in range(4 * hb, 4 * hb + 4):
+                    o = PW * (gp // 2) + 16 * (gp % 2)
+                    mm("Z0", T.Z0[:, o:o + 16], T["ET%d" % h][:, 128 * gp:128 * gp + 128],
+                       T.PT[:, 128 * h + 16 * gp:128 * h + 16 * gp + 16], False, h == 1 and gp == 7,
+                       ["PT"] + (["ET1c%d" % c for c in range(8)] if h else ["ET0%d" % hb]))
+        Pt, LD, LH, DL = T["P%d" % t], T["LD%d" % t], T["LH%d" % t], T["DL%d" % t]
+        ts(Pt[:], T.Z0[:, 0:4 * PW], -1.0, 32768.0, A.mult, A.add, [], ["P%d" % t], ["Z0"])
+
+        tr = []
+        for i, hc in enumerate(helpers):
+            eng = topo.engines(core, hc)
+            half = len(eng) // 2
+            tr.append(RemoteDMATransfer(dst_ids=[_dst(topo, hc, core)], dma_engine_mask=_mask(eng[i * half:(i + 1) * half]),
+                                        remote_sem=T.sem["hin%d" % t], src=Pt[:, 2 * i * PW:(2 * i + 2) * PW], dst=T["HB%d" % t][:]))
+            sent[0] += half
+        op("g", lambda tr=tr: g.remote_dma_fused(tr, local_sem=T.sem.sent), ["P%d" % t])
+        tr = []
+        eng = topo.engines(core, mine[(me + 1) % 4])
+        ne = len(eng)
+        for i, (lo, hi) in enumerate(((0, ne // 2), (ne // 2, 3 * ne // 4), (3 * ne // 4, ne))):
+            k = (me + 1 + i) % 4
+            tr.append(RemoteDMATransfer(dst_ids=[_dst(topo, mine[k], core)], dma_engine_mask=_mask(eng[lo:hi]),
+                                        remote_sem=T.sem["rd%d" % t], src=Pt[:, k * PW:(k + 1) * PW],
+                                        dst=LD[:, me * PW:(me + 1) * PW]))
+        sent[0] += ne
+        op("g", lambda tr=tr: g.remote_dma_fused(tr, local_sem=T.sem.sent), ["P%d" % t])
+        ext("rd%d" % t, ne, ["LD%d" % t])
+        ext("rh%d" % t, 4 * (ne // 2), ["LH%d" % t])
+
+        if t == 0:
+            owner_constants()
+        mm("Z0", T.Z0[:, 0:128], T.ONES[0:64, :], T.OC[0:64, :], True, False, ["ONES", "OCa", "OCb"])
+        tt(T.HS[:, QX:16], T.RY[:, 79:128:16], T.RY[:, 15:64:16], A.is_gt, ["RY"], ["HSb"])
+        tt(T.SF[:], T.SF[:], T.HS[:], A.add, ["SF", "HSa", "HSb"], ["SF"])
+        if not last:
+            mm("Z1", T.Z1[:, 0:128], T.ONES[0:64, :], T.M3[0:64, :], True, False, ["ONES", "M3"])
+            mm("Z1", T.Z1[:, 0:128], T.ID[:], T.ATS[:], False, False, ["ID", "ATS"])
+            bias_banks()
+            lists(T.SF, "SF")
+            candidates()
+            candidate_list()
+            x192(t + 1)
+            xrep(t + 1, range(16), "s")
+            xrep_late(t + 1)
+        else:
+            mm("Z1", T.Z1[:, 0:128], T.ONES[0:64, :], T.M192[0:64, :], True, False, ["ONES", "M192"])
+            for c in range(8):
+                mm("Z1", T.Z1[:, 16 * c:16 * c + 16], T.BD[:, c::8], T.J64[:], False, False, BDK + ["J64"])
+            cp(T.SI[:], T.SF[:], ["SF"], ["SI"])
+            ts(T.SJ[:], T.SI[:], 1023, None, A.bitwise_and, None, ["SI"], ["SJ"])
+            cp(T.OUT[:, 48:64], T.SJ[:], ["SJ"], ["OUT3"])
+        if t >= 1:
+            blk = t - 1
+            op("v", lambda blk=blk: V.transpose(T.OUTT[:, 32 * blk:32 * blk + 32], T.OUT[:, 32 * blk:32 * blk + 32]),
+               ["OUT%d" % (2 * blk), "OUT%d" % (2 * blk + 1)], ["OUTT%d" % blk])
+            for gp in range(8):
+                p0, o = 32 * (gp // 2), 32 * blk + 16 * (gp % 2)
+                if blk == 0:
+                    dma("y", T.yw[gp:gp + 1, 0:512], T.OUTT[p0:p0 + 32, o:o + 16], "d_o0", ["OUTT0"], ["o0"] if gp == 7 else [], 128)
+                else:
+                    dma("y", T.yw[gp:gp + 1, 512:768], T.OUTT[p0:p0 + 16, o:o + 16], "d_o1", ["OUTT1"], [], 256)
+                    dma("y", T.ys[gp:gp + 1, :], T.OUTT[p0 + 16:p0 + 32, o:o + 16], "d_o1", ["OUTT1"], ["o1"] if gp == 7 else [], 256)
+        for k in [me] + [k for k in range(4) if k != me]:
+            src = Pt if k == me else LD
+            ts(T.LB[:, k::8], src[:, k * PW:(k + 1) * PW], -32768.0, None, A.add, None,
+               ["P%d" % t if k == me else "LD%d" % t], ["LB%d" % k])
+        for k in range(4):
+            ts(T.LB[:, 4 + k::8], LH[:, k * PW:(k + 1) * PW], -32768.0, None, A.add, None, ["LH%d" % t], ["LB%d" % (k + 4)])
+        scan(T.LBS[:], T.SS[:], T.LB[:], A.mult, A.add, ["SS"] + ["LB%d" % k for k in range(8)], ["LBS"])
+        for s in range(2):
+            o = 8 * (32 + s) + 7
+            ts(T.NR[:, 16 * s:16 * s + 16], T.C260[:], T.LBS[:, o:o + 1], -130.0, A.min, A.add, ["C260", "LBS"], ["NR%d" % s])
+        for i, name in enumerate(("SB2", "SB1", "SB0", "LF0")):
+            mm("Z0", T.Z0[:, i:128:4], T[name][:], T.LBS[:, 7:256:8], False, i == 3, [name, "LBS"])
+            if i == 1:
+                for m, nm in enumerate(("ID", "L2B", "L1B", "ID")):
+                    mm("KY", T.KY[:, m:128:4], T[nm][:], T.NR[:], True, True, [nm, "NR0", "NR1"])
+        tt(T.UU[:], T.KY[:, 0:128], T.THR[:], A.is_lt, ["THR%d" % i for i in range(4)], ["UU"], ["KY"])
+        scan(T.DS[:], T.UU[:], T.Z0[:, 0:128], A.mult, A.add, ["UU"], ["DS"], ["Z0"])
+        own = DL[:, 32 * me:32 * me + 32]
+        ts(own, T.DS[:, 3::4], 190.0, 194.0, A.max, A.min, ["DS"], ["DLo%d" % t])
+        peers = [c for c in mine if c != core]
+        tr = [RemoteDMATransfer(dst_ids=[_dst(topo, c, core) for c in peers], dma_engine_mask=_mask(eng),
+                                remote_sem=T.sem["ag%d" % t], srcs=[own], dsts=[own for c in peers])]
+        sent[0] += ne
+        op("g", lambda tr=tr: g.remote_dma_fused(tr, local_sem=T.sem.sent), ["DLo%d" % t])
+        ext("ag%d" % t, 3 * ne, ["DLr%d" % t])
+        if not last:
+            late_list()
+            for h in range(2):
+                ms(T["EW%d" % h][:], 0.0, ["EW%d" % h])
+            if t == 0:
+                ts(T.PERM[:], T.PD[:], 0.0, None, A.is_equal, None, ["PD"], ["PERM"])
+                ts(T.J64[:], T.R16[:], icol, 64.0, A.is_equal, A.mult, ["R16", "CF"], ["J64"])
+                ms(T.M192[0:64, :], -3.0, ["M192"])
+            key_start()
+            mm("Z1", T.Z1[:, 0:128], DL[:], T.ID64[:], False, True, ["DLo%d" % t, "DLr%d" % t, "ID64"])
+            ts(T.ATS[:], T.Z1[:, 0:128], -127.0 / 64, 127.0 / 64, A.max, A.min, [], ["ATS"], ["Z1"])
+            expand()
+        else:
+            mm("Z1", T.Z1[:, 0:128], DL[:], T.PERM[:], False, True, ["DLo%d" % t, "DLr%d" % t, "PERM"])
+            ts(T.YA[:], T.Z1[:, 0:128], -127.0, 127.0, A.max, A.min, [], ["YA"], ["Z1"])
+            dma("y", T.ya[:], T.YA[:], "d_ya", ["YA"], ["ya"])
+    op("g", lambda: g.wait_ge(T.sem.sent, sent[0]), ["o0", "o1", "ya"])
+    _emit(ops, g, T)

@@ -15,24 +15,24 @@ def _sb(dtype, **kw):
         SCRATCH[k] = ("sbuf", [128] + (v if isinstance(v, list) else [v]), dtype)
 
 
-_sb(BF, MU=4096, MT=4096, FR=768, X192=768, A0=128, TA=128, XR=256 * QX + 2048, D=8192, SQ=[2 * QX, 16, 16], SQY=2048, HI=512, LO=512,
+_sb(BF, MU=4096, MT=4096, FR=768, X192=768, A0=128, TA=128, XR=256 * QX + 1024, D=8192, SQ=[2 * QX, 16, 16], SQY=2048, HI=512, LO=512,
     THI=[16, 2, 16], TLO=[16, 2, 16], ATS=128, BD=1024, NE=256, MW=256, EW0=1024, EW1=1024, ET0=1024, ET1=1024,
     PT=256, FN=256, RN=4 * PW, NR=32, DL0=128, DL1=128, DL2=128,
-    ONES=128, ID=128, NID=128, ID64=128, PERM=128, P00=128, P01=128, P10=128, P11=128, SW=144, J64=16, OH=16, KN=128,
+    ONES=128, ID=128, NID=128, C64=128, XT=64, ID64=128, PERM=128, P00=128, P01=128, P10=128, P11=128, SW=144, J64=16, OH=16, KN=128,
     ZB=512, OC=128, M3=128, M192=128, TBX=32 * QX, TBY=256, L1B=128, L2B=128)
-_sb(F32, MIXF=1032, CF=16, DD=128, PD=128, KC=128, R16=16, N1=128, N2=128, N3=128, BI=8, BN=8, U8=16, U8R=16,
+_sb(F32, MIXF=1032, CF=16, DD=128, KC=128, R16=16, C256=128, BI=8, BN=8, U8=16, U8R=16,
     SP=32 * QX, SS=8 * PW, RX1=32 * QX, RX2=32 * QX, RY=256, H64=16, SCF=16, HS=16, SF=16,
     OUT=64, OUTT=64, NCOL=4, LB=8 * PW, LBS=8 * PW, C260=16, THR=128, UU=128, DS=128,
-    LF0=128, LF1=128, LF2=128, LF3=128, SB0=128, SB1=128, SB2=128, YA=128)
+    LF0=128, SB0=128, SB1=128, SB2=128, YA=128)
 _sb(I32, MIX=1032, S0=16, PI=1, CI=8, LOI=512, KI=32, HL=32, CL=16, SI=16, SJ=16)
-_sb(U16, LS1=32, LS2=32, CAND=640, XL=128, W16=16, SC16=16, CL16=16)
+_sb(U16, LS1=32, LS2=32, CAND=640, XL=64, W16=16, SC16=16, CL16=16)
 for _t in range(R):
     _sb(U16, **{"P%d" % _t: 4 * PW, "LD%d" % _t: 4 * PW, "LH%d" % _t: 4 * PW, "HB%d" % _t: 2 * PW})
 for _n in ("Z0", "Z1", "Z2", "Z3", "KX1", "KX2", "KY"):
     SCRATCH[_n] = ("psum", [128, 512], F32)
 SCRATCH["ZT"] = ("psum", [128, 1024], BF)
 
-SEMAPHORES = ["qv", "qs", "qp", "qg", "sent", "d_s0", "d_fr0", "d_fr1", "d_a0", "d_mix", "d_mixw", "d_mu0", "d_mu1", "d_mu2", "d_mu3",
+SEMAPHORES = ["qv", "qs", "qp", "qg", "sent", "d_s0", "d_fr0", "d_fr1", "d_a0", "d_mix", "d_mu0", "d_mu1", "d_mu2", "d_mu3",
               "d_o0", "d_o1", "d_ya"]
 SEMAPHORES += ["%s%d" % (n, t) for t in range(R) for n in ("rd", "rh", "ag", "hin")]
 
@@ -65,7 +65,7 @@ def _dst(topo, dst, src):
 def helper_program(g, core, owner, T, topo, planes):
     mine, other, helpers = planes[owner]
     h, k = helpers.index(core), mine.index(owner)
-    n_in = len(topo.engines(owner, core)) // 2
+    n_in = len([e for e in topo.engines(owner, core) if e not in topo.engines(owner, mine[(k + 1) % 4])]) // 2
     total = 0
     for t in range(R):
         g.wait_ge(T.sem["hin%d" % t], n_in)
@@ -212,13 +212,13 @@ def rank_program(g, core, T, topo):
     SCL = [1, 2, 4, 5, 7]
     NX = 16 * QX
     XO, YO = 16 * NX, 32 * NX
+    XYK = ["XY%d" % i for i in range(16)]
     CYK = ["CY%d" % i for i in range(8)]
 
     dma("s", T.S0[:], T.s0[:], "d_s0", w=["S0"])
     dma("y", T.MIX[:, 0:1024], T.mix[:], "d_mix", w=["MIX"])
     dma("s", T.A0[:], T.a0[:], "d_a0", w=["A0"])
     dma("s", T.FR[:, 0:256], T.fr[:, 0:256], "d_fr0", w=["FR0"])
-    dma("s", T.MIX[:, 1024:1028], T.mix[:, 0:4], "d_mixw", w=["MIXW"])
     for i in range(4):
         dma("y", T.MU[:, 1024 * i:1024 * i + 1024], T.mu[:, 1024 * i:1024 * i + 1024], "d_mu%d" % i, w=[MUK[i]])
     dma("y", T.FR[:, 256:768], T.fr[:, 256:768], "d_fr1", w=["FR1", "FR2"])
@@ -226,30 +226,62 @@ def rank_program(g, core, T, topo):
     iota(T.PI[:], [[0, 1]], 1, ["PI"], False)
     iota(T.DD[:], [[-1, 128]], 1, ["DD"])
     iota(T.R16[:], [[1, 16]], 0, ["R16"])
-    op("g", lambda: g.iota(T.LOI[:, 0:128], [[1, 16], [0, 2], [16, 16 - QX]], NX, 0), (), ["LOI"])
-    iota(T.TBX[0:64, :], [[-16, 2], [0, QX], [-1, 16]], 0, ["TBX"])
-    for k in range(2):
-        iota(T.TBY[0:64, 128 * k:128 * k + 128], [[-16, 2], [0, 16 - QX], [-1, 16]], 0, ["TBY%d" % k])
+    op("g", lambda: g.iota(T.LOI[:, 0:64], [[1, 16], [16, 16 - QX]], NX, 0), (), ["LOI"])
     iota(T.U8R[:], [[0, 2], [128, 8]], 0, ["U8R"])
     iota(T.KC[:], [[0, 16], [1, 8]], 0, ["KC"])
-    for l, buf in ((1, T.N1), (2, T.N2), (3, T.N3)):
-        iota(buf[:], [[1, 128 >> l], [0, 1 << l]], 0, ["N%d" % l])
-    iota(T.PD[:], [[-1, 8], [-8, 16]], 1, ["PD"])
-
     ms(T.ONES[:], 1.0, ["ONES"])
     ms(T.ZB[0:32, :], 192.0 / 32, ["ZBa"])
     ms(T.ZB[32:64, :], 1.0 / 128 / 32, ["ZBb"])
     ms(T.SW[:], 0.0, ["SW"])
-    ms(T.SP[:], 0.0, ["SP"])
-    ms(T.EW0[:], 0.0, ["EW0"])
-    ms(T.EW1[:], 0.0, ["EW1"])
-    ms(T.RN[:], 0.0, ["RN0", "RN1"])
-    ms(T.SP[:, 0::16], -float(1 << 25), ["SP"])
-    for i, sh in enumerate((1, 2, 3, 4)):
-        ts(T.CI[:, i:i + 1], T.PI[:], sh, None, A.arith_shift_right, None, ["PI"], ["CI%d" % i])
+    ms(T.C256[:], 1.0 / 256, ["C256"])
+    ms(T.C64[:], 1.0 / 64, ["C64"])
+    ms(T.M3[0:64, :], -3.0 / 64, ["M3"])
+    ms(T.OC[0:32, :], 192.0 / 32, ["OCa"])
+    ms(T.OC[32:64, :], -255.0 / 512 / 32, ["OCb"])
+
+    def fill(name, value, w):
+        op("g", lambda: g.iota(T[name][:], [[0, SCRATCH[name][1][1]]], value, 0, allow_small_or_imprecise_dtypes=True), (), w)
+
+    def keep(out, in_, pat, cmp, base, cm, r, w):
+        op("g", lambda: g.affine_select(out, in_, pat, cmp, 0.0, base, cm), r, w)
+
+    def band(name, src, pat, base, width):
+        keep(T[name][:], T[src][:], pat, A.is_ge, base, 1, [src], [name])
+        keep(T[name][:], T[name][:], [[-a, n] for a, n in pat], A.is_ge, width - 1 - base, -1, [name], [name])
+
+    iota(T.TBX[0:64, :], [[-16, 2], [0, QX], [-1, 16]], 0, ["TBX"])
+    for k in range(2):
+        iota(T.TBY[0:64, 128 * k:128 * k + 128], [[-16, 2], [0, 16 - QX], [-1, 16]], 0, ["TBY%d" % k])
+    keep(T.ID[:], T.ONES[:], [[-1, 128]], A.is_equal, 0, 1, ["ONES"], ["ID"])
+    fill("NID", -1, ["NID"])
+    keep(T.NID[:], T.NID[:], [[-1, 128]], A.is_equal, 0, 1, ["NID"], ["NID"])
+    fill("SP", -16000000, ["SP"])
+    keep(T.SP[:], T.SP[:], [[0, 2 * QX], [1, 16]], A.is_equal, 0, 0, ["SP"], ["SP"])
+
+    def late_constants():
+        for i in range(16):
+            keep(T.XR[:, XO + i::16], T.XT[:], [[0, 64]], A.is_equal, 0, 0, ["XT%d" % q for q in range(16 - QX)], [XYK[i]])
+        fill("RN", 0, ["RN0", "RN1"])
+        fill("EW0", 0, ["EW0"])
+        fill("EW1", 0, ["EW1"])
+        keep(T.OC[0:64, :], T.OC[0:64, :], [[0, 32], [1, 4]], A.is_equal, -3, 0, ["OCa", "OCb"], ["OCa", "OCb"])
+        fill("SS", 1, ["SS"])
+        fill("C260", 260, ["C260"])
+        keep(T.SS[:], T.SS[:], [[0, PW], [1, 8]], A.is_gt, 0, 0, ["SS"], ["SS"])
+        for i, v in enumerate((-1000000, -260, 0, 130)):
+            op("g", lambda i=i, v=v: g.iota(T.THR[:, i::4], [[0, 32]], v, 0, allow_small_or_imprecise_dtypes=True), (), ["THR%d" % i])
+        keep(T.LF0[:], T.C256[:], [[-1, 128]], A.is_equal, 0, 1, ["C256"], ["LF0"])
+        keep(T.ID64[:], T.C64[:], [[-1, 128]], A.is_equal, 0, 1, ["C64"], ["ID64"])
+        for l in range(3):
+            w = 1 << l
+            band("SB%d" % l, "C256", [[-2 * w, 64 // w], [w, 2], [0, w]], -w, w)
+            if l:
+                band("L%dB" % l, "ONES", [[-w, 128 // w], [0, w]], 0, w)
+
+    ts(T.CI[:, 3:4], T.PI[:], 4, None, A.arith_shift_right, None, ["PI"], ["CI3"])
     ts(T.CI[:, 4:5], T.PI[:], 15, None, A.bitwise_and, None, ["PI"], ["CI4"])
     ts(T.CI[:, 5:6], T.PI[:], 4, 1, A.arith_shift_right, A.bitwise_and, ["PI"], ["CI5"])
-    cp(T.CF[:, 0:6], T.CI[:, 0:6], ["CI%d" % i for i in range(6)], ["CF"])
+    cp(T.CF[:, 3:6], T.CI[:, 3:6], ["CI3", "CI4", "CI5"], ["CF"])
     gcol, icol, par1, par0, i8 = T.CF[:, 3:4], T.CF[:, 4:5], T.CF[:, 5:6], T.CF[:, 6:7], T.CF[:, 7:8]
     ts(par0, par1, -1.0, 1.0, A.mult, A.add, ["CF"], ["par0"])
     ts(i8, icol, 8.0, None, A.mult, None, ["CF"], ["i8"])
@@ -258,6 +290,13 @@ def rank_program(g, core, T, topo):
         for c2 in range(2):
             ts(PM[g2][c2][:], T.DD[:], 16.0 * (c2 - g2), par1 if c2 else par0, A.is_equal, A.mult,
                ["DD", "CF", "par0"], ["PM%d%d" % (g2, c2)])
+    ts(T.SW[:, 15:143:16], T.BI[:], -2048.0, None, A.mult, None, ["BI"], ["SW"])
+    cp(T.XL[:], T.LOI[:, 0:64], ["LOI"], ["XL"])
+    ts(T.BN[:], T.BI[:], -1.0, None, A.mult, None, ["BI"], ["BN"])
+    ts(T.OH[:], T.R16[:], icol, None, A.is_equal, None, ["R16", "CF"], ["OH"])
+    ts(T.J64[:], T.R16[:], icol, 64.0, A.is_equal, A.mult, ["R16", "CF"], ["J64"])
+    ts(T.U8[:], T.U8R[:], i8, None, A.add, None, ["U8R", "i8"], ["U8"])
+    ts(T.KN[:], T.KC[:], icol, None, A.is_equal, None, ["KC", "CF"], ["KN"])
 
     def bias_banks(names=("Z2", "Z3")):
         for z in names:
@@ -280,10 +319,13 @@ def rank_program(g, core, T, topo):
                 act(T.XR[:, i:XO:16], src, F.Identity, ["FR%d" % t], [XRK[i]], bias=192.0)
 
     def xrep_late(t):
-        act(T.XR[:, XO:XO + 2048], T.FR[:, 256 * t:256 * t + 256].indirect(T.XL[:]), F.Identity, ["FR%d" % t, "XL"], ["XY"], bias=192.0)
+        act(T.XR[:, XO:XO + 1024], T.FR[:, 256 * t:256 * t + 256].indirect(T.XL[:]), F.Identity, ["FR%d" % t, "XL"], XYK, bias=192.0)
 
     def x192(t):
-        act(T.X192[:, 256 * t:256 * t + 256], T.FR[:, 256 * t:256 * t + 256], F.Identity, ["FR%d" % t], ["X192_%d" % t], bias=192.0)
+        o, n = 256 * t, 256 if t == R - 1 else 128
+        act(T.X192[:, o:o + n], T.FR[:, o:o + n], F.Identity, ["FR%d" % t], ["X192_%d" % t], bias=192.0)
+        if n == 128:
+            act(T.X192[:, o + n:o + 256], T.FR[:, o + n:o + 256], F.Identity, ["FR%d" % t], ["X192n%d" % t], bias=-192.0, scale=-1.0)
 
     def lists(src, key):
         for h in range(2):
@@ -308,22 +350,26 @@ def rank_program(g, core, T, topo):
     def late_list():
         for c in range(8):
             o = 2 * NX + 16 * c
-            cp(T.CAND[:, 512 + c::8], T.CAND[:, o:o + 16], ["CAND"], [CYK[c]])
+            b = 512 + 64 * (c // 4)
+            cp(T.CAND[:, b + c % 4:b + 64:4], T.CAND[:, o:o + 16], ["CAND"], [CYK[c]])
 
-    def key_start():
-        mm("KX1", T.KX1[:, 0:2 * NX], T.ONES[0:64, :], T.TBX[0:64, :], True, False, ["ONES", "TBX"])
-        mm("KX2", T.KX2[:, 0:2 * NX], T.ONES[0:64, :], T.TBX[0:64, :], True, False, ["ONES", "TBX"])
-        mm("KY", T.KY[:, 0:256], T.ONES[0:64, :], T.TBY[0:64, :], True, False, ["ONES", "TBY0", "TBY1"])
+    def key_start(late):
+        if late:
+            mm("KY", T.KY[:, 0:256], T.ONES[0:64, :], T.TBY[0:64, :], True, False, ["ONES", "TBY0", "TBY1"])
         for k, (src, name) in enumerate(((T.THI, "THI"), (T.TLO, "TLO"))):
             kx = "KX%d" % (k + 1)
+            if not late:
+                mm(kx, T[kx][:, 0:2 * NX], T.ONES[0:64, :], T.TBX[0:64, :], True, False, ["ONES", "TBX"])
             for h in range(2):
                 for g2 in range(2):
                     r = [name, "PM%d%d" % (g2, h)]
-                    mm(kx, T[kx][:, h * NX:h * NX + NX], PM[g2][h][:], src[:, 0:QX, g2, :], False, False, r)
                     o = 128 * k + 64 * h
-                    mm("KY", T.KY[:, o:o + 64], PM[g2][h][:], src[:, QX:16, g2, :], False, False, r)
+                    if late:
+                        mm("KY", T.KY[:, o:o + 64], PM[g2][h][:], src[:, QX:16, g2, :], False, False, r)
+                    else:
+                        mm(kx, T[kx][:, h * NX:h * NX + NX], PM[g2][h][:], src[:, 0:QX, g2, :], False, False, r)
 
-    bias_banks()
+    bias_banks(["Z2"])
     op("v", lambda: V.transpose(T.TA[:], T.A0[:]), ["A0"], ["TA"])
     for c in range(8):
         for g2 in range(2):
@@ -332,46 +378,24 @@ def rank_program(g, core, T, topo):
     cp(T.SF[:], T.S0[:], ["S0"], ["SF"])
     lists(T.S0, "S0")
     ts(T.ATS[:], T.Z1[:, 0:128], 1.0 / 64, None, A.mult, None, [], ["ATS"], ["Z1"])
-    ts(T.SW[:, 15:143:16], T.BI[:], -2048.0, None, A.mult, None, ["BI"], ["SW"])
-    cp(T.XL[:], T.LOI[:, 0:128], ["LOI"], ["XL"])
     expand()
+    for q in range(16 - QX):
+        act(T.XT[:, q::16 - QX], T.FR[:, NX + 16 * q:NX + 16 * q + 16], F.Identity, ["FR0"], ["XT%d" % q], bias=192.0)
     x192(0)
-    xrep_late(0)
-    xrep(0, range(0, 16), "v")
-    ts(T.ID[:], T.DD[:], 0.0, None, A.is_equal, None, ["DD"], ["ID"])
-    ts(T.NID[:], T.DD[:], 0.0, -1.0, A.is_equal, A.mult, ["DD"], ["NID"])
-    ts(T.BN[:], T.BI[:], -1.0, None, A.mult, None, ["BI"], ["BN"])
-    ts(T.OH[:], T.R16[:], icol, None, A.is_equal, None, ["R16", "CF"], ["OH"])
-    ts(T.U8[:], T.U8R[:], i8, None, A.add, None, ["U8R", "i8"], ["U8"])
-    ts(T.KN[:], T.KC[:], icol, None, A.is_equal, None, ["KC", "CF"], ["KN"])
+    xrep(0, range(0, 8), "s")
+    late_constants()
+    xrep(0, range(8, 16), "v")
+    cp(T.MIX[:, 1024:1028], T.MIX[:, 0:4], ["MIX"], ["MIXW"])
     cp(T.MIXF[:, 0:1028], T.MIX[:, 0:1028], ["MIX", "MIXW"], ["MIXF"])
     candidates()
     candidate_list()
     late_list()
-    key_start()
 
-    def owner_constants():
-        ts(T.ID64[:], T.DD[:], 0.0, 1.0 / 64, A.is_equal, A.mult, ["DD"], ["ID64"])
-        ts(T.LF0[:], T.DD[:], 0.0, 1.0 / 256, A.is_equal, A.mult, ["DD"], ["LF0"])
-        for l in (1, 2, 3):
-            ts(T["LF%d" % l][:], T["N%d" % l][:], T.CF[:, l - 1:l], 1.0 / 256, A.is_equal, A.mult, ["N%d" % l, "CF"], ["LF%d" % l])
-        for l in (1, 2):
-            ts(T["L%dB" % l][:], T["N%d" % l][:], T.CF[:, l - 1:l], None, A.is_equal, None, ["N%d" % l, "CF"], ["L%dB" % l])
-        ms(T.OC[0:64, :], 0.0, ["OCa", "OCb"])
-        ms(T.M3[0:64, :], -3.0 / 64, ["M3"])
-        ms(T.SS[:], 1.0, ["SS"])
-        ms(T.C260[:], 260.0, ["C260"])
-        for i, v in enumerate((-1.0e6, -260.0, 0.0, 130.0)):
-            ms(T.THR[:, i::4], v, ["THR%d" % i])
-        for l in range(3):
-            tt(T["SB%d" % l][:], T["LF%d" % (l + 1)][:], T["LF%d" % l][:], A.subtract, ["LF%d" % l, "LF%d" % (l + 1)], ["SB%d" % l])
-        ms(T.OC[0:32, 3:128:4], 192.0 / 32, ["OCa"])
-        ms(T.OC[32:64, 3:128:4], -255.0 / 512 / 32, ["OCb"])
-        ms(T.SS[:, 0::8], 0.0, ["SS"])
 
     own_s = [(0, "Z0"), (2, "Z1"), (4, "Z3")]
     chunks = [(0, 2), (2, 4), (4, 6), (6, 8)] + [(c, c + 4) for c in range(8, 2 * QX, 4)]
-    zbank = {0: "Z2", 3: "Z3", 6: "Z2", 1: "Z0", 2: "Z1", 4: "Z0", 5: "Z1", 7: "Z0"}
+    zfirst = {0: "Z0", 1: "Z1", 2: "Z3", 3: "Z0", 4: "Z1", 5: "Z3", 6: "Z0", 7: "Z2"}
+    zlater = {0: "Z2", 3: "Z3", 6: "Z2", 1: "Z0", 2: "Z1", 4: "Z0", 5: "Z1", 7: "Z0"}
 
     def qof(c):
         return c % QX if c < 2 * QX else QX + (c - 2 * QX) % (16 - QX)
@@ -379,9 +403,13 @@ def rank_program(g, core, T, topo):
     for t in range(R):
         last = t == R - 1
         vplan = {0: [("d", 0)], 3: [("d", 3), ("c", 1), ("c", 2)], 6: [("d", 6), ("c", 4)], 7: [("c", 5), ("c", 7)]}
-        for c in (1, 0, 2, 3, 4, 5, 6, 7):
+        SCL, zbank, order = [1, 2, 4, 5, 7], zlater, (1, 0, 2, 3, 4, 5, 6, 7)
+        if t == 0:
+            SCL, zbank, order = list(range(7)), zfirst, (0, 1, 2, 3, 4, 5, 7, 6)
+            vplan = {5: [("c", c) for c in range(5)], 6: [("d", 7), ("c", 5), ("c", 6)]}
+        for c in order:
             z = zbank[c]
-            if c == 4:
+            if c == 5 and t:
                 bias_banks([zbank[6]])
             mm(z, T[z][:], T.BD[:, c::8], T.MU[:, 512 * c:512 * c + 512], c in SCL, True, BDK + ["MU%d" % (c // 2)])
             if c in SCL:
@@ -393,6 +421,9 @@ def rank_program(g, core, T, topo):
                     ts(dst, T[zd][:], 184.0, 199.0, A.max, A.min, [], [MTK[d]], [zd])
                 else:
                     ts(dst, dst, 184.0, 199.0, A.max, A.min, [MTK[d]], [MTK[d]])
+        if t == 0:
+            key_start(False)
+            key_start(True)
         for c0, z in own_s:
             mc = T.D[:, 256 * c0:256 * c0 + 512]
             act(mc, T.MT[:, 0:4096].indirect(T.CAND[:, 16 * c0:16 * c0 + 32]), F.Identity, MTK + ["CAND"], ["D%d" % c0])
@@ -416,23 +447,22 @@ def rank_program(g, core, T, topo):
                 for j in range(16):
                     mm(name, T[name][:, 16 * b0:16 * c1], T.SW[:, 15 - j:143 - j], T.SQ[:, b0:c1, j, :], False,
                        c1 == 2 * QX and j == 15, r)
-        for j0, j1 in ((0, 8), (8, 12), (12, 14), (14, 16)):
-            a, b = 128 * j0, 128 * j1
-            if j0 == 12:
-                for k, rx in enumerate((T.RX1, T.RX2)):
-                    kx = "KX%d" % (k + 1)
-                    scan(rx[:], T.SP[:], T[kx][:, 0:2 * NX], A.add, A.max, ["SP"], ["RX%d" % k], [kx])
-            tt(T.D[:, YO + a:YO + b], T.MT[:, 0:4096].indirect(T.CAND[:, 512 + 8 * j0:512 + 8 * j1]),
-               T.XR[:, XO + a:XO + b], A.subtract, MTK + CYK + ["XY"], ["DY%d" % j0])
-            act(T.SQY[:, a:b], T.D[:, YO + a:YO + b], F.Square, ["DY%d" % j0], ["SY%d" % j0])
+        for h, j0, j1 in ((0, 0, 8), (0, 8, 16), (1, 0, 8), (1, 8, 12), (1, 12, 16)):
+            a, b, key = 1024 * h + 64 * j0, 1024 * h + 64 * j1, "%d_%d" % (h, j0)
+            tt(T.D[:, YO + a:YO + b], T.MT[:, 0:4096].indirect(T.CAND[:, 512 + a // 16:512 + b // 16]),
+               T.XR[:, XO + 64 * j0:XO + 64 * j1], A.subtract, MTK + CYK + XYK, ["DY" + key])
+            act(T.SQY[:, a:b], T.D[:, YO + a:YO + b], F.Square, ["DY" + key], ["SY" + key])
             for j in range(j0, j1):
                 for k in range(2):
-                    mm("KY", T.KY[:, 128 * k:128 * k + 128], T.SW[:, 15 - j:143 - j], T.SQY[:, 128 * j:128 * j + 128], False,
-                       j == 15 and k == 1, ["SW", "SY%d" % j0])
+                    o, i = 128 * k + 64 * h, 1024 * h + 64 * j
+                    mm("KY", T.KY[:, o:o + 64], T.SW[:, 15 - j:143 - j], T.SQY[:, i:i + 64], False,
+                       h == 1 and j == 15 and k == 1, ["SW", "SY" + key])
         for k, rx in enumerate((T.RX1, T.RX2)):
-            tt(T.KI[:, 16 * k:16 * k + QX], rx[:, 15:NX:16], rx[:, NX + 15:2 * NX:16], A.max, ["RX%d" % k], ["KIa%d" % k])
-        tt(T.HS[:, 0:QX], T.RX1[:, NX + 15:2 * NX:16], T.RX1[:, 15:NX:16], A.is_gt, ["RX0"], ["HSa"])
+            kx = "KX%d" % (k + 1)
+            scan(rx[:], T.SP[:], T[kx][:, 0:2 * NX], A.add, A.max, ["SP"], ["RX%d" % k], [kx])
+        tt(T.KI[:, 0:QX], T.RX1[:, 15:NX:16], T.RX1[:, NX + 15:2 * NX:16], A.max, ["RX0"], ["KIa0"])
         scan(T.RY[:], T.SP[:, 0:256], T.KY[:, 0:256], A.add, A.max, ["SP"], ["RY"], ["KY"])
+        tt(T.KI[:, 16:16 + QX], T.RX2[:, 15:NX:16], T.RX2[:, NX + 15:2 * NX:16], A.max, ["RX1"], ["KIa1"])
         for k in range(2):
             o = 128 * k
             tt(T.KI[:, 16 * k + QX:16 * k + 16], T.RY[:, o + 15:o + 64:16], T.RY[:, o + 79:o + 128:16], A.max, ["RY"], ["KIb%d" % k])
@@ -446,15 +476,24 @@ def rank_program(g, core, T, topo):
         cp(T.CL16[:], T.CL[:], ["CL"], ["CL16"])
         cp(T.SC16[:], T.SCF[:], ["SCF"], ["SC16"])
         xs = T.X192[:, 256 * t:256 * t + 256]
-        tt(T.NE[:], T.MT[:, 0:4096].indirect(T.W16[:]), xs, A.subtract, MTK + ["W16", "X192_%d" % t], ["NE"])
-        act(T.MW[:], T.MU[:, 0:4096].indirect(T.W16[:]), F.Identity, MUK + ["W16"], ["MW"])
-        masked, plain = ((T.MW, "MW"), (T.NE, "NE")) if last else ((T.NE, "NE"), (T.MW, "MW"))
-        for h in range(2):
-            cp(T["EW%d" % h][:, 0:1024].indirect(T.SC16[:, 8 * h:8 * h + 8]), masked[0][:, 128 * h:128 * h + 128],
-               [masked[1], "SC16"], ["EW%d" % h])
+        win = [T["EW%d" % h][:, 0:1024].indirect(T.SC16[:, 8 * h:8 * h + 8]) for h in range(2)]
+        if last:
+            tt(T.NE[:], T.MT[:, 0:4096].indirect(T.W16[:]), xs, A.subtract, MTK + ["W16", "X192_%d" % t], ["NE", "NE1"])
+            act(T.MW[:], T.MU[:, 0:4096].indirect(T.W16[:]), F.Identity, MUK + ["W16"], ["MW"])
+            for h in range(2):
+                cp(win[h], T.MW[:, 128 * h:128 * h + 128], ["MW", "SC16"], ["EW%d" % h])
+            plain = (T.NE, "NE")
+        else:
+            tt(T.NE[:, 0:128], T.MT[:, 0:4096].indirect(T.W16[:, 0:8]), T.X192[:, 256 * t:256 * t + 128], A.subtract,
+               MTK + ["W16", "X192_%d" % t], ["NE"])
+            act(T.NE[:, 128:256], T.MT[:, 0:4096].indirect(T.W16[:, 8:16]), F.Identity, MTK + ["W16"], ["NE1"])
+            act(T.MW[:], T.MU[:, 0:4096].indirect(T.W16[:]), F.Identity, MUK + ["W16"], ["MW"])
+            cp(win[0], T.NE[:, 0:128], ["NE", "SC16"], ["EW0"])
+            tt(win[1], T.NE[:, 128:256], T.X192[:, 256 * t + 128:256 * t + 256], A.add, ["NE1", "SC16", "X192n%d" % t], ["EW1"])
+            plain = (T.MW, "MW")
         act(T.FN[:], T.OH[:, 0:16].indirect(T.CL16[:]), F.Identity, ["OH", "CL16"], ["FN", "NCOL"], accum_out=T.NCOL[:, 0:1])
         for s in range(2):
-            act(T.RN[:, 32 + s::PW], T.BN[:, s::2], F.Identity, ["BN", "NCOL"], ["RN%d" % s], scale=T.NCOL[:, 0:1])
+            ts(T.RN[:, 32 + s::PW], T.BN[:, s::2], T.NCOL[:, 0:1], None, A.mult, None, ["BN", "NCOL"], ["RN%d" % s])
         for h in range(2):
             mm("KY", T.KY[:, 128 * h:128 * h + 128], plain[0][:, 128 * h:128 * h + 128], T.ID[:], True, True, [plain[1], "ID"])
         act(T.PT[:], T.KY[:, 0:256], F.Copy, [], ["PT"], ["KY"])
@@ -480,7 +519,7 @@ def rank_program(g, core, T, topo):
 
         tr = []
         for i, hc in enumerate(helpers):
-            eng = topo.engines(core, hc)
+            eng = [e for e in topo.engines(core, hc) if e not in topo.engines(core, mine[(me + 1) % 4])]
             half = len(eng) // 2
             tr.append(RemoteDMATransfer(dst_ids=[_dst(topo, hc, core)], dma_engine_mask=_mask(eng[i * half:(i + 1) * half]),
                                         remote_sem=T.sem["hin%d" % t], src=Pt[:, 2 * i * PW:(2 * i + 2) * PW], dst=T["HB%d" % t][:]))
@@ -499,9 +538,8 @@ def rank_program(g, core, T, topo):
         ext("rd%d" % t, ne, ["LD%d" % t])
         ext("rh%d" % t, 4 * (ne // 2), ["LH%d" % t])
 
-        if t == 0:
-            owner_constants()
         mm("Z0", T.Z0[:, 0:128], T.ONES[0:64, :], T.OC[0:64, :], True, False, ["ONES", "OCa", "OCb"])
+        tt(T.HS[:, 0:QX], T.RX1[:, NX + 15:2 * NX:16], T.RX1[:, 15:NX:16], A.is_gt, ["RX0"], ["HSa"])
         tt(T.HS[:, QX:16], T.RY[:, 79:128:16], T.RY[:, 15:64:16], A.is_gt, ["RY"], ["HSb"])
         tt(T.SF[:], T.SF[:], T.HS[:], A.add, ["SF", "HSa", "HSb"], ["SF"])
         if not last:
@@ -510,7 +548,7 @@ def rank_program(g, core, T, topo):
             bias_banks()
             lists(T.SF, "SF")
             candidates()
-            candidate_list()
+            key_start(False)
             x192(t + 1)
             xrep(t + 1, range(16), "s")
             xrep_late(t + 1)
@@ -558,14 +596,14 @@ def rank_program(g, core, T, topo):
         op("g", lambda tr=tr: g.remote_dma_fused(tr, local_sem=T.sem.sent), ["DLo%d" % t])
         ext("ag%d" % t, 3 * ne, ["DLr%d" % t])
         if not last:
+            candidate_list()
             late_list()
             for h in range(2):
-                ms(T["EW%d" % h][:], 0.0, ["EW%d" % h])
+                fill("EW%d" % h, 0, ["EW%d" % h])
             if t == 0:
-                ts(T.PERM[:], T.PD[:], 0.0, None, A.is_equal, None, ["PD"], ["PERM"])
-                ts(T.J64[:], T.R16[:], icol, 64.0, A.is_equal, A.mult, ["R16", "CF"], ["J64"])
-                ms(T.M192[0:64, :], -3.0, ["M192"])
-            key_start()
+                keep(T.PERM[:], T.ONES[:], [[-1, 8], [-8, 16]], A.is_equal, 0, 1, ["ONES"], ["PERM"])
+                op("g", lambda: g.iota(T.M192[0:64, :], [[0, 128]], -3, 0, allow_small_or_imprecise_dtypes=True), (), ["M192"])
+            key_start(True)
             mm("Z1", T.Z1[:, 0:128], DL[:], T.ID64[:], False, True, ["DLo%d" % t, "DLr%d" % t, "ID64"])
             ts(T.ATS[:], T.Z1[:, 0:128], -127.0 / 64, 127.0 / 64, A.max, A.min, [], ["ATS"], ["Z1"])
             expand()

@@ -1,11 +1,13 @@
 from concourse.bass import DstId, RemoteDMATransfer
 from concourse.mybir import AluOpType as A
 from concourse.mybir import ActivationFunctionType as F
+from concourse.mybir import AxisListType as X
 
 R = 3
-PW = 34
-QX = 12
-BF, F32, I32, U16 = "bfloat16", "float32", "int32", "uint16"
+PW = 32
+QX = 14
+NS = 3
+BF, F32, F16, I32, U16 = "bfloat16", "float32", "float16", "int32", "uint16"
 
 SCRATCH = {}
 
@@ -15,26 +17,30 @@ def _sb(dtype, **kw):
         SCRATCH[k] = ("sbuf", [128] + (v if isinstance(v, list) else [v]), dtype)
 
 
-_sb(BF, MU=4096, MT=4096, FR=768, X192=768, A0=128, TA=128, XR=256 * QX + 1024, D=8192, SQ=[2 * QX, 16, 16], SQY=2048, HI=512, LO=512,
-    THI=[16, 2, 16], TLO=[16, 2, 16], ATS=128, BD=1024, NE=256, MW=256, EW0=1024, EW1=1024, ET0=1024, ET1=1024,
-    PT=256, FN=256, RN=4 * PW, NR=32, DL0=128, DL1=128, DL2=128,
-    ONES=128, ID=128, NID=128, C64=128, XT=64, ID64=128, PERM=128, P00=128, P01=128, P10=128, P11=128, SW=144, J64=16, OH=16, KN=128,
-    ZB=512, OC=128, M3=128, M192=128, TBX=32 * QX, TBY=256, L1B=128, L2B=128)
-_sb(F32, MIXF=1032, CF=16, DD=128, KC=128, R16=16, C256=128, BI=8, BN=8, U8=16, U8R=16,
-    SP=32 * QX, SS=8 * PW, RX1=32 * QX, RX2=32 * QX, RY=256, H64=16, SCF=16, HS=16, SF=16,
-    OUT=64, OUTT=64, NCOL=4, LB=8 * PW, LBS=8 * PW, C260=16, THR=128, UU=128, DS=128,
-    LF0=128, SB0=128, SB1=128, SB2=128, YA=128)
-_sb(I32, MIX=1032, S0=16, PI=1, CI=8, LOI=512, KI=32, HL=32, CL=16, SI=16, SJ=16)
-_sb(U16, LS1=32, LS2=32, CAND=640, XL=64, W16=16, SC16=16, CL16=16)
+_sb(BF, MU=4096, MT=4096, FR=768, X192=256, A0=128, TA=128, XR=256 * QX + 1024, D=8192, SQ=[2 * QX, 16, 16], SQY=1024,
+    ATS=128, BD=[8, 128], NE=256, MW=256, EW0=1024, EW1=1024, ET0=[8, 128], ET1=[8, 128],
+    PT=256, FN=256, ZR=128, UB=128, EX=256, KE=256, C260=128, LEV=128, DL0=128, DL1=128, DL2=128, NM=512,
+    ONES=512, ID=128, XT=64, ID64=128, P00=128, P01=128, P10=128, P11=128,
+    N00=128, N01=128, N10=128, N11=128, SW=144, J64=16, OH=16,
+    ZB=128, OC=32, M3=128, M192=128, TB=320, L1B=128, L2B=128, M16=128)
+_sb(F16, WG=512, TT=[16, 2, 16])
+_sb(F32, CF=16, DD=128, KA=128, R16=16, BI=8, U4=16, U4R=16,
+    SP=256, SS=128, R1=512, R2=512, TW=512, SCF=16, SF=16,
+    OUT=64, OUTT=64, LA=128, LB=128, LAS=128, LBS=128, NT=4, BL=48, SEL=256, YA=128)
+_sb(I32, MIX=1032, S0=16, PI=1, CI=8, LOI=64, SI=16, SJ=16, HS=16)
+_sb(U16, LS2=32, CAND=512, XL=64, W16=16, SC16=16, CL16=16)
 for _t in range(R):
     _sb(U16, **{"P%d" % _t: 4 * PW, "LD%d" % _t: 4 * PW, "LH%d" % _t: 4 * PW, "HB%d" % _t: 2 * PW})
-for _n in ("Z0", "Z1", "Z2", "Z3", "KX1", "KX2", "KY"):
+    _sb(F32, **{"NC%d" % _t: 32, "HC%d" % _t: 4})
+for _n in ("Z0", "Z1", "K1", "K2", "K3"):
     SCRATCH[_n] = ("psum", [128, 512], F32)
-SCRATCH["ZT"] = ("psum", [128, 1024], BF)
+SCRATCH["Z2"] = ("psum", [128, 8, 64], F32)
+for _n in ("ZT0", "ZT1"):
+    SCRATCH[_n] = ("psum", [128, 8, 128], BF)
 
 SEMAPHORES = ["qv", "qs", "qp", "qg", "sent", "d_s0", "d_fr0", "d_fr1", "d_a0", "d_mix", "d_mu0", "d_mu1", "d_mu2", "d_mu3",
               "d_o0", "d_o1", "d_ya"]
-SEMAPHORES += ["%s%d" % (n, t) for t in range(R) for n in ("rd", "rh", "ag", "hin")]
+SEMAPHORES += ["%s%d" % (n, t) for t in range(R) for n in ("rd", "rh", "ag", "hin", "cin", "cn")]
 
 
 def _mask(engines):
@@ -62,23 +68,31 @@ def _dst(topo, dst, src):
     return DstId(rid=rid, pnc=pid)
 
 
+def _hop_engines(topo, rank, helper, peer, t):
+    return [e for e in topo.engines(rank, helper) if e not in topo.engines(rank, peer)]
+
+
 def helper_program(g, core, owner, T, topo, planes):
     mine, other, helpers = planes[owner]
     h, k = helpers.index(core), mine.index(owner)
-    n_in = len([e for e in topo.engines(owner, core) if e not in topo.engines(owner, mine[(k + 1) % 4])]) // 2
     total = 0
+    rank = T.rank_of(owner)
     for t in range(R):
-        g.wait_ge(T.sem["hin%d" % t], n_in)
-        tr = []
-        for i in range(2):
-            dst = other[2 * h + i]
-            eng = topo.engines(core, dst)
-            half = len(eng) // 2
-            tr.append(RemoteDMATransfer(dst_ids=[_dst(topo, dst, core)], dma_engine_mask=_mask(eng[i * half:(i + 1) * half]),
-                                        remote_sem=T.sem["rh%d" % t], src=T["HB%d" % t][:, i * PW:(i + 1) * PW],
-                                        dst=T["LH%d" % t][:, k * PW:(k + 1) * PW]))
-            total += half
-        g.remote_dma_fused(tr, local_sem=T.sem.sent)
+        for sums in (False, True):
+            g.wait_ge(T.sem[("hin%d" if sums else "cin%d") % t], len(_hop_engines(topo, owner, core, mine[(k + 1) % 4], t)) // 2)
+            tr = []
+            for i in range(2):
+                dst = other[2 * h + i]
+                eng = topo.engines(core, dst)
+                half = len(eng) // 2
+                if sums:
+                    sem, src, land = "rh%d", T["HB%d" % t][:, i * PW:(i + 1) * PW], T["LH%d" % t][:, k * PW:(k + 1) * PW]
+                else:
+                    sem, src, land = "cn%d", T["HC%d" % t][:], T["NC%d" % t][:, 4 * rank:4 * rank + 4]
+                tr.append(RemoteDMATransfer(dst_ids=[_dst(topo, dst, core)], dma_engine_mask=_mask(eng[i * half:(i + 1) * half]),
+                                            remote_sem=T.sem[sem % t], src=src, dst=land))
+                total += half
+            g.remote_dma_fused(tr, local_sem=T.sem.sent)
     g.wait_ge(T.sem.sent, total)
 
 
@@ -151,6 +165,43 @@ def _emit(ops, g, T):
             ins.then_inc(T.sem["q" + o["e"]], 1)
 
 
+def _weave(ops, plans):
+    made = []
+    for plan in plans:
+        steps = []
+        for fn, *args in plan:
+            start = len(ops)
+            fn(*args)
+            steps.append(ops[start:])
+            del ops[start:]
+        made.append(steps)
+    pending = {k for steps in made for s in steps for o in s for k in o["w"]}
+    full, reads = set(), {}
+    while any(made):
+        for steps in made:
+            if not steps:
+                continue
+            s = steps[0]
+            wrote = {k for o in s for k in o["w"]}
+            banks = {k for o in s for k in o["b"]}
+            on_p = s[0]["e"] == "p"
+            if any(k in pending and k not in wrote for o in s for k in o["r"]) or any((k in full) == on_p for k in banks):
+                continue
+            ops.extend(steps.pop(0))
+            pending -= wrote
+            for k in banks:
+                if on_p and any(o.get("stop") for o in s if k in o["b"]):
+                    full.add(k)
+                    reads[k] = max(o.get("stop", 0) for o in s)
+                elif not on_p:
+                    reads[k] -= 1
+                    if not reads[k]:
+                        full.discard(k)
+            break
+        else:
+            raise ValueError("the queues' orders contradict one another")
+
+
 def rank_program(g, core, T, topo):
     planes = _layout(T, topo)
     if T.rank_of(core) is None:
@@ -159,7 +210,7 @@ def rank_program(g, core, T, topo):
                 helper_program(g, core, c, T, topo, planes)
         return
     mine, other, helpers = planes[core]
-    me = mine.index(core)
+    me, rank = mine.index(core), T.rank_of(core)
     V, S, P = g.vector, g.scalar, g.tensor
     ops = []
     sent = [0]
@@ -192,7 +243,8 @@ def rank_program(g, core, T, topo):
         op("s", lambda: S.activation(out, in_, func, **kw), r, w, b)
 
     def mm(bank, out, lhsT, rhs, start, stop, r):
-        op("p", lambda: P.matmul(out, lhsT, rhs, start, stop), r, (), [bank])
+        op("p", lambda: P.matmul(out, lhsT, rhs, start, bool(stop)), r, (), [bank])
+        ops[-1]["stop"] = int(stop)
 
     def iota(out, pat, cm, w, fl=True):
         if fl:
@@ -208,16 +260,18 @@ def rank_program(g, core, T, topo):
     XRK = ["XR%d" % i for i in range(16)]
     BDK = ["BD%d" % i for i in range(8)]
     PM = [[T.P00, T.P01], [T.P10, T.P11]]
+    NM = [[T.N00, T.N01], [T.N10, T.N11]]
     MUK = ["MU%d" % i for i in range(4)]
-    SCL = [1, 2, 4, 5, 7]
     NX = 16 * QX
     XO, YO = 16 * NX, 32 * NX
     XYK = ["XY%d" % i for i in range(16)]
-    CYK = ["CY%d" % i for i in range(8)]
+    CYK = ["CY%d" % i for i in range(4)]
+    HK = [["K1"], ["K2", "K3"]]
+    CLASS_OF = 4.0 - 255.5 / 512
 
-    dma("s", T.S0[:], T.s0[:], "d_s0", w=["S0"])
-    dma("y", T.MIX[:, 0:1024], T.mix[:], "d_mix", w=["MIX"])
     dma("s", T.A0[:], T.a0[:], "d_a0", w=["A0"])
+    dma("y", T.MIX[:, 0:1024], T.mix[:], "d_mix", w=["MIX"])
+    dma("s", T.S0[:], T.s0[:], "d_s0", w=["S0"])
     dma("s", T.FR[:, 0:256], T.fr[:, 0:256], "d_fr0", w=["FR0"])
     for i in range(4):
         dma("y", T.MU[:, 1024 * i:1024 * i + 1024], T.mu[:, 1024 * i:1024 * i + 1024], "d_mu%d" % i, w=[MUK[i]])
@@ -226,21 +280,25 @@ def rank_program(g, core, T, topo):
     iota(T.PI[:], [[0, 1]], 1, ["PI"], False)
     iota(T.DD[:], [[-1, 128]], 1, ["DD"])
     iota(T.R16[:], [[1, 16]], 0, ["R16"])
-    op("g", lambda: g.iota(T.LOI[:, 0:64], [[1, 16], [16, 16 - QX]], NX, 0), (), ["LOI"])
-    iota(T.U8R[:], [[0, 2], [128, 8]], 0, ["U8R"])
-    iota(T.KC[:], [[0, 16], [1, 8]], 0, ["KC"])
+    iota(T.U4R[:], [[0, 2], [16, 8]], 0, ["U4R"])
+    iota(T.KA[:], [[0, 8], [1, 16]], 0, ["KA"])
+    op("g", lambda: g.iota(T.LOI[:], [[1, 16], [16, 2], [0, 2]], NX, 0), (), ["LOI"])
     ms(T.ONES[:], 1.0, ["ONES"])
     ms(T.ZB[0:32, :], 192.0 / 32, ["ZBa"])
     ms(T.ZB[32:64, :], 1.0 / 128 / 32, ["ZBb"])
     ms(T.SW[:], 0.0, ["SW"])
-    ms(T.C256[:], 1.0 / 256, ["C256"])
-    ms(T.C64[:], 1.0 / 64, ["C64"])
-    ms(T.M3[0:64, :], -3.0 / 64, ["M3"])
-    ms(T.OC[0:32, :], 192.0 / 32, ["OCa"])
-    ms(T.OC[32:64, :], -255.0 / 512 / 32, ["OCb"])
+    ones = T.ONES[:, 0:128]
+    act(T.M3[0:64, :], T.ONES[0:64, 0:128], F.Identity, ["ONES"], ["M3"], scale=-3.0 / 64)
+    act(T.OC[0:32, :], T.ONES[0:32, 0:32], F.Identity, ["ONES"], ["OCa"], scale=192.0 / 32)
+    act(T.OC[32:64, :], T.ONES[32:64, 0:32], F.Identity, ["ONES"], ["OCb"], scale=-255.0 / 512 / 32)
+    for t in range(R):
+        act(T["NC%d" % t][:, 4 * rank:4 * rank + 4], T.ONES[:, 0:4], F.Identity, ["ONES"], ["NCz", "NC%d0" % t, "NC%d1" % t], scale=0.0)
 
     def fill(name, value, w):
-        op("g", lambda: g.iota(T[name][:], [[0, SCRATCH[name][1][1]]], value, 0, allow_small_or_imprecise_dtypes=True), (), w)
+        n = 1
+        for k in SCRATCH[name][1][1:]:
+            n *= k
+        op("g", lambda: g.iota(T[name][:], [[0, n]], value, 0, allow_small_or_imprecise_dtypes=True), (), w)
 
     def keep(out, in_, pat, cmp, base, cm, r, w):
         op("g", lambda: g.affine_select(out, in_, pat, cmp, 0.0, base, cm), r, w)
@@ -249,63 +307,67 @@ def rank_program(g, core, T, topo):
         keep(T[name][:], T[src][:], pat, A.is_ge, base, 1, [src], [name])
         keep(T[name][:], T[name][:], [[-a, n] for a, n in pat], A.is_ge, width - 1 - base, -1, [name], [name])
 
-    iota(T.TBX[0:64, :], [[-16, 2], [0, QX], [-1, 16]], 0, ["TBX"])
-    for k in range(2):
-        iota(T.TBY[0:64, 128 * k:128 * k + 128], [[-16, 2], [0, 16 - QX], [-1, 16]], 0, ["TBY%d" % k])
-    keep(T.ID[:], T.ONES[:], [[-1, 128]], A.is_equal, 0, 1, ["ONES"], ["ID"])
-    fill("NID", -1, ["NID"])
-    keep(T.NID[:], T.NID[:], [[-1, 128]], A.is_equal, 0, 1, ["NID"], ["NID"])
-    fill("SP", -16000000, ["SP"])
-    keep(T.SP[:], T.SP[:], [[0, 2 * QX], [1, 16]], A.is_equal, 0, 0, ["SP"], ["SP"])
+    keep(T.ID[:], ones, [[-1, 128]], A.is_equal, 0, 1, ["ONES"], ["ID"])
 
     def late_constants():
+        iota(T.TB[0:64, 0:256], [[0, 8], [-1, 16], [-16, 2]], 0, ["TB0"])
+        iota(T.TB[0:64, 256:320], [[0, 2], [-1, 32]], 0, ["TB1"])
+        fill("SP", -16000000, ["SP"])
+        keep(T.SP[:], T.SP[:], [[0, 8], [1, 32]], A.is_equal, 0, 0, ["SP"], ["SP"])
         for i in range(16):
-            keep(T.XR[:, XO + i::16], T.XT[:], [[0, 64]], A.is_equal, 0, 0, ["XT%d" % q for q in range(16 - QX)], [XYK[i]])
-        fill("RN", 0, ["RN0", "RN1"])
+            keep(T.XR[:, XO + i::16], T.XT[:], [[0, 64]], A.is_equal, 0, 0, ["XT%d" % q for q in range(4)], [XYK[i]])
         fill("EW0", 0, ["EW0"])
+        fill("ZR", 0, ["ZR"])
         fill("EW1", 0, ["EW1"])
-        keep(T.OC[0:64, :], T.OC[0:64, :], [[0, 32], [1, 4]], A.is_equal, -3, 0, ["OCa", "OCb"], ["OCa", "OCb"])
         fill("SS", 1, ["SS"])
         fill("C260", 260, ["C260"])
-        keep(T.SS[:], T.SS[:], [[0, PW], [1, 8]], A.is_gt, 0, 0, ["SS"], ["SS"])
-        for i, v in enumerate((-1000000, -260, 0, 130)):
-            op("g", lambda i=i, v=v: g.iota(T.THR[:, i::4], [[0, 32]], v, 0, allow_small_or_imprecise_dtypes=True), (), ["THR%d" % i])
-        keep(T.LF0[:], T.C256[:], [[-1, 128]], A.is_equal, 0, 1, ["C256"], ["LF0"])
-        keep(T.ID64[:], T.C64[:], [[-1, 128]], A.is_equal, 0, 1, ["C64"], ["ID64"])
+        keep(T.SS[:], T.SS[:], [[0, PW], [1, 4]], A.is_gt, 0, 0, ["SS"], ["SS"])
+        iota(T.KE[:], [[1, 16], [0, 16]], 0, ["KE"])
+        fill("BL", 1, ["BL0", "BL1", "BL2"])
         for l in range(3):
-            w = 1 << l
-            band("SB%d" % l, "C256", [[-2 * w, 64 // w], [w, 2], [0, w]], -w, w)
-            if l:
-                band("L%dB" % l, "ONES", [[-w, 128 // w], [0, w]], 0, w)
+            w, part, key = 1 << l, T.BL[:, 16 * l:16 * l + 16], ["BL%d" % l]
+            keep(part, part, [[-16, 2], [-w, 8 // w], [0, w]], A.is_ge, -32 * me, 1, key, key)
+            keep(part, part, [[16, 2], [w, 8 // w], [0, w]], A.is_ge, w - 1 + 32 * me, -1, key, key)
+
+    def heights():
+        ts(T.LEV[:], T.M16[:], -96.0, 99.0, A.mult, A.add, ["M16"], ["LEV"])
+        tt(T.L1B[:], T.L1B[:], T.L2B[:], A.add, ["L1B", "L2B"], ["L1B"])
+        ts(T.EX[:], T.KE[:], icol, None, A.is_equal, None, ["KE", "CF"], ["EX"])
+        for name in ("ID", "L1B"):
+            tt(T.LEV[:], T.LEV[:], T[name][:], A.subtract, ["LEV", name], ["LEV"])
+
+    def tree_constants():
+        act(T.ID64[:], T.ID[:], F.Identity, ["ID"], ["ID64"], scale=1.0 / 64)
+        for l in (1, 2):
+            band("L%dB" % l, "M16", [[-16 << l, 8 >> l], [0, 16 << l]], 0, 16 << l)
+        op("g", lambda: g.iota(T.M192[0:64, :], [[0, 128]], -3, 0, allow_small_or_imprecise_dtypes=True), (), ["M192"])
 
     ts(T.CI[:, 3:4], T.PI[:], 4, None, A.arith_shift_right, None, ["PI"], ["CI3"])
     ts(T.CI[:, 4:5], T.PI[:], 15, None, A.bitwise_and, None, ["PI"], ["CI4"])
     ts(T.CI[:, 5:6], T.PI[:], 4, 1, A.arith_shift_right, A.bitwise_and, ["PI"], ["CI5"])
     cp(T.CF[:, 3:6], T.CI[:, 3:6], ["CI3", "CI4", "CI5"], ["CF"])
-    gcol, icol, par1, par0, i8 = T.CF[:, 3:4], T.CF[:, 4:5], T.CF[:, 5:6], T.CF[:, 6:7], T.CF[:, 7:8]
+    gcol, icol, par1, par0 = T.CF[:, 3:4], T.CF[:, 4:5], T.CF[:, 5:6], T.CF[:, 6:7]
     ts(par0, par1, -1.0, 1.0, A.mult, A.add, ["CF"], ["par0"])
-    ts(i8, icol, 8.0, None, A.mult, None, ["CF"], ["i8"])
     ts(T.BI[:], T.R16[:, 0:8], gcol, None, A.is_equal, None, ["R16", "CF"], ["BI"])
-    for g2 in range(2):
-        for c2 in range(2):
-            ts(PM[g2][c2][:], T.DD[:], 16.0 * (c2 - g2), par1 if c2 else par0, A.is_equal, A.mult,
-               ["DD", "CF", "par0"], ["PM%d%d" % (g2, c2)])
-    ts(T.SW[:, 15:143:16], T.BI[:], -2048.0, None, A.mult, None, ["BI"], ["SW"])
-    cp(T.XL[:], T.LOI[:, 0:64], ["LOI"], ["XL"])
-    ts(T.BN[:], T.BI[:], -1.0, None, A.mult, None, ["BI"], ["BN"])
     ts(T.OH[:], T.R16[:], icol, None, A.is_equal, None, ["R16", "CF"], ["OH"])
     ts(T.J64[:], T.R16[:], icol, 64.0, A.is_equal, A.mult, ["R16", "CF"], ["J64"])
-    ts(T.U8[:], T.U8R[:], i8, None, A.add, None, ["U8R", "i8"], ["U8"])
-    ts(T.KN[:], T.KC[:], icol, None, A.is_equal, None, ["KC", "CF"], ["KN"])
+    for c2 in (1, 0):
+        for g2 in range(2):
+            ts(PM[g2][c2][:], T.DD[:], 16.0 * (c2 - g2), par1 if c2 else par0, A.is_equal, A.mult,
+               ["DD", "CF", "par0"] if c2 == 0 else ["DD", "CF"], ["PM%d%d" % (g2, c2)])
+            act(NM[g2][c2][:], PM[g2][c2][:], F.Identity, ["PM%d%d" % (g2, c2)], ["NM%d%d" % (g2, c2)], scale=-1.0)
+    ts(T.SW[:, 15:143:16], T.BI[:], -2048.0, None, A.mult, None, ["BI"], ["SW"])
+    ts(T.U4[:], T.U4R[:], icol, 4096.0, A.add, A.mult, ["U4R", "CF"], ["U4"])
+    ts(T.M16[:], T.KA[:], icol, None, A.is_equal, None, ["KA", "CF"], ["M16"])
+    cp(T.XL[:], T.LOI[:], ["LOI"], ["XL"])
 
-    def bias_banks(names=("Z2", "Z3")):
-        for z in names:
-            mm(z, T[z][:], T.ONES[0:64, :], T.ZB[0:64, :], True, False, ["ONES", "ZBa", "ZBb"])
+    def bias_bank(z):
+        mm(z, T[z][:], T.ZB[0:64, :], T.ONES[0:64, :], True, False, ["ONES", "ZBa", "ZBb"])
 
     def expand():
         for gp in range(8):
-            out = T.BD[:, 128 * gp:128 * gp + 128]
-            if gp < 5:
+            out = T.BD[:, :, 16 * gp:16 * gp + 16]
+            if gp < 6:
                 ts(out, T.ATS[:], T.BI[:, gp:gp + 1], None, A.mult, None, ["ATS", "BI"], [BDK[gp]])
             else:
                 act(out, T.ATS[:], F.Identity, ["ATS", "BI"], [BDK[gp]], scale=T.BI[:, gp:gp + 1])
@@ -314,104 +376,95 @@ def rank_program(g, core, T, topo):
         src = T.FR[:, 256 * t:256 * t + NX]
         for i in which:
             if eng == "v":
-                ts(T.XR[:, i:XO:16], src, 192.0, None, A.add, None, ["FR%d" % t], [XRK[i]])
+                ts(T.XR[:, i:XO:16], src, -1.0, -192.0, A.mult, A.add, ["FR%d" % t], [XRK[i]])
+            elif eng == "g":
+                keep(T.XR[:, i:XO:16], T.X192[:, 0:NX], [[0, NX]], A.is_equal, 0, 0, ["X192"], [XRK[i]])
             else:
-                act(T.XR[:, i:XO:16], src, F.Identity, ["FR%d" % t], [XRK[i]], bias=192.0)
+                act(T.XR[:, i:XO:16], src, F.Identity, ["FR%d" % t], [XRK[i]], bias=-192.0, scale=-1.0)
 
     def xrep_late(t):
-        act(T.XR[:, XO:XO + 1024], T.FR[:, 256 * t:256 * t + 256].indirect(T.XL[:]), F.Identity, ["FR%d" % t, "XL"], XYK, bias=192.0)
+        act(T.XR[:, XO:XO + 1024], T.FR[:, 256 * t:256 * t + 256].indirect(T.XL[:]), F.Identity, ["FR%d" % t, "XL"], XYK,
+            bias=-192.0, scale=-1.0)
 
     def x192(t):
-        o, n = 256 * t, 256 if t == R - 1 else 128
-        act(T.X192[:, o:o + n], T.FR[:, o:o + n], F.Identity, ["FR%d" % t], ["X192_%d" % t], bias=192.0)
-        if n == 128:
-            act(T.X192[:, o + n:o + 256], T.FR[:, o + n:o + 256], F.Identity, ["FR%d" % t], ["X192n%d" % t], bias=-192.0, scale=-1.0)
+        act(T.X192[:], T.FR[:, 256 * t:256 * t + 256], F.Identity, ["FR%d" % t], ["X192"], bias=-192.0, scale=-1.0)
 
-    def lists(src, key):
+    def states(src, key):
         for h in range(2):
-            ts(T.LS2[:, h::2], src[:, 0:16], float(h), None, A.add, None, [key], ["LS2%d" % h])
-        for h in range(2):
-            ts(T.LS1[:, h * QX:h * QX + QX], src[:, 0:QX], float(h), None, A.add, None, [key], ["LS1a%d" % h])
-            o = 2 * QX + h * (16 - QX)
-            ts(T.LS1[:, o:o + 16 - QX], src[:, QX:16], float(h), None, A.add, None, [key], ["LS1b%d" % h])
+            ts(T.LS2[:, 16 * h:16 * h + 16], src[:, 0:16], float(h), None, A.add, None, [key], ["LS2%d" % h])
 
     def candidates():
-        l2 = ["LS20", "LS21"]
-        act(T.HI[:], T.MIXF[:, 0:1028].indirect(T.LS2[:]), F.Identity, ["MIXF"] + l2, ["HI"],
-            scale=1.0 / 64, bias=127.5 + 1.0 / 128)
-        ts(T.LOI[:], T.MIX[:, 0:1028].indirect(T.LS2[:]), 63, None, A.bitwise_and, None, ["MIX", "MIXW"] + l2, ["LOI"])
-        cp(T.LO[:], T.LOI[:], ["LOI"], ["LO"])
-        op("v", lambda: V.transpose(T.THI[:], T.HI[:]), ["HI"], ["THI"])
-        op("v", lambda: V.transpose(T.TLO[:], T.LO[:]), ["LO"], ["TLO"])
+        ts(T.WG[:], T.MIX[:, 0:1028].indirect(T.LS2[:]), -2048.0, None, A.add, None, ["MIX", "MIXW", "LS20", "LS21"], ["WG"])
+        for h in range(2):
+            ts(T.CAND[:, NX * h:NX * h + NX], T.WG[:, 256 * h:256 * h + NX], 2048.0, None, A.add, None, ["WG"], ["CAND%d" % h])
+        for k in range(4):
+            o = 256 * (k % 2) + NX + 16 * (k // 2)
+            ts(T.CAND[:, 2 * NX + k:512:4], T.WG[:, o:o + 16], 2048.0, None, A.add, None, ["WG"], [CYK[k]])
 
-    def candidate_list():
-        cp(T.CAND[:, 0:512], T.MIX[:, 0:1028].indirect(T.LS1[:]), ["MIX", "MIXW", "LS1a0", "LS1a1", "LS1b0", "LS1b1"], ["CAND"])
+    def turn_list():
+        op("v", lambda: V.transpose(T.TT[:], T.WG[:]), ["WG"], ["TT"])
 
-    def late_list():
-        for c in range(8):
-            o = 2 * NX + 16 * c
-            b = 512 + 64 * (c // 4)
-            cp(T.CAND[:, b + c % 4:b + 64:4], T.CAND[:, o:o + 16], ["CAND"], [CYK[c]])
-
-    def key_start(late):
-        if late:
-            mm("KY", T.KY[:, 0:256], T.ONES[0:64, :], T.TBY[0:64, :], True, False, ["ONES", "TBY0", "TBY1"])
-        for k, (src, name) in enumerate(((T.THI, "THI"), (T.TLO, "TLO"))):
-            kx = "KX%d" % (k + 1)
-            if not late:
-                mm(kx, T[kx][:, 0:2 * NX], T.ONES[0:64, :], T.TBX[0:64, :], True, False, ["ONES", "TBX"])
+    def steps():
+        for q2 in range(2):
             for h in range(2):
+                o, b, n = 32 * q2, 8 * h, QX // 2
                 for g2 in range(2):
-                    r = [name, "PM%d%d" % (g2, h)]
-                    o = 128 * k + 64 * h
-                    if late:
-                        mm("KY", T.KY[:, o:o + 64], PM[g2][h][:], src[:, QX:16, g2, :], False, False, r)
-                    else:
-                        mm(kx, T[kx][:, h * NX:h * NX + NX], PM[g2][h][:], src[:, 0:QX, g2, :], False, False, r)
+                    r = ["TT", "PM%d%d" % (g2, q2), "NM%d%d" % (g2, q2)]
+                    mm("Z2", T.Z2[:, 0:n, o + h:o + 32:2], PM[g2][q2][:], T.TT[:, b:b + n, g2, :], g2 == 0, False, r)
+                    mm("Z2", T.Z2[:, 0:n, o + h:o + 32 - h:2], NM[g2][q2][:], T.TT[:, 8 - b:8 - b + n, g2, h:16], False, g2 == 1, r)
+                o += 16 * h
+                for g2 in range(2):
+                    r = ["TT", "PM%d%d" % (g2, q2), "NM%d%d" % (g2, q2)]
+                    mm("Z2", T.Z2[:, n, o:o + 16], PM[g2][q2][:], T.TT[:, b + n, g2, :], g2 == 0, False, r)
+                    if h == 0:
+                        mm("Z2", T.Z2[:, n, o + 15:o + 16], NM[g2][q2][:], T.TT[:, 8 + n, g2, 0:1], False, False, r)
+                    mm("Z2", T.Z2[:, n, o:o + 15], NM[g2][q2][:], T.TT[:, b + n, g2, 1:16], False, g2 == 1, r)
 
-    bias_banks(["Z2"])
+    def steps_copy():
+        act(T.TW[:], T.Z2[:], F.Copy, [], ["TW"], ["Z2"])
+
+    def key_start(k, n):
+        o = 256 if k == "K3" else 0
+        mm(k, T[k][:, 0:32 * n], T.ONES[0:64, 0:128], T.TB[0:64, o:o + 32 * n], True, False, ["ONES", "TB0", "TB1"])
+
     op("v", lambda: V.transpose(T.TA[:], T.A0[:]), ["A0"], ["TA"])
     for c in range(8):
         for g2 in range(2):
             o = 32 * (c // 2) + 16 * g2
-            mm("Z1", T.Z1[:, c:128:8], PM[g2][c % 2][:], T.TA[:, o:o + 16], g2 == 0, g2 == 1, ["TA", "PM%d%d" % (g2, c % 2)])
+            mm("Z1", T.Z1[:, 16 * c:16 * c + 16], PM[g2][c % 2][:], T.TA[:, o:o + 16], g2 == 0, g2 == 1, ["TA", "PM%d%d" % (g2, c % 2)])
+    bias_bank("K3")
+    bias_bank("Z2")
     cp(T.SF[:], T.S0[:], ["S0"], ["SF"])
-    lists(T.S0, "S0")
+    states(T.S0, "S0")
+    x192(0)
+    xrep(0, range(0, 4), "v")
+    xrep(0, range(4, 10), "g")
+    xrep(0, range(10, 12), "s")
     ts(T.ATS[:], T.Z1[:, 0:128], 1.0 / 64, None, A.mult, None, [], ["ATS"], ["Z1"])
     expand()
-    for q in range(16 - QX):
-        act(T.XT[:, q::16 - QX], T.FR[:, NX + 16 * q:NX + 16 * q + 16], F.Identity, ["FR0"], ["XT%d" % q], bias=192.0)
-    x192(0)
-    xrep(0, range(0, 8), "s")
-    late_constants()
-    xrep(0, range(8, 16), "v")
+    xrep(0, range(12, 16), "v")
     cp(T.MIX[:, 1024:1028], T.MIX[:, 0:4], ["MIX"], ["MIXW"])
-    cp(T.MIXF[:, 0:1028], T.MIX[:, 0:1028], ["MIX", "MIXW"], ["MIXF"])
+    for k in range(4):
+        o = NX + 16 * (k // 2)
+        act(T.XT[:, k::4], T.X192[:, o:o + 16], F.Copy, ["X192"], ["XT%d" % k])
+    late_constants()
     candidates()
-    candidate_list()
-    late_list()
-
-
-    own_s = [(0, "Z0"), (2, "Z1"), (4, "Z3")]
-    chunks = [(0, 2), (2, 4), (4, 6), (6, 8)] + [(c, c + 4) for c in range(8, 2 * QX, 4)]
-    zfirst = {0: "Z0", 1: "Z1", 2: "Z3", 3: "Z0", 4: "Z1", 5: "Z3", 6: "Z0", 7: "Z2"}
-    zlater = {0: "Z2", 3: "Z3", 6: "Z2", 1: "Z0", 2: "Z1", 4: "Z0", 5: "Z1", 7: "Z0"}
-
-    def qof(c):
-        return c % QX if c < 2 * QX else QX + (c - 2 * QX) % (16 - QX)
 
     for t in range(R):
         last = t == R - 1
+        NC = T["NC%d" % t]
+        zbank = {0: "Z2", 3: "K3", 6: "Z2", 1: "Z0", 2: "Z1", 4: "Z0", 5: "Z1", 7: "Z0"}
         vplan = {0: [("d", 0)], 3: [("d", 3), ("c", 1), ("c", 2)], 6: [("d", 6), ("c", 4)], 7: [("c", 5), ("c", 7)]}
-        SCL, zbank, order = [1, 2, 4, 5, 7], zlater, (1, 0, 2, 3, 4, 5, 6, 7)
+        SCL, order = [1, 2, 4, 5, 7], (1, 0, 2, 3, 4, 5, 6, 7)
         if t == 0:
-            SCL, zbank, order = list(range(7)), zfirst, (0, 1, 2, 3, 4, 5, 7, 6)
-            vplan = {5: [("c", c) for c in range(5)], 6: [("d", 7), ("c", 5), ("c", 6)]}
+            zbank = {0: "Z0", 1: "Z1", 2: "Z0", 3: "K3", 4: "Z1", 5: "Z0", 6: "Z1", 7: "Z2"}
+            vplan = {4: [("d", 3), ("c", 0), ("c", 1), ("c", 2)], 6: [("d", 7), ("c", 4), ("c", 5), ("c", 6)]}
+            SCL, order = [0, 1, 2, 4, 5, 6], (0, 1, 2, 3, 4, 5, 7, 6)
         for c in order:
             z = zbank[c]
             if c == 5 and t:
-                bias_banks([zbank[6]])
-            mm(z, T[z][:], T.BD[:, c::8], T.MU[:, 512 * c:512 * c + 512], c in SCL, True, BDK + ["MU%d" % (c // 2)])
+                bias_bank(zbank[6])
+            mm(z, T[z][:], T.BD[:, c, :], T.MU[:, 512 * c:512 * c + 512], c in SCL, True, BDK + ["MU%d" % (c // 2)])
             if c in SCL:
                 act(T.MT[:, 512 * c:512 * c + 512], T[z][:], F.Identity, [], [MTK[c]], [z], bias=192.0 + 1.0 / 128)
             for kind, d in vplan.get(c, []):
@@ -421,105 +474,186 @@ def rank_program(g, core, T, topo):
                     ts(dst, T[zd][:], 184.0, 199.0, A.max, A.min, [], [MTK[d]], [zd])
                 else:
                     ts(dst, dst, 184.0, 199.0, A.max, A.min, [MTK[d]], [MTK[d]])
+
         if t == 0:
-            key_start(False)
-            key_start(True)
-        for c0, z in own_s:
-            mc = T.D[:, 256 * c0:256 * c0 + 512]
-            act(mc, T.MT[:, 0:4096].indirect(T.CAND[:, 16 * c0:16 * c0 + 32]), F.Identity, MTK + ["CAND"], ["D%d" % c0])
-            mm(z, T[z][:], T.NID[:], T.XR[:, 256 * c0:256 * c0 + 512], True, False, ["NID"] + XRK)
-            mm(z, T[z][:], T.ID[:], mc, False, True, ["ID", "D%d" % c0])
-        for c0, c1 in chunks:
-            q0 = qof(c0)
-            if c0 in dict(own_s):
-                z = dict(own_s)[c0]
-                act(T.SQ[:, c0:c1], T[z][:], F.Square, [], ["SQ%d" % c0], [z])
-            else:
-                tt(T.D[:, 256 * c0:256 * c1], T.MT[:, 0:4096].indirect(T.CAND[:, 16 * c0:16 * c1]),
-                   T.XR[:, 256 * q0:256 * (q0 + c1 - c0)], A.subtract, MTK + XRK + ["CAND"], ["D%d" % c0])
-                act(T.SQ[:, c0:c1], T.D[:, 256 * c0:256 * c1], F.Square, ["D%d" % c0], ["SQ%d" % c0])
-            if c1 % 4:
-                continue
-            b0 = c1 - 4
-            r = ["SW", "SQ%d" % b0, "SQ%d" % c0]
-            for k in range(2):
-                name = "KX%d" % (k + 1)
-                for j in range(16):
-                    mm(name, T[name][:, 16 * b0:16 * c1], T.SW[:, 15 - j:143 - j], T.SQ[:, b0:c1, j, :], False,
-                       c1 == 2 * QX and j == 15, r)
-        for h, j0, j1 in ((0, 0, 8), (0, 8, 16), (1, 0, 8), (1, 8, 12), (1, 12, 16)):
-            a, b, key = 1024 * h + 64 * j0, 1024 * h + 64 * j1, "%d_%d" % (h, j0)
-            tt(T.D[:, YO + a:YO + b], T.MT[:, 0:4096].indirect(T.CAND[:, 512 + a // 16:512 + b // 16]),
-               T.XR[:, XO + 64 * j0:XO + 64 * j1], A.subtract, MTK + CYK + XYK, ["DY" + key])
-            act(T.SQY[:, a:b], T.D[:, YO + a:YO + b], F.Square, ["DY" + key], ["SY" + key])
+            key_start("K1", 8)
+            key_start("K2", 6)
+
+        def own(h, q, z, n=2):
+            b, keys = QX * h + q, ["D%d_%d" % (h, k) for k in range(q, q + n)]
+            mc = T.D[:, 256 * b:256 * (b + n)]
+            act(mc, T.MT[:, 0:4096].indirect(T.CAND[:, 16 * b:16 * (b + n)]), F.Identity, MTK + ["CAND%d" % h], keys)
+
+        def own_sub(h, q, z, n=2):
+            b, keys = QX * h + q, ["D%d_%d" % (h, k) for k in range(q, q + n)]
+            mc = T.D[:, 256 * b:256 * (b + n)]
+            mm(z, T[z][:, 0:256 * n], T.ID[:], T.XR[:, 256 * q:256 * (q + n)], True, False, ["ID"] + XRK)
+            mm(z, T[z][:, 0:256 * n], T.ID[:], mc, False, True, ["ID"] + keys)
+
+        def own_square(h, q, z, n=2):
+            b = QX * h + q
+            act(T.SQ[:, b:b + n], T[z][:, 0:256 * n], F.Square, [], ["SQ%d" % k for k in range(b, b + n)], [z])
+
+        def gather(h, q0, q1):
+            b0, b1 = QX * h + q0, QX * h + q1
+            tt(T.D[:, 256 * b0:256 * b1], T.MT[:, 0:4096].indirect(T.CAND[:, 16 * b0:16 * b1]),
+               T.XR[:, 256 * q0:256 * q1], A.add, MTK + XRK + ["CAND%d" % h], ["D%d_%d" % (h, q) for q in range(q0, q1)])
+
+        def square(h, q0, q1):
+            b0, b1 = QX * h + q0, QX * h + q1
+            act(T.SQ[:, b0:b1], T.D[:, 256 * b0:256 * b1], F.Square, ["D%d_%d" % (h, q) for q in range(q0, q1)],
+                ["SQ%d" % b for b in range(b0, b1)])
+
+        def add(h, q0, q1, stop=False):
+            b0, b1 = QX * h + q0, QX * h + q1
+            k, o = ("K1", 0) if q0 < 8 else ("K2", 8)
+            for j in range(16):
+                mm(k, T[k][:, 32 * (q0 - o) + h:32 * (q1 - o):2], T.SW[:, 15 - j:143 - j], T.SQ[:, b0:b1, j, :], False,
+                   2 * (stop and j == 15), ["SW"] + ["SQ%d" % b for b in range(b0, b1)])
+
+        def late_gather(j0, j1):
+            a, b = 64 * j0, 64 * j1
+            tt(T.D[:, YO + a:YO + b], T.MT[:, 0:4096].indirect(T.CAND[:, 2 * NX + 4 * j0:2 * NX + 4 * j1]),
+               T.XR[:, XO + a:XO + b], A.add, MTK + CYK + XYK, ["DY%d" % j for j in range(j0, j1)])
+
+        def late_square(j0, j1):
+            a, b = 64 * j0, 64 * j1
+            act(T.SQY[:, a:b], T.D[:, YO + a:YO + b], F.Square, ["DY%d" % j for j in range(j0, j1)], ["SY%d" % j for j in range(j0, j1)])
+
+        def late_add(j0, j1):
             for j in range(j0, j1):
-                for k in range(2):
-                    o, i = 128 * k + 64 * h, 1024 * h + 64 * j
-                    mm("KY", T.KY[:, o:o + 64], T.SW[:, 15 - j:143 - j], T.SQY[:, i:i + 64], False,
-                       h == 1 and j == 15 and k == 1, ["SW", "SY" + key])
-        for k, rx in enumerate((T.RX1, T.RX2)):
-            kx = "KX%d" % (k + 1)
-            scan(rx[:], T.SP[:], T[kx][:, 0:2 * NX], A.add, A.max, ["SP"], ["RX%d" % k], [kx])
-        tt(T.KI[:, 0:QX], T.RX1[:, 15:NX:16], T.RX1[:, NX + 15:2 * NX:16], A.max, ["RX0"], ["KIa0"])
-        scan(T.RY[:], T.SP[:, 0:256], T.KY[:, 0:256], A.add, A.max, ["SP"], ["RY"], ["KY"])
-        tt(T.KI[:, 16:16 + QX], T.RX2[:, 15:NX:16], T.RX2[:, NX + 15:2 * NX:16], A.max, ["RX1"], ["KIa1"])
-        for k in range(2):
-            o = 128 * k
-            tt(T.KI[:, 16 * k + QX:16 * k + 16], T.RY[:, o + 15:o + 64:16], T.RY[:, o + 79:o + 128:16], A.max, ["RY"], ["KIb%d" % k])
-        ts(T.HL[:], T.KI[:], 63, None, A.bitwise_and, None, ["KIa0", "KIa1", "KIb0", "KIb1"], ["HL"])
-        ts(T.H64[:], T.HL[:, 0:16], 64.0, None, A.mult, None, ["HL"], ["H64"])
-        ts(T.CL[:], T.HL[:, 0:16], 3, None, A.arith_shift_right, None, ["HL"], ["CL"])
-        wf = T.OUT[:, 16 * t:16 * t + 16]
-        tt(wf, T.H64[:], T.HL[:, 16:32], A.add, ["H64", "HL"], ["OUT%d" % t])
-        tt(T.SCF[:], T.CL[:], T.U8[:], A.add, ["CL", "U8"], ["SCF"])
-        cp(T.W16[:], wf, ["OUT%d" % t], ["W16"])
-        cp(T.CL16[:], T.CL[:], ["CL"], ["CL16"])
-        cp(T.SC16[:], T.SCF[:], ["SCF"], ["SC16"])
-        xs = T.X192[:, 256 * t:256 * t + 256]
-        win = [T["EW%d" % h][:, 0:1024].indirect(T.SC16[:, 8 * h:8 * h + 8]) for h in range(2)]
-        if last:
-            tt(T.NE[:], T.MT[:, 0:4096].indirect(T.W16[:]), xs, A.subtract, MTK + ["W16", "X192_%d" % t], ["NE", "NE1"])
-            act(T.MW[:], T.MU[:, 0:4096].indirect(T.W16[:]), F.Identity, MUK + ["W16"], ["MW"])
-            for h in range(2):
-                cp(win[h], T.MW[:, 128 * h:128 * h + 128], ["MW", "SC16"], ["EW%d" % h])
-            plain = (T.NE, "NE")
-        else:
-            tt(T.NE[:, 0:128], T.MT[:, 0:4096].indirect(T.W16[:, 0:8]), T.X192[:, 256 * t:256 * t + 128], A.subtract,
-               MTK + ["W16", "X192_%d" % t], ["NE"])
-            act(T.NE[:, 128:256], T.MT[:, 0:4096].indirect(T.W16[:, 8:16]), F.Identity, MTK + ["W16"], ["NE1"])
-            act(T.MW[:], T.MU[:, 0:4096].indirect(T.W16[:]), F.Identity, MUK + ["W16"], ["MW"])
-            cp(win[0], T.NE[:, 0:128], ["NE", "SC16"], ["EW0"])
-            tt(win[1], T.NE[:, 128:256], T.X192[:, 256 * t + 128:256 * t + 256], A.add, ["NE1", "SC16", "X192n%d" % t], ["EW1"])
-            plain = (T.MW, "MW")
-        act(T.FN[:], T.OH[:, 0:16].indirect(T.CL16[:]), F.Identity, ["OH", "CL16"], ["FN", "NCOL"], accum_out=T.NCOL[:, 0:1])
-        for s in range(2):
-            ts(T.RN[:, 32 + s::PW], T.BN[:, s::2], T.NCOL[:, 0:1], None, A.mult, None, ["BN", "NCOL"], ["RN%d" % s])
-        for h in range(2):
-            mm("KY", T.KY[:, 128 * h:128 * h + 128], plain[0][:, 128 * h:128 * h + 128], T.ID[:], True, True, [plain[1], "ID"])
-        act(T.PT[:], T.KY[:, 0:256], F.Copy, [], ["PT"], ["KY"])
-        for hb in range(2):
-            z = "Z%d" % (1 + hb)
+                mm("K3", T.K3[:, 0:64], T.SW[:, 15 - j:143 - j], T.SQY[:, 64 * j:64 * j + 64], False, 2 * (j == 15), ["SW", "SY%d" % j])
+
+        def pick(step, k, q0, q1):
+            a, b, keys = 32 * q0, 32 * q1, T[k][:, 0:32 * (q1 - q0)]
+            if step == 0:
+                scan(T.R1[:, a:b], T.SP[:, 0:b - a], keys, A.add, A.max, ["SP"], ["R1" + k], [k])
+            elif step == 1:
+                tt(T.NM[:, a:b], keys, T.R1[:, a:b], A.not_equal, ["R1" + k], ["NM" + k], [k])
+            else:
+                scan(T.R2[:, a:b], T.NM[:, a:b], T.TW[:, a:b], A.mult, A.add, ["NM" + k, "TW"], ["R2" + k])
+
+        def sums_lists(k, q0, q1):
+            r = ["R2" + n for n in k.split()]
+            wf, s8 = T.R2[:, 32 * q0 + 31:32 * q1:32], slice(q0, q1)
+            ts(T.W16[:, s8], wf, 2048.0, None, A.add, None, r, ["W16" + n for n in k.split()])
+            tt(T.SCF[:, s8], wf, T.U4[:, s8], A.add, r + ["U4"], ["SCF" + k])
+            ts(T.CL16[:, s8], wf, 1.0 / 512, CLASS_OF, A.mult, A.add, r, ["CL16" + n for n in k.split()])
+
+        def sums_gather(k, q0, q1):
+            s8, u = slice(q0, q1), slice(16 * q0, 16 * q1)
+            w = ["W16" + n for n in k.split()]
+            if last:
+                cp(T.NE[:, u], T.MU[:, 0:4096].indirect(T.W16[:, s8]), MUK + w, ["NE" + k])
+            else:
+                tt(T.NE[:, u], T.MT[:, 0:4096].indirect(T.W16[:, s8]), T.X192[:, u], A.add, MTK + w + ["X192"], ["NE" + k])
+            ts(T.SC16[:, s8], T.SCF[:, s8], 1.0 / 512, CLASS_OF, A.mult, A.add, ["SCF" + k], ["SC16" + k])
+
+        def sums_scatter(k, q0, q1):
+            s8, u, h = slice(q0, q1), slice(16 * q0, 16 * q1), q0 // 8
+            cp(T["EW%d" % h][:, 0:1024].indirect(T.SC16[:, s8]), T.NE[:, u], ["NE" + k, "SC16" + k],
+               ["EW%d" % h] + ["EW" + n for n in k.split()])
+
+        def sums_gather_s(k, q0, q1):
+            src, keys = (T.MU, MUK) if last else (T.MT, MTK)
+            act(T.NE[:, 16 * q0:16 * q1], src[:, 0:4096].indirect(T.W16[:, q0:q1]), F.Identity, keys + ["W16" + k], ["NE" + k])
+
+        def sums_places(k, q0, q1):
+            ts(T.SC16[:, q0:q1], T.SCF[:, q0:q1], 1.0 / 512, CLASS_OF, A.mult, A.add, ["SCF" + k], ["SC16" + k])
+
+        def sums_scatter_s(k, q0, q1):
+            if last:
+                return sums_scatter(k, q0, q1)
+            s8, u, h = slice(q0, q1), slice(16 * q0, 16 * q1), q0 // 8
+            tt(T["EW%d" % h][:, 0:1024].indirect(T.SC16[:, s8]), T.NE[:, u], T.X192[:, u], A.add, ["NE" + k, "SC16" + k, "X192"],
+               ["EW%d" % h, "EW" + k])
+
+        def sums_side(h):
+            s8, u = slice(8 * h, 8 * h + 8), slice(128 * h, 128 * h + 128)
+            src, keys = (T.MT, MTK) if last else (T.MU, MUK)
+            act(T.MW[:, u], src[:, 0:4096].indirect(T.W16[:, s8]), F.Identity, keys + ["W16" + k for k in HK[h]], ["MW%d" % h])
+
+        def sums_count(h):
+            s8, u = slice(8 * h, 8 * h + 8), slice(128 * h, 128 * h + 128)
+            act(T.FN[:, u], T.OH[:, 0:16].indirect(T.CL16[:, s8]), F.Identity, ["OH"] + ["CL16" + k for k in HK[h]],
+                ["FN%d" % h, "NC%d%d" % (t, h)], accum_out=NC[:, 4 * rank + h:4 * rank + h + 1])
+
+        def sums_plain(h):
+            u, pz = slice(128 * h, 128 * h + 128), "Z1"
+            if last:
+                mm(pz, T[pz][:, 0:128], T.X192[:, u], T.ID[:], True, False, ["X192", "ID"])
+            mm(pz, T[pz][:, 0:128], T.MW[:, u], T.ID[:], not last, True, ["MW%d" % h, "ID"])
+
+        def sums_plain_copy(h):
+            act(T.PT[:, 128 * h:128 * h + 128], T.Z1[:, 0:128], F.Copy, [], ["PT%d" % h], ["Z1"])
+
+        def sums_turn(h, k):
+            z, p = "ZT%d" % k, slice(64 * k, 64 * k + 64)
             for c in range(8):
-                mm(z, T[z][:, c::8], T.EW0[:, c::8], T.ID[:, 64 * hb:64 * hb + 64], True, True, ["EW0", "ID"])
-            act(T.ET0[:, 512 * hb:512 * hb + 512], T[z][:], F.Copy, [], ["ET0%d" % hb], [z])
-        for c in range(8):
-            op("p", lambda c=c: P.transpose(T.ZT[:, 128 * c:128 * c + 128], T.EW1[:, c::8], T.ID[:]), ["EW1", "ID"], (), ["ZT"])
-        for c in range(8):
-            cp(T.ET1[:, c::8], T.ZT[:, 128 * c:128 * c + 128], [], ["ET1c%d" % c], ["ZT"])
-        mm("Z0", T.Z0[:, 0:4 * PW], T.KN[:], T.RN[:], True, False, ["KN", "RN0", "RN1"])
-        for h in range(2):
-            for hb in range(2):
-                for gp in range(4 * hb, 4 * hb + 4):
-                    o = PW * (gp // 2) + 16 * (gp % 2)
-                    mm("Z0", T.Z0[:, o:o + 16], T["ET%d" % h][:, 128 * gp:128 * gp + 128],
-                       T.PT[:, 128 * h + 16 * gp:128 * h + 16 * gp + 16], False, h == 1 and gp == 7,
-                       ["PT"] + (["ET1c%d" % c for c in range(8)] if h else ["ET0%d" % hb]))
+                op("p", lambda c=c: P.transpose(T[z][:, 0:4, 16 * c:16 * c + 16], T["EW%d" % h][p, c::8], T.ID[p, p]),
+                   ["EW%d" % h, "ID"] + ["EW" + n for n in HK[h]], ["ZT%d%d" % (h, k)] if c == 7 else [], [z])
+                ops[-1]["stop"] = 1
+
+        def sums_copy(h, k, eng):
+            out, z = T["ET%d" % h][:, 4 * k:4 * k + 4, :], "ZT%d" % k
+            if eng == "v":
+                cp(out, T[z][:, 0:4, :], ["ZT%d%d" % (h, k)], ["ET%d%d" % (h, k)], [z])
+            else:
+                act(out, T[z][:, 0:4, :], F.Copy, ["ZT%d%d" % (h, k)], ["ET%d%d" % (h, k)], [z])
+
+        def sums_add(h, k):
+            if k == h == 0:
+                mm("Z0", T.Z0[:, 0:128], T.ONES[0:32, 0:128], T.ZR[0:32, :], True, False, ["ONES", "ZR"])
+            for gp in range(4 * k, 4 * k + 4):
+                o = PW * (gp // 2) + 16 * (gp % 2)
+                mm("Z0", T.Z0[:, o:o + 16], T["ET%d" % h][:, gp, :],
+                   T.PT[:, 128 * h + 16 * gp:128 * h + 16 * gp + 16], False, h == 1 and gp == 7,
+                   ["PT%d" % h, "ET%d%d" % (h, gp // 4)])
+
+        K1, K2, K3, K23 = ("K1", 0, 8), ("K2", 8, QX), ("K3", QX, 16), ("K2 K3", 8, 16)
+        a, b, c, d = (0, 0, "Z1"), (0, 2, "K3"), (0, 8, "Z1"), (0, 10, "Z0", 1)
+        first = t == 0
+        on_v = [(gather, 0, 4, 8)] + [(turn_list,)] * first + [
+            (gather, 1, 0, 4), (gather, 1, 4, 8), (gather, 0, 11, 14), (gather, 1, 8, 10),
+            (pick, 0, *K1), (gather, 1, 10, 12), (pick, 1, *K1), (gather, 1, 12, 14), (pick, 2, *K1),
+            (late_gather, 0, 8), (sums_lists, *K1), (late_gather, 8, 12), (sums_gather, *K1), (late_gather, 12, 16), (pick, 0, *K2),
+            (sums_scatter, *K1), (pick, 1, *K2), (pick, 0, *K3), (pick, 2, *K2), (pick, 1, *K3), (pick, 2, *K3),
+            (sums_lists, *K23), (sums_gather, *K23), (sums_scatter, *K23), (sums_copy, 1, 0, "v"), (sums_copy, 1, 1, "v")]
+        on_s = [(own, *a), (own, *b), (own_square, *a), (own_square, *b), (square, 0, 4, 8), (square, 1, 0, 4), (square, 1, 4, 8)]
+        on_s += [(steps_copy,)] * first + [
+            (own, *c), (own, *d), (square, 0, 11, 14), (own_square, *c), (own_square, *d), (square, 1, 8, 12), (square, 1, 12, 14),
+            (late_square, 0, 8), (late_square, 8, 12), (late_square, 12, 16), (sums_side, 0), (sums_count, 0),
+            (sums_plain_copy, 0), (sums_copy, 0, 0, "s"), (sums_copy, 0, 1, "s"), (sums_count, 1),
+            (sums_side, 1), (sums_plain_copy, 1)]
+        on_p = [(own_sub, *a), (own_sub, *b), (add, 0, 0, 4), (key_start, "K3", 2)] + [(steps,)] * first + [
+            (add, 0, 4, 8), (add, 1, 0, 4), (add, 1, 4, 8, True), (own_sub, *c), (own_sub, *d), (add, 0, 11, 14), (add, 0, 8, 11),
+            (add, 1, 8, 12), (add, 1, 12, 14, True), (late_add, 0, 8), (late_add, 8, 12), (late_add, 12, 16), (sums_plain, 0),
+            (sums_turn, 0, 0), (sums_turn, 0, 1), (sums_add, 0, 0), (sums_add, 0, 1), (sums_plain, 1),
+            (sums_turn, 1, 0), (sums_turn, 1, 1), (sums_add, 1, 0), (sums_add, 1, 1)]
+        _weave(ops, [on_v, on_s, on_p])
         Pt, LD, LH, DL = T["P%d" % t], T["LD%d" % t], T["LH%d" % t], T["DL%d" % t]
         ts(Pt[:], T.Z0[:, 0:4 * PW], -1.0, 32768.0, A.mult, A.add, [], ["P%d" % t], ["Z0"])
 
+        peers = [c for c in mine if c != core]
+        eng = topo.engines(core, peers[0])
+        counts, r = NC[:, 4 * rank:4 * rank + 4], ["NC%d0" % t, "NC%d1" % t, "NCz"]
         tr = []
         for i, hc in enumerate(helpers):
-            eng = [e for e in topo.engines(core, hc) if e not in topo.engines(core, mine[(me + 1) % 4])]
+            hop = _hop_engines(topo, core, hc, peers[0], t)
+            half = len(hop) // 2
+            tr.append(RemoteDMATransfer(dst_ids=[_dst(topo, hc, core)], dma_engine_mask=_mask(hop[i * half:(i + 1) * half]),
+                                        remote_sem=T.sem["cin%d" % t], src=counts, dst=T["HC%d" % t][:]))
+            sent[0] += half
+        op("g", lambda tr=tr: g.remote_dma_fused(tr, local_sem=T.sem.sent), r)
+        tr = [RemoteDMATransfer(dst_ids=[_dst(topo, c, core) for c in peers], dma_engine_mask=_mask(eng),
+                                remote_sem=T.sem["cn%d" % t], srcs=[counts], dsts=[counts for c in peers])]
+        sent[0] += len(eng)
+        op("g", lambda tr=tr: g.remote_dma_fused(tr, local_sem=T.sem.sent), r)
+        ext("cn%d" % t, 3 * len(eng) + 4 * (len(eng) // 2), ["NCr%d" % t])
+
+        tr = []
+        for i, hc in enumerate(helpers):
+            eng = _hop_engines(topo, core, hc, mine[(me + 1) % 4], t)
             half = len(eng) // 2
             tr.append(RemoteDMATransfer(dst_ids=[_dst(topo, hc, core)], dma_engine_mask=_mask(eng[i * half:(i + 1) * half]),
                                         remote_sem=T.sem["hin%d" % t], src=Pt[:, 2 * i * PW:(2 * i + 2) * PW], dst=T["HB%d" % t][:]))
@@ -538,24 +672,49 @@ def rank_program(g, core, T, topo):
         ext("rd%d" % t, ne, ["LD%d" % t])
         ext("rh%d" % t, 4 * (ne // 2), ["LH%d" % t])
 
-        mm("Z0", T.Z0[:, 0:128], T.ONES[0:64, :], T.OC[0:64, :], True, False, ["ONES", "OCa", "OCb"])
-        tt(T.HS[:, 0:QX], T.RX1[:, NX + 15:2 * NX:16], T.RX1[:, 15:NX:16], A.is_gt, ["RX0"], ["HSa"])
-        tt(T.HS[:, QX:16], T.RY[:, 79:128:16], T.RY[:, 15:64:16], A.is_gt, ["RY"], ["HSb"])
-        tt(T.SF[:], T.SF[:], T.HS[:], A.add, ["SF", "HSa", "HSb"], ["SF"])
+        RK = ["K1", "K2", "K3"]
+        if t == 0:
+            tree_constants()
+
+        def choose(step):
+            if step == 0:
+                op("v", lambda nc=NC: V.tensor_reduce(T.NT[:, 0:1], nc[:], X.X, A.add), ["NC%d0" % t, "NC%d1" % t, "NCz", "NCr%d" % t], ["NT"])
+                mm("K3", T.K3[0:48, 0:1], T.BL[:], T.NT[:, 0:1], True, True, ["BL0", "BL1", "BL2", "NT"])
+            elif step == 1:
+                ts(T.UB[0:48, :], T.C260[0:48, :], T.K3[0:48, 0:1], None, A.is_gt, None, ["C260"], ["UB"], ["K3"])
+                mm("K3", T.K3[:, 0:256], T.UB[0:48, :], T.EX[0:48, :], True, True, ["UB", "EX"])
+            else:
+                for s in range(2):
+                    tt(T.SEL[:, 128 * s:128 * s + 128], T.K3[:, 128 * s:128 * s + 128], T.LEV[:], A.is_ge, ["LEV"], ["SEL%d" % s], ["K3"])
+
+        mm("Z0", T.Z0[:, 0:32], T.ONES[0:64, 0:128], T.OC[0:64, :], True, False, ["ONES", "OCa", "OCb"])
+        ts(T.SI[:], T.R1[:, 31::32], -1.0 / 64, None, A.mult, None, ["R1" + k for k in RK], ["SI"])
+        ts(T.HS[:], T.SI[:], 4, 1, A.arith_shift_right, A.bitwise_and, ["SI"], ["HS"])
+        ts(T.OUT[:, 16 * t:16 * t + 16], T.R2[:, 31::32], 2048.0, None, A.add, None, ["R2" + k for k in RK], ["OUT%d" % t])
+        tt(T.SF[:], T.SF[:], T.HS[:], A.add, ["SF", "HS"], ["SF"])
         if not last:
-            mm("Z1", T.Z1[:, 0:128], T.ONES[0:64, :], T.M3[0:64, :], True, False, ["ONES", "M3"])
+            mm("Z1", T.Z1[:, 0:128], T.ONES[0:64, 0:128], T.M3[0:64, :], True, False, ["ONES", "M3"])
             mm("Z1", T.Z1[:, 0:128], T.ID[:], T.ATS[:], False, False, ["ID", "ATS"])
-            bias_banks()
-            lists(T.SF, "SF")
+            key_start("K1", 8)
+            key_start("K2", 6)
+            states(T.SF, "SF")
+            xrep(t + 1, range(0, 2), "v")
             candidates()
-            key_start(False)
+            turn_list()
+            if t == 0:
+                heights()
+            choose(0)
+            xrep(t + 1, range(2, 5), "v")
+            choose(1)
+            xrep(t + 1, range(5, 8), "v")
+            choose(2)
             x192(t + 1)
-            xrep(t + 1, range(16), "s")
+            xrep(t + 1, range(8, 16), "s")
             xrep_late(t + 1)
         else:
-            mm("Z1", T.Z1[:, 0:128], T.ONES[0:64, :], T.M192[0:64, :], True, False, ["ONES", "M192"])
+            mm("Z1", T.Z1[:, 0:128], T.ONES[0:64, 0:128], T.M192[0:64, :], True, False, ["ONES", "M192"])
             for c in range(8):
-                mm("Z1", T.Z1[:, 16 * c:16 * c + 16], T.BD[:, c::8], T.J64[:], False, False, BDK + ["J64"])
+                mm("Z1", T.Z1[:, 16 * c:16 * c + 16], T.BD[:, c, :], T.J64[:], False, False, BDK + ["J64"])
             cp(T.SI[:], T.SF[:], ["SF"], ["SI"])
             ts(T.SJ[:], T.SI[:], 1023, None, A.bitwise_and, None, ["SI"], ["SJ"])
             cp(T.OUT[:, 48:64], T.SJ[:], ["SJ"], ["OUT3"])
@@ -570,45 +729,40 @@ def rank_program(g, core, T, topo):
                 else:
                     dma("y", T.yw[gp:gp + 1, 512:768], T.OUTT[p0:p0 + 16, o:o + 16], "d_o1", ["OUTT1"], [], 256)
                     dma("y", T.ys[gp:gp + 1, :], T.OUTT[p0 + 16:p0 + 32, o:o + 16], "d_o1", ["OUTT1"], ["o1"] if gp == 7 else [], 256)
+        if last:
+            for step in range(3):
+                choose(step)
         for k in [me] + [k for k in range(4) if k != me]:
             src = Pt if k == me else LD
-            ts(T.LB[:, k::8], src[:, k * PW:(k + 1) * PW], -32768.0, None, A.add, None,
-               ["P%d" % t if k == me else "LD%d" % t], ["LB%d" % k])
+            ts(T.LA[:, k::4], src[:, k * PW:(k + 1) * PW], -32768.0, 1.0 / 256, A.add, A.mult,
+               ["P%d" % t if k == me else "LD%d" % t], ["LA%d" % k])
+        scan(T.LAS[:], T.SS[:], T.LA[:], A.mult, A.add, ["SS"] + ["LA%d" % k for k in range(4)], ["LAS"])
         for k in range(4):
-            ts(T.LB[:, 4 + k::8], LH[:, k * PW:(k + 1) * PW], -32768.0, None, A.add, None, ["LH%d" % t], ["LB%d" % (k + 4)])
-        scan(T.LBS[:], T.SS[:], T.LB[:], A.mult, A.add, ["SS"] + ["LB%d" % k for k in range(8)], ["LBS"])
-        for s in range(2):
-            o = 8 * (32 + s) + 7
-            ts(T.NR[:, 16 * s:16 * s + 16], T.C260[:], T.LBS[:, o:o + 1], -130.0, A.min, A.add, ["C260", "LBS"], ["NR%d" % s])
-        for i, name in enumerate(("SB2", "SB1", "SB0", "LF0")):
-            mm("Z0", T.Z0[:, i:128:4], T[name][:], T.LBS[:, 7:256:8], False, i == 3, [name, "LBS"])
-            if i == 1:
-                for m, nm in enumerate(("ID", "L2B", "L1B", "ID")):
-                    mm("KY", T.KY[:, m:128:4], T[nm][:], T.NR[:], True, True, [nm, "NR0", "NR1"])
-        tt(T.UU[:], T.KY[:, 0:128], T.THR[:], A.is_lt, ["THR%d" % i for i in range(4)], ["UU"], ["KY"])
-        scan(T.DS[:], T.UU[:], T.Z0[:, 0:128], A.mult, A.add, ["UU"], ["DS"], ["Z0"])
-        own = DL[:, 32 * me:32 * me + 32]
-        ts(own, T.DS[:, 3::4], 190.0, 194.0, A.max, A.min, ["DS"], ["DLo%d" % t])
-        peers = [c for c in mine if c != core]
+            ts(T.LB[:, k::4], LH[:, k * PW:(k + 1) * PW], -32768.0, 1.0 / 256, A.add, A.mult, ["LH%d" % t], ["LB%d" % k])
+        scan(T.LBS[:], T.SS[:], T.LB[:], A.mult, A.add, ["SS"] + ["LB%d" % k for k in range(4)], ["LBS"])
+        for name in ("LAS", "LBS"):
+            for s in range(2):
+                mm("Z0", T.Z0[:, 16 * s:16 * s + 16], T.SEL[:, 128 * s:128 * s + 128], T[name][:, 64 * s + 3:64 * s + 64:4],
+                   False, name == "LBS" and s == 1, ["SEL%d" % s, name])
+        own_d = DL[:, 32 * me:32 * me + 32]
+        ts(own_d, T.Z0[:, 0:32], 190.0, 194.0, A.max, A.min, [], ["DLo%d" % t], ["Z0"])
         tr = [RemoteDMATransfer(dst_ids=[_dst(topo, c, core) for c in peers], dma_engine_mask=_mask(eng),
-                                remote_sem=T.sem["ag%d" % t], srcs=[own], dsts=[own for c in peers])]
+                                remote_sem=T.sem["ag%d" % t], srcs=[own_d], dsts=[own_d for c in peers])]
         sent[0] += ne
         op("g", lambda tr=tr: g.remote_dma_fused(tr, local_sem=T.sem.sent), ["DLo%d" % t])
         ext("ag%d" % t, 3 * ne, ["DLr%d" % t])
         if not last:
-            candidate_list()
-            late_list()
             for h in range(2):
                 fill("EW%d" % h, 0, ["EW%d" % h])
-            if t == 0:
-                keep(T.PERM[:], T.ONES[:], [[-1, 8], [-8, 16]], A.is_equal, 0, 1, ["ONES"], ["PERM"])
-                op("g", lambda: g.iota(T.M192[0:64, :], [[0, 128]], -3, 0, allow_small_or_imprecise_dtypes=True), (), ["M192"])
-            key_start(True)
+            steps()
+            steps_copy()
+            bias_bank("K3")
             mm("Z1", T.Z1[:, 0:128], DL[:], T.ID64[:], False, True, ["DLo%d" % t, "DLr%d" % t, "ID64"])
+            bias_bank("Z2")
             ts(T.ATS[:], T.Z1[:, 0:128], -127.0 / 64, 127.0 / 64, A.max, A.min, [], ["ATS"], ["Z1"])
             expand()
         else:
-            mm("Z1", T.Z1[:, 0:128], DL[:], T.PERM[:], False, True, ["DLo%d" % t, "DLr%d" % t, "PERM"])
+            mm("Z1", T.Z1[:, 0:128], DL[:], T.ID[:], False, True, ["DLo%d" % t, "DLr%d" % t, "ID"])
             ts(T.YA[:], T.Z1[:, 0:128], -127.0, 127.0, A.max, A.min, [], ["YA"], ["Z1"])
             dma("y", T.ya[:], T.YA[:], "d_ya", ["YA"], ["ya"])
     op("g", lambda: g.wait_ge(T.sem.sent, sent[0]), ["o0", "o1", "ya"])

@@ -6,7 +6,7 @@ from concourse.mybir import AxisListType as X
 R = 3
 PW = 32
 QX = 14
-NS = 3
+XV = 2
 BF, F32, F16, I32, U16 = "bfloat16", "float32", "float16", "int32", "uint16"
 
 SCRATCH = {}
@@ -25,7 +25,7 @@ _sb(BF, MU=4096, MT=4096, FR=768, X192=256, A0=128, TA=128, XR=256 * QX + 1024, 
     ZB=128, OC=32, M3=128, M192=128, TB=320, L1B=128, L2B=128, M16=128)
 _sb(F16, WG=512, TT=[16, 2, 16])
 _sb(F32, CF=16, DD=128, KA=128, R16=16, BI=8, U4=16, U4R=16,
-    SP=256, SS=128, R1=512, R2=512, TW=512, SCF=16, SF=16,
+    SP=256, SS=128, R1=512, R2=512, SCF=16, SF=16,
     OUT=64, OUTT=64, LA=128, LB=128, LAS=128, LBS=128, NT=4, BL=48, SEL=256, YA=128)
 _sb(I32, MIX=1032, S0=16, PI=1, CI=8, LOI=64, SI=16, SJ=16, HS=16)
 _sb(U16, LS2=32, CAND=512, XL=64, W16=16, SC16=16, CL16=16)
@@ -39,7 +39,7 @@ for _n in ("ZT0", "ZT1"):
     SCRATCH[_n] = ("psum", [128, 8, 128], BF)
 
 SEMAPHORES = ["qv", "qs", "qp", "qg", "sent", "d_s0", "d_fr0", "d_fr1", "d_a0", "d_mix", "d_mu0", "d_mu1", "d_mu2", "d_mu3",
-              "d_o0", "d_o1", "d_ya"]
+              "d_mw", "d_o0", "d_o1", "d_ya"]
 SEMAPHORES += ["%s%d" % (n, t) for t in range(R) for n in ("rd", "rh", "ag", "hin", "cin", "cn")]
 
 
@@ -59,7 +59,8 @@ def _layout(T, topo):
         for c in mine:
             helpers = [h for h in topo.cores_of(c) if h != c and topo.die(h) == topo.die(c)
                        and all(topo.may_write(h, o) for o in other)]
-            planes[c] = (mine, other, helpers[:2])
+            plain = [h for h in topo.cores_of(c) if h != c and not topo.may_write(h, other[0])]
+            planes[c] = (mine, other, helpers[:2], plain[:2])
     return planes
 
 
@@ -68,32 +69,29 @@ def _dst(topo, dst, src):
     return DstId(rid=rid, pnc=pid)
 
 
-def _hop_engines(topo, rank, helper, peer, t):
-    return [e for e in topo.engines(rank, helper) if e not in topo.engines(rank, peer)]
+def _write(g, T, topo, core, engines, items):
+    part = len(engines) // len(items)
+    g.remote_dma_fused([RemoteDMATransfer(dst_ids=[_dst(topo, dst, core)], dma_engine_mask=_mask(engines[i * part:(i + 1) * part]),
+                                          remote_sem=T.sem[sem], src=src, dst=land)
+                        for i, (dst, sem, src, land) in enumerate(items)], local_sem=T.sem.sent)
 
 
 def helper_program(g, core, owner, T, topo, planes):
-    mine, other, helpers = planes[owner]
-    h, k = helpers.index(core), mine.index(owner)
-    total = 0
-    rank = T.rank_of(owner)
+    mine, other, helpers, plain = planes[owner]
+    k, rank = mine.index(owner), T.rank_of(owner)
+    if core in helpers:
+        targets = other[2 * helpers.index(core):][:2]
+    else:
+        targets = [mine[(k + i) % 4] for i in (1, 2, 3)][plain.index(core)::2]
+    on_chip, eng = len(topo.engines(owner, core)), topo.engines(core, targets[0])
     for t in range(R):
-        for sums in (False, True):
-            g.wait_ge(T.sem[("hin%d" if sums else "cin%d") % t], len(_hop_engines(topo, owner, core, mine[(k + 1) % 4], t)) // 2)
-            tr = []
-            for i in range(2):
-                dst = other[2 * h + i]
-                eng = topo.engines(core, dst)
-                half = len(eng) // 2
-                if sums:
-                    sem, src, land = "rh%d", T["HB%d" % t][:, i * PW:(i + 1) * PW], T["LH%d" % t][:, k * PW:(k + 1) * PW]
-                else:
-                    sem, src, land = "cn%d", T["HC%d" % t][:], T["NC%d" % t][:, 4 * rank:4 * rank + 4]
-                tr.append(RemoteDMATransfer(dst_ids=[_dst(topo, dst, core)], dma_engine_mask=_mask(eng[i * half:(i + 1) * half]),
-                                            remote_sem=T.sem[sem % t], src=src, dst=land))
-                total += half
-            g.remote_dma_fused(tr, local_sem=T.sem.sent)
-    g.wait_ge(T.sem.sent, total)
+        g.wait_ge(T.sem["cin%d" % t], on_chip // 4)
+        _write(g, T, topo, core, eng, [(c, "cn%d" % t, T["HC%d" % t][:], T["NC%d" % t][:, 4 * rank:4 * rank + 4]) for c in targets])
+        if core in helpers:
+            g.wait_ge(T.sem["hin%d" % t], on_chip // 2)
+            _write(g, T, topo, core, eng, [(c, "rh%d" % t, T["HB%d" % t][:, i * PW:(i + 1) * PW], T["LH%d" % t][:, k * PW:(k + 1) * PW])
+                                           for i, c in enumerate(targets)])
+    g.wait_ge(T.sem.sent, R * len(eng) * (2 if core in helpers else 1))
 
 
 def _emit(ops, g, T):
@@ -206,10 +204,10 @@ def rank_program(g, core, T, topo):
     planes = _layout(T, topo)
     if T.rank_of(core) is None:
         for c in planes:
-            if core in planes[c][2]:
+            if core in planes[c][2] + planes[c][3]:
                 helper_program(g, core, c, T, topo, planes)
         return
-    mine, other, helpers = planes[core]
+    mine, other, helpers, plain = planes[core]
     me, rank = mine.index(core), T.rank_of(core)
     V, S, P = g.vector, g.scalar, g.tensor
     ops = []
@@ -217,6 +215,10 @@ def rank_program(g, core, T, topo):
 
     def op(e, f, r=(), w=(), b=(), sem=None, n=0):
         ops.append({"e": e, "f": f, "r": list(r), "w": list(w), "b": list(b), "sem": sem, "n": n})
+
+    def write(engines, items, r):
+        op("g", lambda: _write(g, T, topo, core, engines, items), r)
+        sent[0] += len(engines)
 
     def ext(sem, n, w):
         ops.append({"e": "ext", "sem": sem, "n": n, "w": list(w)})
@@ -258,7 +260,7 @@ def rank_program(g, core, T, topo):
 
     MTK = ["MT%d" % c for c in range(8)]
     XRK = ["XR%d" % i for i in range(16)]
-    BDK = ["BD%d" % i for i in range(8)]
+    BDK = [["BD%d%d" % (k, i) for i in range(8)] for k in range(2)]
     PM = [[T.P00, T.P01], [T.P10, T.P11]]
     NM = [[T.N00, T.N01], [T.N10, T.N11]]
     MUK = ["MU%d" % i for i in range(4)]
@@ -273,6 +275,7 @@ def rank_program(g, core, T, topo):
     dma("y", T.MIX[:, 0:1024], T.mix[:], "d_mix", w=["MIX"])
     dma("s", T.S0[:], T.s0[:], "d_s0", w=["S0"])
     dma("s", T.FR[:, 0:256], T.fr[:, 0:256], "d_fr0", w=["FR0"])
+    dma("s", T.MIX[:, 1024:1028], T.mix[:, 0:4], "d_mw", w=["MIXW"])
     for i in range(4):
         dma("y", T.MU[:, 1024 * i:1024 * i + 1024], T.mu[:, 1024 * i:1024 * i + 1024], "d_mu%d" % i, w=[MUK[i]])
     dma("y", T.FR[:, 256:768], T.fr[:, 256:768], "d_fr1", w=["FR1", "FR2"])
@@ -303,31 +306,32 @@ def rank_program(g, core, T, topo):
     def keep(out, in_, pat, cmp, base, cm, r, w):
         op("g", lambda: g.affine_select(out, in_, pat, cmp, 0.0, base, cm), r, w)
 
-    def band(name, src, pat, base, width):
-        keep(T[name][:], T[src][:], pat, A.is_ge, base, 1, [src], [name])
-        keep(T[name][:], T[name][:], [[-a, n] for a, n in pat], A.is_ge, width - 1 - base, -1, [name], [name])
-
     keep(T.ID[:], ones, [[-1, 128]], A.is_equal, 0, 1, ["ONES"], ["ID"])
 
+    iota(T.TB[0:64, 0:256], [[0, 8], [-1, 16], [-16, 2]], 0, ["TB0"])
+    for name, value, keys in (("ZR", 0.0, ["ZR"]), ("SS", 1.0, ["SS"]), ("C260", 260.0, ["C260"])):
+        act(T[name][:], ones, F.Identity, ["ONES"], keys, scale=value)
+    act(T.BL[:], T.ONES[:, 0:48], F.Identity, ["ONES"], ["BL0", "BL1", "BL2"])
+
     def late_constants():
-        iota(T.TB[0:64, 0:256], [[0, 8], [-1, 16], [-16, 2]], 0, ["TB0"])
         iota(T.TB[0:64, 256:320], [[0, 2], [-1, 32]], 0, ["TB1"])
         fill("SP", -16000000, ["SP"])
         keep(T.SP[:], T.SP[:], [[0, 8], [1, 32]], A.is_equal, 0, 0, ["SP"], ["SP"])
         for i in range(16):
             keep(T.XR[:, XO + i::16], T.XT[:], [[0, 64]], A.is_equal, 0, 0, ["XT%d" % q for q in range(4)], [XYK[i]])
         fill("EW0", 0, ["EW0"])
-        fill("ZR", 0, ["ZR"])
         fill("EW1", 0, ["EW1"])
-        fill("SS", 1, ["SS"])
-        fill("C260", 260, ["C260"])
+        for sign in (1, -1):
+            for l in (1, 2):
+                w, name = 16 << l, "L%dB" % l
+                src = "M16" if sign == 1 else name
+                keep(T[name][:], T[src][:], [[-sign * w, 128 // w], [0, w]], A.is_ge, 0 if sign == 1 else w - 1, sign, [src], [name])
+            for l in range(3):
+                w, part, key = 1 << l, T.BL[:, 16 * l:16 * l + 16], ["BL%d" % l]
+                keep(part, part, [[-16 * sign, 2], [-w * sign, 8 // w], [0, w]], A.is_ge,
+                     -32 * me if sign == 1 else w - 1 + 32 * me, sign, key, key)
         keep(T.SS[:], T.SS[:], [[0, PW], [1, 4]], A.is_gt, 0, 0, ["SS"], ["SS"])
         iota(T.KE[:], [[1, 16], [0, 16]], 0, ["KE"])
-        fill("BL", 1, ["BL0", "BL1", "BL2"])
-        for l in range(3):
-            w, part, key = 1 << l, T.BL[:, 16 * l:16 * l + 16], ["BL%d" % l]
-            keep(part, part, [[-16, 2], [-w, 8 // w], [0, w]], A.is_ge, -32 * me, 1, key, key)
-            keep(part, part, [[16, 2], [w, 8 // w], [0, w]], A.is_ge, w - 1 + 32 * me, -1, key, key)
 
     def heights():
         ts(T.LEV[:], T.M16[:], -96.0, 99.0, A.mult, A.add, ["M16"], ["LEV"])
@@ -338,8 +342,6 @@ def rank_program(g, core, T, topo):
 
     def tree_constants():
         act(T.ID64[:], T.ID[:], F.Identity, ["ID"], ["ID64"], scale=1.0 / 64)
-        for l in (1, 2):
-            band("L%dB" % l, "M16", [[-16 << l, 8 >> l], [0, 16 << l]], 0, 16 << l)
         op("g", lambda: g.iota(T.M192[0:64, :], [[0, 128]], -3, 0, allow_small_or_imprecise_dtypes=True), (), ["M192"])
 
     ts(T.CI[:, 3:4], T.PI[:], 4, None, A.arith_shift_right, None, ["PI"], ["CI3"])
@@ -364,13 +366,15 @@ def rank_program(g, core, T, topo):
     def bias_bank(z):
         mm(z, T[z][:], T.ZB[0:64, :], T.ONES[0:64, :], True, False, ["ONES", "ZBa", "ZBb"])
 
-    def expand():
+    def expand(ks, on_v):
+        c0, c1 = 4 * ks[0], 4 * ks[-1] + 4
         for gp in range(8):
-            out = T.BD[:, :, 16 * gp:16 * gp + 16]
-            if gp < 6:
-                ts(out, T.ATS[:], T.BI[:, gp:gp + 1], None, A.mult, None, ["ATS", "BI"], [BDK[gp]])
+            out, src = T.BD[:, c0:c1, 16 * gp:16 * gp + 16], T.ATS[:, 16 * c0:16 * c1]
+            r, w = ["ATS%d" % k for k in ks] + ["BI"], [BDK[k][gp] for k in ks]
+            if gp < on_v:
+                ts(out, src, T.BI[:, gp:gp + 1], None, A.mult, None, r, w)
             else:
-                act(out, T.ATS[:], F.Identity, ["ATS", "BI"], [BDK[gp]], scale=T.BI[:, gp:gp + 1])
+                act(out, src, F.Identity, r, w, scale=T.BI[:, gp:gp + 1])
 
     def xrep(t, which, eng):
         src = T.FR[:, 256 * t:256 * t + NX]
@@ -393,16 +397,21 @@ def rank_program(g, core, T, topo):
         for h in range(2):
             ts(T.LS2[:, 16 * h:16 * h + 16], src[:, 0:16], float(h), None, A.add, None, [key], ["LS2%d" % h])
 
-    def candidates():
-        ts(T.WG[:], T.MIX[:, 0:1028].indirect(T.LS2[:]), -2048.0, None, A.add, None, ["MIX", "MIXW", "LS20", "LS21"], ["WG"])
+    def candidates(h):
+        ts(T.WG[:, 256 * h:256 * h + 256], T.MIX[:, 0:1028].indirect(T.LS2[:, 16 * h:16 * h + 16]), -2048.0, None, A.add, None,
+           ["MIX", "MIXW", "LS2%d" % h], ["WG%d" % h])
+
+    def early_list():
         for h in range(2):
-            ts(T.CAND[:, NX * h:NX * h + NX], T.WG[:, 256 * h:256 * h + NX], 2048.0, None, A.add, None, ["WG"], ["CAND%d" % h])
+            ts(T.CAND[:, NX * h:NX * h + NX], T.WG[:, 256 * h:256 * h + NX], 2048.0, None, A.add, None, ["WG%d" % h], ["CAND%d" % h])
+
+    def late_list():
         for k in range(4):
             o = 256 * (k % 2) + NX + 16 * (k // 2)
-            ts(T.CAND[:, 2 * NX + k:512:4], T.WG[:, o:o + 16], 2048.0, None, A.add, None, ["WG"], [CYK[k]])
+            ts(T.CAND[:, 2 * NX + k:512:4], T.WG[:, o:o + 16], 2048.0, None, A.add, None, ["WG%d" % (k % 2)], [CYK[k]])
 
     def turn_list():
-        op("v", lambda: V.transpose(T.TT[:], T.WG[:]), ["WG"], ["TT"])
+        op("v", lambda: V.transpose(T.TT[:], T.WG[:]), ["WG0", "WG1"], ["TT"])
 
     def steps():
         for q2 in range(2):
@@ -419,9 +428,7 @@ def rank_program(g, core, T, topo):
                     if h == 0:
                         mm("Z2", T.Z2[:, n, o + 15:o + 16], NM[g2][q2][:], T.TT[:, 8 + n, g2, 0:1], False, False, r)
                     mm("Z2", T.Z2[:, n, o:o + 15], NM[g2][q2][:], T.TT[:, b + n, g2, 1:16], False, g2 == 1, r)
-
-    def steps_copy():
-        act(T.TW[:], T.Z2[:], F.Copy, [], ["TW"], ["Z2"])
+        ops[-1]["w"], ops[-1]["stop"] = ["TW"], 3
 
     def key_start(k, n):
         o = 256 if k == "K3" else 0
@@ -440,20 +447,23 @@ def rank_program(g, core, T, topo):
     xrep(0, range(0, 4), "v")
     xrep(0, range(4, 10), "g")
     xrep(0, range(10, 12), "s")
-    ts(T.ATS[:], T.Z1[:, 0:128], 1.0 / 64, None, A.mult, None, [], ["ATS"], ["Z1"])
-    expand()
+    ts(T.ATS[:], T.Z1[:, 0:128], 1.0 / 64, None, A.mult, None, [], ["ATS0", "ATS1"], ["Z1"])
+    expand((0, 1), 6)
     xrep(0, range(12, 16), "v")
-    cp(T.MIX[:, 1024:1028], T.MIX[:, 0:4], ["MIX"], ["MIXW"])
     for k in range(4):
         o = NX + 16 * (k // 2)
         act(T.XT[:, k::4], T.X192[:, o:o + 16], F.Copy, ["X192"], ["XT%d" % k])
     late_constants()
-    candidates()
+    candidates(0)
+    candidates(1)
+    early_list()
+    turn_list()
+    late_list()
 
     for t in range(R):
         last = t == R - 1
         NC = T["NC%d" % t]
-        zbank = {0: "Z2", 3: "K3", 6: "Z2", 1: "Z0", 2: "Z1", 4: "Z0", 5: "Z1", 7: "Z0"}
+        zbank = {0: "Z2", 3: "K3", 6: "Z2", 1: "Z0", 2: "Z1", 4: "K1", 5: "K2", 7: "Z0"}
         vplan = {0: [("d", 0)], 3: [("d", 3), ("c", 1), ("c", 2)], 6: [("d", 6), ("c", 4)], 7: [("c", 5), ("c", 7)]}
         SCL, order = [1, 2, 4, 5, 7], (1, 0, 2, 3, 4, 5, 6, 7)
         if t == 0:
@@ -464,7 +474,7 @@ def rank_program(g, core, T, topo):
             z = zbank[c]
             if c == 5 and t:
                 bias_bank(zbank[6])
-            mm(z, T[z][:], T.BD[:, c, :], T.MU[:, 512 * c:512 * c + 512], c in SCL, True, BDK + ["MU%d" % (c // 2)])
+            mm(z, T[z][:], T.BD[:, c, :], T.MU[:, 512 * c:512 * c + 512], c in SCL, True, BDK[c // 4] + ["MU%d" % (c // 2)])
             if c in SCL:
                 act(T.MT[:, 512 * c:512 * c + 512], T[z][:], F.Identity, [], [MTK[c]], [z], bias=192.0 + 1.0 / 128)
             for kind, d in vplan.get(c, []):
@@ -475,9 +485,8 @@ def rank_program(g, core, T, topo):
                 else:
                     ts(dst, dst, 184.0, 199.0, A.max, A.min, [MTK[d]], [MTK[d]])
 
-        if t == 0:
-            key_start("K1", 8)
-            key_start("K2", 6)
+        key_start("K1", 8)
+        key_start("K2", 6)
 
         def own(h, q, z, n=2):
             b, keys = QX * h + q, ["D%d_%d" % (h, k) for k in range(q, q + n)]
@@ -531,7 +540,10 @@ def rank_program(g, core, T, topo):
             elif step == 1:
                 tt(T.NM[:, a:b], keys, T.R1[:, a:b], A.not_equal, ["R1" + k], ["NM" + k], [k])
             else:
-                scan(T.R2[:, a:b], T.NM[:, a:b], T.TW[:, a:b], A.mult, A.add, ["NM" + k, "TW"], ["R2" + k])
+                for n in range(q0 // 2, q1 // 2):
+                    part = slice(64 * n, 64 * n + 64)
+                    scan(T.R2[:, part], T.NM[:, part], T.Z2[:, n, :], A.mult, A.add, ["NM" + k, "TW"],
+                         ["R2" + k if 2 * n + 2 == q1 else "R2%d" % n], ["Z2"])
 
         def sums_lists(k, q0, q1):
             r = ["R2" + n for n in k.split()]
@@ -610,69 +622,58 @@ def rank_program(g, core, T, topo):
                    T.PT[:, 128 * h + 16 * gp:128 * h + 16 * gp + 16], False, h == 1 and gp == 7,
                    ["PT%d" % h, "ET%d%d" % (h, gp // 4)])
 
+        def move(step):
+            if step == 0:
+                ts(T.SI[:], T.R1[:, 31::32], -1.0 / 64, None, A.mult, None, ["R1" + k for k in HK[0] + HK[1]], ["SI"])
+                ts(T.OUT[:, 16 * t:16 * t + 16], T.R2[:, 31::32], 2048.0, None, A.add, None, ["R2" + k for k in HK[0] + HK[1]], ["OUT%d" % t])
+            elif step == 1:
+                ts(T.HS[:], T.SI[:], 4, 1, A.arith_shift_right, A.bitwise_and, ["SI"], ["HS"])
+            elif step == 2:
+                tt(T.SF[:], T.SF[:], T.HS[:], A.add, ["SF", "HS"], ["SF"])
+            elif not last:
+                states(T.SF, "SF")
+            else:
+                cp(T.SI[:], T.SF[:], ["SF"], ["SI"])
+
         K1, K2, K3, K23 = ("K1", 0, 8), ("K2", 8, QX), ("K3", QX, 16), ("K2 K3", 8, 16)
         a, b, c, d = (0, 0, "Z1"), (0, 2, "K3"), (0, 8, "Z1"), (0, 10, "Z0", 1)
-        first = t == 0
-        on_v = [(gather, 0, 4, 8)] + [(turn_list,)] * first + [
-            (gather, 1, 0, 4), (gather, 1, 4, 8), (gather, 0, 11, 14), (gather, 1, 8, 10),
+        on_v = [
+            (gather, 0, 4, 8), (gather, 1, 0, 4), (gather, 1, 4, 8), (gather, 0, 11, 14), (gather, 1, 8, 10),
             (pick, 0, *K1), (gather, 1, 10, 12), (pick, 1, *K1), (gather, 1, 12, 14), (pick, 2, *K1),
             (late_gather, 0, 8), (sums_lists, *K1), (late_gather, 8, 12), (sums_gather, *K1), (late_gather, 12, 16), (pick, 0, *K2),
             (sums_scatter, *K1), (pick, 1, *K2), (pick, 0, *K3), (pick, 2, *K2), (pick, 1, *K3), (pick, 2, *K3),
-            (sums_lists, *K23), (sums_gather, *K23), (sums_scatter, *K23), (sums_copy, 1, 0, "v"), (sums_copy, 1, 1, "v")]
-        on_s = [(own, *a), (own, *b), (own_square, *a), (own_square, *b), (square, 0, 4, 8), (square, 1, 0, 4), (square, 1, 4, 8)]
-        on_s += [(steps_copy,)] * first + [
+            (sums_lists, *K23), (sums_gather, *K23), (move, 0), (sums_scatter, *K23), (move, 1), (move, 2),
+            (sums_copy, 1, 0, "v"), (sums_copy, 1, 1, "v"), (move, 3)]
+        on_s = [
+            (own, *a), (own, *b), (own_square, *a), (square, 0, 4, 8), (own_square, *b), (square, 1, 0, 4), (square, 1, 4, 8),
             (own, *c), (own, *d), (square, 0, 11, 14), (own_square, *c), (own_square, *d), (square, 1, 8, 12), (square, 1, 12, 14),
             (late_square, 0, 8), (late_square, 8, 12), (late_square, 12, 16), (sums_side, 0), (sums_count, 0),
-            (sums_plain_copy, 0), (sums_copy, 0, 0, "s"), (sums_copy, 0, 1, "s"), (sums_count, 1),
-            (sums_side, 1), (sums_plain_copy, 1)]
-        on_p = [(own_sub, *a), (own_sub, *b), (add, 0, 0, 4), (key_start, "K3", 2)] + [(steps,)] * first + [
-            (add, 0, 4, 8), (add, 1, 0, 4), (add, 1, 4, 8, True), (own_sub, *c), (own_sub, *d), (add, 0, 11, 14), (add, 0, 8, 11),
-            (add, 1, 8, 12), (add, 1, 12, 14, True), (late_add, 0, 8), (late_add, 8, 12), (late_add, 12, 16), (sums_plain, 0),
-            (sums_turn, 0, 0), (sums_turn, 0, 1), (sums_add, 0, 0), (sums_add, 0, 1), (sums_plain, 1),
-            (sums_turn, 1, 0), (sums_turn, 1, 1), (sums_add, 1, 0), (sums_add, 1, 1)]
+            (sums_copy, 0, 0, "s"), (sums_plain_copy, 0), (sums_count, 1), (sums_side, 1), (sums_copy, 0, 1, "s"),
+            (sums_plain_copy, 1)]
+        on_p = [
+            (steps,), (own_sub, *a), (own_sub, *b), (add, 0, 4, 8), (add, 0, 0, 4),
+            (key_start, "K3", 2), (add, 1, 0, 4), (add, 1, 4, 8, True), (own_sub, *c), (own_sub, *d), (add, 0, 11, 14), (add, 0, 8, 11),
+            (add, 1, 8, 12), (add, 1, 12, 14, True), (late_add, 0, 8), (late_add, 8, 12), (late_add, 12, 16),
+            (sums_turn, 0, 0), (sums_turn, 0, 1), (sums_plain, 0), (sums_add, 0, 0), (sums_plain, 1),
+            (sums_turn, 1, 0), (sums_turn, 1, 1), (sums_add, 0, 1), (sums_add, 1, 0), (sums_add, 1, 1)]
         _weave(ops, [on_v, on_s, on_p])
         Pt, LD, LH, DL = T["P%d" % t], T["LD%d" % t], T["LH%d" % t], T["DL%d" % t]
         ts(Pt[:], T.Z0[:, 0:4 * PW], -1.0, 32768.0, A.mult, A.add, [], ["P%d" % t], ["Z0"])
 
         peers = [c for c in mine if c != core]
-        eng = topo.engines(core, peers[0])
-        counts, r = NC[:, 4 * rank:4 * rank + 4], ["NC%d0" % t, "NC%d1" % t, "NCz"]
-        tr = []
-        for i, hc in enumerate(helpers):
-            hop = _hop_engines(topo, core, hc, peers[0], t)
-            half = len(hop) // 2
-            tr.append(RemoteDMATransfer(dst_ids=[_dst(topo, hc, core)], dma_engine_mask=_mask(hop[i * half:(i + 1) * half]),
-                                        remote_sem=T.sem["cin%d" % t], src=counts, dst=T["HC%d" % t][:]))
-            sent[0] += half
-        op("g", lambda tr=tr: g.remote_dma_fused(tr, local_sem=T.sem.sent), r)
-        tr = [RemoteDMATransfer(dst_ids=[_dst(topo, c, core) for c in peers], dma_engine_mask=_mask(eng),
-                                remote_sem=T.sem["cn%d" % t], srcs=[counts], dsts=[counts for c in peers])]
-        sent[0] += len(eng)
-        op("g", lambda tr=tr: g.remote_dma_fused(tr, local_sem=T.sem.sent), r)
-        ext("cn%d" % t, 3 * len(eng) + 4 * (len(eng) // 2), ["NCr%d" % t])
-
-        tr = []
-        for i, hc in enumerate(helpers):
-            eng = _hop_engines(topo, core, hc, mine[(me + 1) % 4], t)
-            half = len(eng) // 2
-            tr.append(RemoteDMATransfer(dst_ids=[_dst(topo, hc, core)], dma_engine_mask=_mask(eng[i * half:(i + 1) * half]),
-                                        remote_sem=T.sem["hin%d" % t], src=Pt[:, 2 * i * PW:(2 * i + 2) * PW], dst=T["HB%d" % t][:]))
-            sent[0] += half
-        op("g", lambda tr=tr: g.remote_dma_fused(tr, local_sem=T.sem.sent), ["P%d" % t])
-        tr = []
-        eng = topo.engines(core, mine[(me + 1) % 4])
+        eng, on_chip = topo.engines(core, peers[0]), topo.engines(core, helpers[0])
         ne = len(eng)
-        for i, (lo, hi) in enumerate(((0, ne // 2), (ne // 2, 3 * ne // 4), (3 * ne // 4, ne))):
-            k = (me + 1 + i) % 4
-            tr.append(RemoteDMATransfer(dst_ids=[_dst(topo, mine[k], core)], dma_engine_mask=_mask(eng[lo:hi]),
-                                        remote_sem=T.sem["rd%d" % t], src=Pt[:, k * PW:(k + 1) * PW],
-                                        dst=LD[:, me * PW:(me + 1) * PW]))
-        sent[0] += ne
-        op("g", lambda tr=tr: g.remote_dma_fused(tr, local_sem=T.sem.sent), ["P%d" % t])
-        ext("rd%d" % t, ne, ["LD%d" % t])
-        ext("rh%d" % t, 4 * (ne // 2), ["LH%d" % t])
+        counts, r = NC[:, 4 * rank:4 * rank + 4], ["NC%d0" % t, "NC%d1" % t, "NCz"]
+        write([e for e in on_chip if e not in eng], [(c, "cin%d" % t, counts, T["HC%d" % t][:]) for c in helpers], r)
+        write(eng, [(c, "cin%d" % t, counts, T["HC%d" % t][:]) for c in plain], r)
+        ext("cn%d" % t, 4 * ne, ["NCr%d" % t])
+        write(on_chip, [(c, "hin%d" % t, Pt[:, 2 * i * PW:(2 * i + 2) * PW], T["HB%d" % t][:]) for i, c in enumerate(helpers)], ["P%d" % t])
+        for steps_on in ((1, 2), (3,)):
+            ks = [(me + i) % 4 for i in steps_on]
+            write(eng, [(mine[k], "rd%d" % t, Pt[:, k * PW:(k + 1) * PW], LD[:, me * PW:(me + 1) * PW]) for k in ks], ["P%d" % t])
+        ext("rd%d" % t, 2 * ne, ["LD%d" % t])
+        ext("rh%d" % t, 2 * ne, ["LH%d" % t])
 
-        RK = ["K1", "K2", "K3"]
         if t == 0:
             tree_constants()
 
@@ -688,38 +689,22 @@ def rank_program(g, core, T, topo):
                     tt(T.SEL[:, 128 * s:128 * s + 128], T.K3[:, 128 * s:128 * s + 128], T.LEV[:], A.is_ge, ["LEV"], ["SEL%d" % s], ["K3"])
 
         mm("Z0", T.Z0[:, 0:32], T.ONES[0:64, 0:128], T.OC[0:64, :], True, False, ["ONES", "OCa", "OCb"])
-        ts(T.SI[:], T.R1[:, 31::32], -1.0 / 64, None, A.mult, None, ["R1" + k for k in RK], ["SI"])
-        ts(T.HS[:], T.SI[:], 4, 1, A.arith_shift_right, A.bitwise_and, ["SI"], ["HS"])
-        ts(T.OUT[:, 16 * t:16 * t + 16], T.R2[:, 31::32], 2048.0, None, A.add, None, ["R2" + k for k in RK], ["OUT%d" % t])
-        tt(T.SF[:], T.SF[:], T.HS[:], A.add, ["SF", "HS"], ["SF"])
         if not last:
             mm("Z1", T.Z1[:, 0:128], T.ONES[0:64, 0:128], T.M3[0:64, :], True, False, ["ONES", "M3"])
-            mm("Z1", T.Z1[:, 0:128], T.ID[:], T.ATS[:], False, False, ["ID", "ATS"])
-            key_start("K1", 8)
-            key_start("K2", 6)
-            states(T.SF, "SF")
-            xrep(t + 1, range(0, 2), "v")
-            candidates()
-            turn_list()
-            if t == 0:
-                heights()
-            choose(0)
-            xrep(t + 1, range(2, 5), "v")
-            choose(1)
-            xrep(t + 1, range(5, 8), "v")
-            choose(2)
+            mm("Z1", T.Z1[:, 0:128], T.ID[:], T.ATS[:], False, False, ["ID", "ATS0", "ATS1"])
             x192(t + 1)
-            xrep(t + 1, range(8, 16), "s")
+            xrep(t + 1, range(XV, 16), "s")
             xrep_late(t + 1)
         else:
             mm("Z1", T.Z1[:, 0:128], T.ONES[0:64, 0:128], T.M192[0:64, :], True, False, ["ONES", "M192"])
             for c in range(8):
-                mm("Z1", T.Z1[:, 16 * c:16 * c + 16], T.BD[:, c, :], T.J64[:], False, False, BDK + ["J64"])
-            cp(T.SI[:], T.SF[:], ["SF"], ["SI"])
+                mm("Z1", T.Z1[:, 16 * c:16 * c + 16], T.BD[:, c, :], T.J64[:], False, False, BDK[c // 4] + ["J64"])
+
+        def last_states():
             ts(T.SJ[:], T.SI[:], 1023, None, A.bitwise_and, None, ["SI"], ["SJ"])
             cp(T.OUT[:, 48:64], T.SJ[:], ["SJ"], ["OUT3"])
-        if t >= 1:
-            blk = t - 1
+
+        def store(blk):
             op("v", lambda blk=blk: V.transpose(T.OUTT[:, 32 * blk:32 * blk + 32], T.OUT[:, 32 * blk:32 * blk + 32]),
                ["OUT%d" % (2 * blk), "OUT%d" % (2 * blk + 1)], ["OUTT%d" % blk])
             for gp in range(8):
@@ -729,17 +714,42 @@ def rank_program(g, core, T, topo):
                 else:
                     dma("y", T.yw[gp:gp + 1, 512:768], T.OUTT[p0:p0 + 16, o:o + 16], "d_o1", ["OUTT1"], [], 256)
                     dma("y", T.ys[gp:gp + 1, :], T.OUTT[p0 + 16:p0 + 32, o:o + 16], "d_o1", ["OUTT1"], ["o1"] if gp == 7 else [], 256)
-        if last:
-            for step in range(3):
-                choose(step)
-        for k in [me] + [k for k in range(4) if k != me]:
-            src = Pt if k == me else LD
-            ts(T.LA[:, k::4], src[:, k * PW:(k + 1) * PW], -32768.0, 1.0 / 256, A.add, A.mult,
-               ["P%d" % t if k == me else "LD%d" % t], ["LA%d" % k])
-        scan(T.LAS[:], T.SS[:], T.LA[:], A.mult, A.add, ["SS"] + ["LA%d" % k for k in range(4)], ["LAS"])
-        for k in range(4):
-            ts(T.LB[:, k::4], LH[:, k * PW:(k + 1) * PW], -32768.0, 1.0 / 256, A.add, A.mult, ["LH%d" % t], ["LB%d" % k])
-        scan(T.LBS[:], T.SS[:], T.LB[:], A.mult, A.add, ["SS"] + ["LB%d" % k for k in range(4)], ["LBS"])
+        def near(ks):
+            for k in ks:
+                src = Pt if k == me else LD
+                ts(T.LA[:, k::4], src[:, k * PW:(k + 1) * PW], -32768.0, 1.0 / 256, A.add, A.mult,
+                   ["P%d" % t if k == me else "LD%d" % t], ["LA%d" % k])
+
+        def add_up(name):
+            scan(T[name + "S"][:], T.SS[:], T[name][:], A.mult, A.add, ["SS"] + [name + "%d" % k for k in range(4)], [name + "S"])
+
+        def far():
+            for k in range(4):
+                ts(T.LB[:, k::4], LH[:, k * PW:(k + 1) * PW], -32768.0, 1.0 / 256, A.add, A.mult, ["LH%d" % t], ["LB%d" % k])
+
+        others = [k for k in range(4) if k != me]
+        if t == 0:
+            candidates(0)
+            candidates(1)
+            early_list()
+            heights()
+            near([me] + others)
+            add_up("LA")
+            choose(0)
+            choose(1)
+            far()
+            choose(2)
+        else:
+            near([me])
+            choose(0)
+            last_states() if last else candidates(0)
+            choose(1)
+            store(1) if last else candidates(1)
+            choose(2)
+            near(others)
+            far()
+            add_up("LA")
+        add_up("LB")
         for name in ("LAS", "LBS"):
             for s in range(2):
                 mm("Z0", T.Z0[:, 16 * s:16 * s + 16], T.SEL[:, 128 * s:128 * s + 128], T[name][:, 64 * s + 3:64 * s + 64:4],
@@ -754,13 +764,20 @@ def rank_program(g, core, T, topo):
         if not last:
             for h in range(2):
                 fill("EW%d" % h, 0, ["EW%d" % h])
-            steps()
-            steps_copy()
+            if t:
+                early_list()
+                store(0)
+            turn_list()
+            late_list()
+            xrep(t + 1, range(0, XV), "v")
+            bias_bank("Z2")
             bias_bank("K3")
             mm("Z1", T.Z1[:, 0:128], DL[:], T.ID64[:], False, True, ["DLo%d" % t, "DLr%d" % t, "ID64"])
-            bias_bank("Z2")
-            ts(T.ATS[:], T.Z1[:, 0:128], -127.0 / 64, 127.0 / 64, A.max, A.min, [], ["ATS"], ["Z1"])
-            expand()
+            for k in range(2):
+                half = slice(64 * k, 64 * k + 64)
+                ts(T.ATS[:, half], T.Z1[:, half], -127.0 / 64, 127.0 / 64, A.max, A.min, [], ["ATS%d" % k], ["Z1"])
+            expand((0,), 6)
+            expand((1,), 8)
         else:
             mm("Z1", T.Z1[:, 0:128], DL[:], T.ID[:], False, True, ["DLo%d" % t, "DLr%d" % t, "ID"])
             ts(T.YA[:], T.Z1[:, 0:128], -127.0, 127.0, A.max, A.min, [], ["YA"], ["Z1"])

from concourse.bass import DstId, RemoteDMATransfer
from concourse.mybir import AluOpType as A
from concourse.mybir import ActivationFunctionType as F
from concourse.mybir import AxisListType as X

R = 3
PW = 32
QX = 14
XV = 2
BF, F32, F16, I32, U16 = "bfloat16", "float32", "float16", "int32", "uint16"

SCRATCH = {}


def _sb(dtype, **kw):
    for k, v in kw.items():
        SCRATCH[k] = ("sbuf", [128] + (v if isinstance(v, list) else [v]), dtype)


_sb(BF, MU=4096, MT=4096, FR=768, X192=256, A0=128, TA=128, XR=256 * QX + 1024, D=8192, SQ=[2 * QX, 16, 16], SQY=1024,
    ATS=128, BD=[8, 128], NE=256, MW=256, EW0=1024, EW1=1024, ET0=[8, 128], ET1=[8, 128],
    PT=256, FN=256, ZR=128, UB=128, EX=256, KE=256, C260=128, LEV=128, DL0=128, DL1=128, DL2=128, NM=512,
    ONES=512, ID=128, XT=64, ID64=128, P00=128, P01=128, P10=128, P11=128,
    N00=128, N01=128, N10=128, N11=128, SW=144, J64=16, OH=16,
    ZB=128, OC=32, M3=128, M192=128, TB=320, L1B=128, L2B=128, M16=128)
_sb(F16, WG=512, TT=[16, 2, 16])
_sb(F32, CF=16, DD=128, KA=128, R16=16, BI=8, U4=16, U4R=16,
    SP=256, SS=128, R1=512, R2=512, SCF=16, SF=16,
    OUT=64, OUTT=64, LA=128, LB=128, LAS=128, LBS=128, NT=4, BL=48, SEL=256, YA=128)
_sb(I32, MIX=1032, S0=16, PI=1, CI=8, LOI=64, SI=16, SJ=16, HS=16)
_sb(U16, LS2=32, CAND=512, XL=64, W16=16, SC16=16, CL16=16)
for _t in range(R):
    _sb(U16, **{"P%d" % _t: 4 * PW, "LD%d" % _t: 4 * PW, "LH%d" % _t: 4 * PW, "HB%d" % _t: 2 * PW})
    _sb(F32, **{"NC%d" % _t: 32, "HC%d" % _t: 4})
for _n in ("Z0", "Z1", "K1", "K2", "K3"):
    SCRATCH[_n] = ("psum", [128, 512], F32)
SCRATCH["Z2"] = ("psum", [128, 8, 64], F32)
for _n in ("ZT0", "ZT1"):
    SCRATCH[_n] = ("psum", [128, 8, 128], BF)

SEMAPHORES = ["qv", "qs", "qp", "qg", "sent", "d_s0", "d_fr0", "d_fr1", "d_a0", "d_mix", "d_mu0", "d_mu1", "d_mu2", "d_mu3",
              "d_mw", "d_o0", "d_o1", "d_ya"]
SEMAPHORES += ["%s%d" % (n, t) for t in range(R) for n in ("rd", "rh", "ag", "hin", "cin", "cn")]


def _mask(engines):
    m = 0
    for e in engines:
        m |= 1 << e
    return m


def _layout(T, topo):
    cores = list(T.cores)
    first = [c for c in cores if c == cores[0] or topo.may_write(cores[0], c)]
    second = [c for c in cores if c not in first]
    planes = {}
    for mine, other in ((first, second), (second, first)):
        for c in mine:
            helpers = [h for h in topo.cores_of(c) if h != c and topo.die(h) == topo.die(c)
                       and all(topo.may_write(h, o) for o in other)]
            plain = [h for h in topo.cores_of(c) if h != c and not topo.may_write(h, other[0])]
            planes[c] = (mine, other, helpers[:2], plain[:2])
    return planes


def _dst(topo, dst, src):
    rid, pid = topo.addr(dst, src)
    return DstId(rid=rid, pnc=pid)


def _write(g, T, topo, core, engines, items):
    part = len(engines) // len(items)
    g.remote_dma_fused([RemoteDMATransfer(dst_ids=[_dst(topo, dst, core)], dma_engine_mask=_mask(engines[i * part:(i + 1) * part]),
                                          remote_sem=T.sem[sem], src=src, dst=land)
                        for i, (dst, sem, src, land) in enumerate(items)], local_sem=T.sem.sent)


def helper_program(g, core, owner, T, topo, planes):
    mine, other, helpers, plain = planes[owner]
    k, rank = mine.index(owner), T.rank_of(owner)
    if core in helpers:
        targets = other[2 * helpers.index(core):][:2]
    else:
        targets = [mine[(k + i) % 4] for i in (1, 2, 3)][plain.index(core)::2]
    on_chip, eng = len(topo.engines(owner, core)), topo.engines(core, targets[0])
    for t in range(R):
        g.wait_ge(T.sem["cin%d" % t], on_chip // 4)
        _write(g, T, topo, core, eng, [(c, "cn%d" % t, T["HC%d" % t][:], T["NC%d" % t][:, 4 * rank:4 * rank + 4]) for c in targets])
        if core in helpers:
            g.wait_ge(T.sem["hin%d" % t], on_chip // 2)
            _write(g, T, topo, core, eng, [(c, "rh%d" % t, T["HB%d" % t][:, i * PW:(i + 1) * PW], T["LH%d" % t][:, k * PW:(k + 1) * PW])
                                           for i, c in enumerate(targets)])
    g.wait_ge(T.sem.sent, R * len(eng) * (2 if core in helpers else 1))


def _emit(ops, g, T):
    queue = {"v": g.vector, "s": g.scalar, "p": g.tensor, "g": g, "y": g.sync}
    wr, rd, bank, known, count = {}, {}, {}, {e: {} for e in queue}, {}
    marked = set()
    for o in ops:
        e = o["e"]
        if e == "ext":
            ev = (o["sem"], o["n"], {o["sem"]: o["n"]})
            for k in o["w"]:
                wr[k], rd[k] = ev, []
            continue
        deps = []
        for k in o["r"]:
            if k in wr:
                deps.append(wr[k])
        for k in o["w"]:
            deps += rd.get(k, [])
            if k in wr:
                deps.append(wr[k])
        for k in o["b"]:
            deps += [ev for e2, ev in bank.get(k, {}).items() if e2 != e]
        need = {}
        for ev in deps:
            if known[e].get(ev[0], 0) < ev[1] and (ev[0] not in need or need[ev[0]][1] < ev[1]):
                need[ev[0]] = ev
        waits = []
        for ev in need.values():
            if not any(z is not ev and z[2].get(ev[0], 0) >= ev[1] for z in need.values()):
                waits.append((ev[0], ev[1]))
        for ev in need.values():
            for k, v in ev[2].items():
                if known[e].get(k, 0) < v:
                    known[e][k] = v
        for w in waits:
            marked.add(w)
        o["waits"] = waits
        key = o["sem"] if o["sem"] else e
        count[key] = count.get(key, 0) + (16 if o["sem"] else 1)
        val = o["n"] if o["n"] else count[key]
        clock = dict(known[e])
        clock[key] = val
        ev = (key, val, clock)
        o["ev"] = (key, count[key])
        for k in o["r"]:
            rd.setdefault(k, []).append(ev)
        for k in o["w"]:
            wr[k], rd[k] = ev, []
        for k in o["b"]:
            bank.setdefault(k, {})[e] = ev
    number = {}
    for e in queue:
        for i, w in enumerate(sorted(w for w in marked if w[0] == e)):
            number[w] = i + 1
    for o in ops:
        if o["e"] == "ext":
            continue
        q = queue[o["e"]]
        for w in o["waits"]:
            if w in number:
                q.wait_ge(T.sem["q" + w[0]], number[w])
            else:
                q.wait_ge(T.sem[w[0]], w[1])
        ins = o["f"]()
        if o["sem"]:
            ins.then_inc(T.sem[o["sem"]], 16)
        elif o["ev"] in number:
            ins.then_inc(T.sem["q" + o["e"]], 1)


def _weave(ops, plans):
    made = []
    for plan in plans:
        steps = []
        for fn, *args in plan:
            start = len(ops)
            fn(*args)
            steps.append(ops[start:])
            del ops[start:]
        made.append(steps)
    pending = {k for steps in made for s in steps for o in s for k in o["w"]}
    full, reads = set(), {}
    while any(made):
        for steps in made:
            if not steps:
                continue
            s = steps[0]
            wrote = {k for o in s for k in o["w"]}
            banks = {k for o in s for k in o["b"]}
            on_p = s[0]["e"] == "p"
            if any(k in pending and k not in wrote for o in s for k in o["r"]) or any((k in full) == on_p for k in banks):
                continue
            ops.extend(steps.pop(0))
            pending -= wrote
            for k in banks:
                if on_p and any(o.get("stop") for o in s if k in o["b"]):
                    full.add(k)
                    reads[k] = max(o.get("stop", 0) for o in s)
                elif not on_p:
                    reads[k] -= 1
                    if not reads[k]:
                        full.discard(k)
            break
        else:
            raise ValueError("the queues' orders contradict one another")


def rank_program(g, core, T, topo):
    planes = _layout(T, topo)
    if T.rank_of(core) is None:
        for c in planes:
            if core in planes[c][2] + planes[c][3]:
                helper_program(g, core, c, T, topo, planes)
        return
    mine, other, helpers, plain = planes[core]
    me, rank = mine.index(core), T.rank_of(core)
    V, S, P = g.vector, g.scalar, g.tensor
    ops = []
    sent = [0]

    def op(e, f, r=(), w=(), b=(), sem=None, n=0):
        ops.append({"e": e, "f": f, "r": list(r), "w": list(w), "b": list(b), "sem": sem, "n": n})

    def write(engines, items, r):
        op("g", lambda: _write(g, T, topo, core, engines, items), r)
        sent[0] += len(engines)

    def ext(sem, n, w):
        ops.append({"e": "ext", "sem": sem, "n": n, "w": list(w)})

    def ts(out, in0, s1, s2, o0, o1, r, w, b=()):
        if o1 is None:
            op("v", lambda: V.tensor_scalar(out, in0, s1, None, o0), r, w, b)
        else:
            op("v", lambda: V.tensor_scalar(out, in0, s1, s2, o0, o1), r, w, b)

    def tt(out, in0, in1, o, r, w, b=()):
        op("v", lambda: V.tensor_tensor(out, in0, in1, o), r, w, b)

    def cp(out, in_, r, w, b=()):
        op("v", lambda: V.tensor_copy(out, in_), r, w, b)

    def ms(out, c, w):
        op("v", lambda: V.memset(out, c), (), w)

    def scan(out, d0, d1, o0, o1, r, w, b=()):
        op("v", lambda: V.tensor_tensor_scan(out, d0, d1, 0.0, o0, o1), r, w, b)

    def act(out, in_, func, r, w, b=(), **kw):
        op("s", lambda: S.activation(out, in_, func, **kw), r, w, b)

    def mm(bank, out, lhsT, rhs, start, stop, r):
        op("p", lambda: P.matmul(out, lhsT, rhs, start, bool(stop)), r, (), [bank])
        ops[-1]["stop"] = int(stop)

    def iota(out, pat, cm, w, fl=True):
        if fl:
            op("g", lambda: g.iota(out, pat, 0, cm, allow_small_or_imprecise_dtypes=True), (), w)
        else:
            op("g", lambda: g.iota(out, pat, 0, cm), (), w)

    def dma(e, out, in_, sem, r=(), w=(), n=0):
        q = g.sync if e == "y" else g.scalar
        op(e, lambda: q.dma_start(out, in_), r, w, (), sem, n)

    MTK = ["MT%d" % c for c in range(8)]
    XRK = ["XR%d" % i for i in range(16)]
    BDK = [["BD%d%d" % (k, i) for i in range(8)] for k in range(2)]
    PM = [[T.P00, T.P01], [T.P10, T.P11]]
    NM = [[T.N00, T.N01], [T.N10, T.N11]]
    MUK = ["MU%d" % i for i in range(4)]
    NX = 16 * QX
    XO, YO = 16 * NX, 32 * NX
    XYK = ["XY%d" % i for i in range(16)]
    CYK = ["CY%d" % i for i in range(4)]
    HK = [["K1"], ["K2", "K3"]]
    CLASS_OF = 4.0 - 255.5 / 512

    dma("s", T.A0[:], T.a0[:], "d_a0", w=["A0"])
    dma("y", T.MIX[:, 0:1024], T.mix[:], "d_mix", w=["MIX"])
    dma("s", T.S0[:], T.s0[:], "d_s0", w=["S0"])
    dma("s", T.FR[:, 0:256], T.fr[:, 0:256], "d_fr0", w=["FR0"])
    dma("s", T.MIX[:, 1024:1028], T.mix[:, 0:4], "d_mw", w=["MIXW"])
    for i in range(4):
        dma("y", T.MU[:, 1024 * i:1024 * i + 1024], T.mu[:, 1024 * i:1024 * i + 1024], "d_mu%d" % i, w=[MUK[i]])
    dma("y", T.FR[:, 256:768], T.fr[:, 256:768], "d_fr1", w=["FR1", "FR2"])

    iota(T.PI[:], [[0, 1]], 1, ["PI"], False)
    iota(T.DD[:], [[-1, 128]], 1, ["DD"])
    iota(T.R16[:], [[1, 16]], 0, ["R16"])
    iota(T.U4R[:], [[0, 2], [16, 8]], 0, ["U4R"])
    iota(T.KA[:], [[0, 8], [1, 16]], 0, ["KA"])
    op("g", lambda: g.iota(T.LOI[:], [[1, 16], [16, 2], [0, 2]], NX, 0), (), ["LOI"])
    ms(T.ONES[:], 1.0, ["ONES"])
    ms(T.ZB[0:32, :], 192.0 / 32, ["ZBa"])
    ms(T.ZB[32:64, :], 1.0 / 128 / 32, ["ZBb"])
    ms(T.SW[:], 0.0, ["SW"])
    ones = T.ONES[:, 0:128]
    act(T.M3[0:64, :], T.ONES[0:64, 0:128], F.Identity, ["ONES"], ["M3"], scale=-3.0 / 64)
    act(T.OC[0:32, :], T.ONES[0:32, 0:32], F.Identity, ["ONES"], ["OCa"], scale=192.0 / 32)
    act(T.OC[32:64, :], T.ONES[32:64, 0:32], F.Identity, ["ONES"], ["OCb"], scale=-255.0 / 512 / 32)
    for t in range(R):
        act(T["NC%d" % t][:, 4 * rank:4 * rank + 4], T.ONES[:, 0:4], F.Identity, ["ONES"], ["NCz", "NC%d0" % t, "NC%d1" % t], scale=0.0)

    def fill(name, value, w):
        n = 1
        for k in SCRATCH[name][1][1:]:
            n *= k
        op("g", lambda: g.iota(T[name][:], [[0, n]], value, 0, allow_small_or_imprecise_dtypes=True), (), w)

    def keep(out, in_, pat, cmp, base, cm, r, w):
        op("g", lambda: g.affine_select(out, in_, pat, cmp, 0.0, base, cm), r, w)

    keep(T.ID[:], ones, [[-1, 128]], A.is_equal, 0, 1, ["ONES"], ["ID"])

    iota(T.TB[0:64, 0:256], [[0, 8], [-1, 16], [-16, 2]], 0, ["TB0"])
    for name, value, keys in (("ZR", 0.0, ["ZR"]), ("SS", 1.0, ["SS"]), ("C260", 260.0, ["C260"])):
        act(T[name][:], ones, F.Identity, ["ONES"], keys, scale=value)
    act(T.BL[:], T.ONES[:, 0:48], F.Identity, ["ONES"], ["BL0", "BL1", "BL2"])

    def late_constants():
        iota(T.TB[0:64, 256:320], [[0, 2], [-1, 32]], 0, ["TB1"])
        fill("SP", -16000000, ["SP"])
        keep(T.SP[:], T.SP[:], [[0, 8], [1, 32]], A.is_equal, 0, 0, ["SP"], ["SP"])
        for i in range(16):
            keep(T.XR[:, XO + i::16], T.XT[:], [[0, 64]], A.is_equal, 0, 0, ["XT%d" % q for q in range(4)], [XYK[i]])
        fill("EW0", 0, ["EW0"])
        fill("EW1", 0, ["EW1"])
        for sign in (1, -1):
            for l in (1, 2):
                w, name = 16 << l, "L%dB" % l
                src = "M16" if sign == 1 else name
                keep(T[name][:], T[src][:], [[-sign * w, 128 // w], [0, w]], A.is_ge, 0 if sign == 1 else w - 1, sign, [src], [name])
            for l in range(3):
                w, part, key = 1 << l, T.BL[:, 16 * l:16 * l + 16], ["BL%d" % l]
                keep(part, part, [[-16 * sign, 2], [-w * sign, 8 // w], [0, w]], A.is_ge,
                     -32 * me if sign == 1 else w - 1 + 32 * me, sign, key, key)
        keep(T.SS[:], T.SS[:], [[0, PW], [1, 4]], A.is_gt, 0, 0, ["SS"], ["SS"])
        iota(T.KE[:], [[1, 16], [0, 16]], 0, ["KE"])

    def heights():
        ts(T.LEV[:], T.M16[:], -96.0, 99.0, A.mult, A.add, ["M16"], ["LEV"])
        tt(T.L1B[:], T.L1B[:], T.L2B[:], A.add, ["L1B", "L2B"], ["L1B"])
        ts(T.EX[:], T.KE[:], icol, None, A.is_equal, None, ["KE", "CF"], ["EX"])
        for name in ("ID", "L1B"):
            tt(T.LEV[:], T.LEV[:], T[name][:], A.subtract, ["LEV", name], ["LEV"])

    def tree_constants():
        act(T.ID64[:], T.ID[:], F.Identity, ["ID"], ["ID64"], scale=1.0 / 64)
        op("g", lambda: g.iota(T.M192[0:64, :], [[0, 128]], -3, 0, allow_small_or_imprecise_dtypes=True), (), ["M192"])

    ts(T.CI[:, 3:4], T.PI[:], 4, None, A.arith_shift_right, None, ["PI"], ["CI3"])
    ts(T.CI[:, 4:5], T.PI[:], 15, None, A.bitwise_and, None, ["PI"], ["CI4"])
    ts(T.CI[:, 5:6], T.PI[:], 4, 1, A.arith_shift_right, A.bitwise_and, ["PI"], ["CI5"])
    cp(T.CF[:, 3:6], T.CI[:, 3:6], ["CI3", "CI4", "CI5"], ["CF"])
    gcol, icol, par1, par0 = T.CF[:, 3:4], T.CF[:, 4:5], T.CF[:, 5:6], T.CF[:, 6:7]
    ts(par0, par1, -1.0, 1.0, A.mult, A.add, ["CF"], ["par0"])
    ts(T.BI[:], T.R16[:, 0:8], gcol, None, A.is_equal, None, ["R16", "CF"], ["BI"])
    ts(T.OH[:], T.R16[:], icol, None, A.is_equal, None, ["R16", "CF"], ["OH"])
    ts(T.J64[:], T.R16[:], icol, 64.0, A.is_equal, A.mult, ["R16", "CF"], ["J64"])
    for c2 in (1, 0):
        for g2 in range(2):
            ts(PM[g2][c2][:], T.DD[:], 16.0 * (c2 - g2), par1 if c2 else par0, A.is_equal, A.mult,
               ["DD", "CF", "par0"] if c2 == 0 else ["DD", "CF"], ["PM%d%d" % (g2, c2)])
            act(NM[g2][c2][:], PM[g2][c2][:], F.Identity, ["PM%d%d" % (g2, c2)], ["NM%d%d" % (g2, c2)], scale=-1.0)
    ts(T.SW[:, 15:143:16], T.BI[:], -2048.0, None, A.mult, None, ["BI"], ["SW"])
    ts(T.U4[:], T.U4R[:], icol, 4096.0, A.add, A.mult, ["U4R", "CF"], ["U4"])
    ts(T.M16[:], T.KA[:], icol, None, A.is_equal, None, ["KA", "CF"], ["M16"])
    cp(T.XL[:], T.LOI[:], ["LOI"], ["XL"])

    def bias_bank(z):
        mm(z, T[z][:], T.ZB[0:64, :], T.ONES[0:64, :], True, False, ["ONES", "ZBa", "ZBb"])

    def expand(ks, on_v):
        c0, c1 = 4 * ks[0], 4 * ks[-1] + 4
        for gp in range(8):
            out, src = T.BD[:, c0:c1, 16 * gp:16 * gp + 16], T.ATS[:, 16 * c0:16 * c1]
            r, w = ["ATS%d" % k for k in ks] + ["BI"], [BDK[k][gp] for k in ks]
            if gp < on_v:
                ts(out, src, T.BI[:, gp:gp + 1], None, A.mult, None, r, w)
            else:
                act(out, src, F.Identity, r, w, scale=T.BI[:, gp:gp + 1])

    def xrep(t, which, eng):
        src = T.FR[:, 256 * t:256 * t + NX]
        for i in which:
            if eng == "v":
                ts(T.XR[:, i:XO:16], src, -1.0, -192.0, A.mult, A.add, ["FR%d" % t], [XRK[i]])
            elif eng == "g":
                keep(T.XR[:, i:XO:16], T.X192[:, 0:NX], [[0, NX]], A.is_equal, 0, 0, ["X192"], [XRK[i]])
            else:
                act(T.XR[:, i:XO:16], src, F.Identity, ["FR%d" % t], [XRK[i]], bias=-192.0, scale=-1.0)

    def xrep_late(t):
        act(T.XR[:, XO:XO + 1024], T.FR[:, 256 * t:256 * t + 256].indirect(T.XL[:]), F.Identity, ["FR%d" % t, "XL"], XYK,
            bias=-192.0, scale=-1.0)

    def x192(t):
        act(T.X192[:], T.FR[:, 256 * t:256 * t + 256], F.Identity, ["FR%d" % t], ["X192"], bias=-192.0, scale=-1.0)

    def states(src, key):
        for h in range(2):
            ts(T.LS2[:, 16 * h:16 * h + 16], src[:, 0:16], float(h), None, A.add, None, [key], ["LS2%d" % h])

    def candidates(h):
        ts(T.WG[:, 256 * h:256 * h + 256], T.MIX[:, 0:1028].indirect(T.LS2[:, 16 * h:16 * h + 16]), -2048.0, None, A.add, None,
           ["MIX", "MIXW", "LS2%d" % h], ["WG%d" % h])

    def early_list():
        for h in range(2):
            ts(T.CAND[:, NX * h:NX * h + NX], T.WG[:, 256 * h:256 * h + NX], 2048.0, None, A.add, None, ["WG%d" % h], ["CAND%d" % h])

    def late_list():
        for k in range(4):
            o = 256 * (k % 2) + NX + 16 * (k // 2)
            ts(T.CAND[:, 2 * NX + k:512:4], T.WG[:, o:o + 16], 2048.0, None, A.add, None, ["WG%d" % (k % 2)], [CYK[k]])

    def turn_list():
        op("v", lambda: V.transpose(T.TT[:], T.WG[:]), ["WG0", "WG1"], ["TT"])

    def steps():
        for q2 in range(2):
            for h in range(2):
                o, b, n = 32 * q2, 8 * h, QX // 2
                for g2 in range(2):
                    r = ["TT", "PM%d%d" % (g2, q2), "NM%d%d" % (g2, q2)]
                    mm("Z2", T.Z2[:, 0:n, o + h:o + 32:2], PM[g2][q2][:], T.TT[:, b:b + n, g2, :], g2 == 0, False, r)
                    mm("Z2", T.Z2[:, 0:n, o + h:o + 32 - h:2], NM[g2][q2][:], T.TT[:, 8 - b:8 - b + n, g2, h:16], False, g2 == 1, r)
                o += 16 * h
                for g2 in range(2):
                    r = ["TT", "PM%d%d" % (g2, q2), "NM%d%d" % (g2, q2)]
                    mm("Z2", T.Z2[:, n, o:o + 16], PM[g2][q2][:], T.TT[:, b + n, g2, :], g2 == 0, False, r)
                    if h == 0:
                        mm("Z2", T.Z2[:, n, o + 15:o + 16], NM[g2][q2][:], T.TT[:, 8 + n, g2, 0:1], False, False, r)
                    mm("Z2", T.Z2[:, n, o:o + 15], NM[g2][q2][:], T.TT[:, b + n, g2, 1:16], False, g2 == 1, r)
        ops[-1]["w"], ops[-1]["stop"] = ["TW"], 3

    def key_start(k, n):
        o = 256 if k == "K3" else 0
        mm(k, T[k][:, 0:32 * n], T.ONES[0:64, 0:128], T.TB[0:64, o:o + 32 * n], True, False, ["ONES", "TB0", "TB1"])

    op("v", lambda: V.transpose(T.TA[:], T.A0[:]), ["A0"], ["TA"])
    for c in range(8):
        for g2 in range(2):
            o = 32 * (c // 2) + 16 * g2
            mm("Z1", T.Z1[:, 16 * c:16 * c + 16], PM[g2][c % 2][:], T.TA[:, o:o + 16], g2 == 0, g2 == 1, ["TA", "PM%d%d" % (g2, c % 2)])
    bias_bank("K3")
    bias_bank("Z2")
    cp(T.SF[:], T.S0[:], ["S0"], ["SF"])
    states(T.S0, "S0")
    x192(0)
    xrep(0, range(0, 4), "v")
    xrep(0, range(4, 10), "g")
    xrep(0, range(10, 12), "s")
    ts(T.ATS[:], T.Z1[:, 0:128], 1.0 / 64, None, A.mult, None, [], ["ATS0", "ATS1"], ["Z1"])
    expand((0, 1), 6)
    xrep(0, range(12, 16), "v")
    for k in range(4):
        o = NX + 16 * (k // 2)
        act(T.XT[:, k::4], T.X192[:, o:o + 16], F.Copy, ["X192"], ["XT%d" % k])
    late_constants()
    candidates(0)
    candidates(1)
    early_list()
    turn_list()
    late_list()

    for t in range(R):
        last = t == R - 1
        NC = T["NC%d" % t]
        zbank = {0: "Z2", 3: "K3", 6: "Z2", 1: "Z0", 2: "Z1", 4: "K1", 5: "K2", 7: "Z0"}
        vplan = {0: [("d", 0)], 3: [("d", 3), ("c", 1), ("c", 2)], 6: [("d", 6), ("c", 4)], 7: [("c", 5), ("c", 7)]}
        SCL, order = [1, 2, 4, 5, 7], (1, 0, 2, 3, 4, 5, 6, 7)
        if t == 0:
            zbank = {0: "Z0", 1: "Z1", 2: "Z0", 3: "K3", 4: "Z1", 5: "Z0", 6: "Z1", 7: "Z2"}
            vplan = {4: [("d", 3), ("c", 0), ("c", 1), ("c", 2)], 6: [("d", 7), ("c", 4), ("c", 5), ("c", 6)]}
            SCL, order = [0, 1, 2, 4, 5, 6], (0, 1, 2, 3, 4, 5, 7, 6)
        for c in order:
            z = zbank[c]
            if c == 5 and t:
                bias_bank(zbank[6])
            mm(z, T[z][:], T.BD[:, c, :], T.MU[:, 512 * c:512 * c + 512], c in SCL, True, BDK[c // 4] + ["MU%d" % (c // 2)])
            if c in SCL:
                act(T.MT[:, 512 * c:512 * c + 512], T[z][:], F.Identity, [], [MTK[c]], [z], bias=192.0 + 1.0 / 128)
            for kind, d in vplan.get(c, []):
                dst = T.MT[:, 512 * d:512 * d + 512]
                if kind == "d":
                    zd = zbank[d]
                    ts(dst, T[zd][:], 184.0, 199.0, A.max, A.min, [], [MTK[d]], [zd])
                else:
                    ts(dst, dst, 184.0, 199.0, A.max, A.min, [MTK[d]], [MTK[d]])

        key_start("K1", 8)
        key_start("K2", 6)

        def own(h, q, z, n=2):
            b, keys = QX * h + q, ["D%d_%d" % (h, k) for k in range(q, q + n)]
            mc = T.D[:, 256 * b:256 * (b + n)]
            act(mc, T.MT[:, 0:4096].indirect(T.CAND[:, 16 * b:16 * (b + n)]), F.Identity, MTK + ["CAND%d" % h], keys)

        def own_sub(h, q, z, n=2):
            b, keys = QX * h + q, ["D%d_%d" % (h, k) for k in range(q, q + n)]
            mc = T.D[:, 256 * b:256 * (b + n)]
            mm(z, T[z][:, 0:256 * n], T.ID[:], T.XR[:, 256 * q:256 * (q + n)], True, False, ["ID"] + XRK)
            mm(z, T[z][:, 0:256 * n], T.ID[:], mc, False, True, ["ID"] + keys)

        def own_square(h, q, z, n=2):
            b = QX * h + q
            act(T.SQ[:, b:b + n], T[z][:, 0:256 * n], F.Square, [], ["SQ%d" % k for k in range(b, b + n)], [z])

        def gather(h, q0, q1):
            b0, b1 = QX * h + q0, QX * h + q1
            tt(T.D[:, 256 * b0:256 * b1], T.MT[:, 0:4096].indirect(T.CAND[:, 16 * b0:16 * b1]),
               T.XR[:, 256 * q0:256 * q1], A.add, MTK + XRK + ["CAND%d" % h], ["D%d_%d" % (h, q) for q in range(q0, q1)])

        def square(h, q0, q1):
            b0, b1 = QX * h + q0, QX * h + q1
            act(T.SQ[:, b0:b1], T.D[:, 256 * b0:256 * b1], F.Square, ["D%d_%d" % (h, q) for q in range(q0, q1)],
                ["SQ%d" % b for b in range(b0, b1)])

        def add(h, q0, q1, stop=False):
            b0, b1 = QX * h + q0, QX * h + q1
            k, o = ("K1", 0) if q0 < 8 else ("K2", 8)
            for j in range(16):
                mm(k, T[k][:, 32 * (q0 - o) + h:32 * (q1 - o):2], T.SW[:, 15 - j:143 - j], T.SQ[:, b0:b1, j, :], False,
                   2 * (stop and j == 15), ["SW"] + ["SQ%d" % b for b in range(b0, b1)])

        def late_gather(j0, j1):
            a, b = 64 * j0, 64 * j1
            tt(T.D[:, YO + a:YO + b], T.MT[:, 0:4096].indirect(T.CAND[:, 2 * NX + 4 * j0:2 * NX + 4 * j1]),
               T.XR[:, XO + a:XO + b], A.add, MTK + CYK + XYK, ["DY%d" % j for j in range(j0, j1)])

        def late_square(j0, j1):
            a, b = 64 * j0, 64 * j1
            act(T.SQY[:, a:b], T.D[:, YO + a:YO + b], F.Square, ["DY%d" % j for j in range(j0, j1)], ["SY%d" % j for j in range(j0, j1)])

        def late_add(j0, j1):
            for j in range(j0, j1):
                mm("K3", T.K3[:, 0:64], T.SW[:, 15 - j:143 - j], T.SQY[:, 64 * j:64 * j + 64], False, 2 * (j == 15), ["SW", "SY%d" % j])

        def pick(step, k, q0, q1):
            a, b, keys = 32 * q0, 32 * q1, T[k][:, 0:32 * (q1 - q0)]
            if step == 0:
                scan(T.R1[:, a:b], T.SP[:, 0:b - a], keys, A.add, A.max, ["SP"], ["R1" + k], [k])
            elif step == 1:
                tt(T.NM[:, a:b], keys, T.R1[:, a:b], A.not_equal, ["R1" + k], ["NM" + k], [k])
            else:
                for n in range(q0 // 2, q1 // 2):
                    part = slice(64 * n, 64 * n + 64)
                    scan(T.R2[:, part], T.NM[:, part], T.Z2[:, n, :], A.mult, A.add, ["NM" + k, "TW"],
                         ["R2" + k if 2 * n + 2 == q1 else "R2%d" % n], ["Z2"])

        def sums_lists(k, q0, q1):
            r = ["R2" + n for n in k.split()]
            wf, s8 = T.R2[:, 32 * q0 + 31:32 * q1:32], slice(q0, q1)
            ts(T.W16[:, s8], wf, 2048.0, None, A.add, None, r, ["W16" + n for n in k.split()])
            tt(T.SCF[:, s8], wf, T.U4[:, s8], A.add, r + ["U4"], ["SCF" + k])
            ts(T.CL16[:, s8], wf, 1.0 / 512, CLASS_OF, A.mult, A.add, r, ["CL16" + n for n in k.split()])

        def sums_gather(k, q0, q1):
            s8, u = slice(q0, q1), slice(16 * q0, 16 * q1)
            w = ["W16" + n for n in k.split()]
            if last:
                cp(T.NE[:, u], T.MU[:, 0:4096].indirect(T.W16[:, s8]), MUK + w, ["NE" + k])
            else:
                tt(T.NE[:, u], T.MT[:, 0:4096].indirect(T.W16[:, s8]), T.X192[:, u], A.add, MTK + w + ["X192"], ["NE" + k])
            ts(T.SC16[:, s8], T.SCF[:, s8], 1.0 / 512, CLASS_OF, A.mult, A.add, ["SCF" + k], ["SC16" + k])

        def sums_scatter(k, q0, q1):
            s8, u, h = slice(q0, q1), slice(16 * q0, 16 * q1), q0 // 8
            cp(T["EW%d" % h][:, 0:1024].indirect(T.SC16[:, s8]), T.NE[:, u], ["NE" + k, "SC16" + k],
               ["EW%d" % h] + ["EW" + n for n in k.split()])

        def sums_gather_s(k, q0, q1):
            src, keys = (T.MU, MUK) if last else (T.MT, MTK)
            act(T.NE[:, 16 * q0:16 * q1], src[:, 0:4096].indirect(T.W16[:, q0:q1]), F.Identity, keys + ["W16" + k], ["NE" + k])

        def sums_places(k, q0, q1):
            ts(T.SC16[:, q0:q1], T.SCF[:, q0:q1], 1.0 / 512, CLASS_OF, A.mult, A.add, ["SCF" + k], ["SC16" + k])

        def sums_scatter_s(k, q0, q1):
            if last:
                return sums_scatter(k, q0, q1)
            s8, u, h = slice(q0, q1), slice(16 * q0, 16 * q1), q0 // 8
            tt(T["EW%d" % h][:, 0:1024].indirect(T.SC16[:, s8]), T.NE[:, u], T.X192[:, u], A.add, ["NE" + k, "SC16" + k, "X192"],
               ["EW%d" % h, "EW" + k])

        def sums_side(h):
            s8, u = slice(8 * h, 8 * h + 8), slice(128 * h, 128 * h + 128)
            src, keys = (T.MT, MTK) if last else (T.MU, MUK)
            act(T.MW[:, u], src[:, 0:4096].indirect(T.W16[:, s8]), F.Identity, keys + ["W16" + k for k in HK[h]], ["MW%d" % h])

        def sums_count(h):
            s8, u = slice(8 * h, 8 * h + 8), slice(128 * h, 128 * h + 128)
            act(T.FN[:, u], T.OH[:, 0:16].indirect(T.CL16[:, s8]), F.Identity, ["OH"] + ["CL16" + k for k in HK[h]],
                ["FN%d" % h, "NC%d%d" % (t, h)], accum_out=NC[:, 4 * rank + h:4 * rank + h + 1])

        def sums_plain(h):
            u, pz = slice(128 * h, 128 * h + 128), "Z1"
            if last:
                mm(pz, T[pz][:, 0:128], T.X192[:, u], T.ID[:], True, False, ["X192", "ID"])
            mm(pz, T[pz][:, 0:128], T.MW[:, u], T.ID[:], not last, True, ["MW%d" % h, "ID"])

        def sums_plain_copy(h):
            act(T.PT[:, 128 * h:128 * h + 128], T.Z1[:, 0:128], F.Copy, [], ["PT%d" % h], ["Z1"])

        def sums_turn(h, k):
            z, p = "ZT%d" % k, slice(64 * k, 64 * k + 64)
            for c in range(8):
                op("p", lambda c=c: P.transpose(T[z][:, 0:4, 16 * c:16 * c + 16], T["EW%d" % h][p, c::8], T.ID[p, p]),
                   ["EW%d" % h, "ID"] + ["EW" + n for n in HK[h]], ["ZT%d%d" % (h, k)] if c == 7 else [], [z])
                ops[-1]["stop"] = 1

        def sums_copy(h, k, eng):
            out, z = T["ET%d" % h][:, 4 * k:4 * k + 4, :], "ZT%d" % k
            if eng == "v":
                cp(out, T[z][:, 0:4, :], ["ZT%d%d" % (h, k)], ["ET%d%d" % (h, k)], [z])
            else:
                act(out, T[z][:, 0:4, :], F.Copy, ["ZT%d%d" % (h, k)], ["ET%d%d" % (h, k)], [z])

        def sums_add(h, k):
            if k == h == 0:
                mm("Z0", T.Z0[:, 0:128], T.ONES[0:32, 0:128], T.ZR[0:32, :], True, False, ["ONES", "ZR"])
            for gp in range(4 * k, 4 * k + 4):
                o = PW * (gp // 2) + 16 * (gp % 2)
                mm("Z0", T.Z0[:, o:o + 16], T["ET%d" % h][:, gp, :],
                   T.PT[:, 128 * h + 16 * gp:128 * h + 16 * gp + 16], False, h == 1 and gp == 7,
                   ["PT%d" % h, "ET%d%d" % (h, gp // 4)])

        def move(step):
            if step == 0:
                ts(T.SI[:], T.R1[:, 31::32], -1.0 / 64, None, A.mult, None, ["R1" + k for k in HK[0] + HK[1]], ["SI"])
                ts(T.OUT[:, 16 * t:16 * t + 16], T.R2[:, 31::32], 2048.0, None, A.add, None, ["R2" + k for k in HK[0] + HK[1]], ["OUT%d" % t])
            elif step == 1:
                ts(T.HS[:], T.SI[:], 4, 1, A.arith_shift_right, A.bitwise_and, ["SI"], ["HS"])
            elif step == 2:
                tt(T.SF[:], T.SF[:], T.HS[:], A.add, ["SF", "HS"], ["SF"])
            elif not last:
                states(T.SF, "SF")
            else:
                cp(T.SI[:], T.SF[:], ["SF"], ["SI"])

        K1, K2, K3, K23 = ("K1", 0, 8), ("K2", 8, QX), ("K3", QX, 16), ("K2 K3", 8, 16)
        a, b, c, d = (0, 0, "Z1"), (0, 2, "K3"), (0, 8, "Z1"), (0, 10, "Z0", 1)
        on_v = [
            (gather, 0, 4, 8), (gather, 1, 0, 4), (gather, 1, 4, 8), (gather, 0, 11, 14), (gather, 1, 8, 10),
            (pick, 0, *K1), (gather, 1, 10, 12), (pick, 1, *K1), (gather, 1, 12, 14), (pick, 2, *K1),
            (late_gather, 0, 8), (sums_lists, *K1), (late_gather, 8, 12), (sums_gather, *K1), (late_gather, 12, 16), (pick, 0, *K2),
            (sums_scatter, *K1), (pick, 1, *K2), (pick, 0, *K3), (pick, 2, *K2), (pick, 1, *K3), (pick, 2, *K3),
            (sums_lists, *K23), (sums_gather, *K23), (move, 0), (sums_scatter, *K23), (move, 1), (move, 2),
            (sums_copy, 1, 0, "v"), (sums_copy, 1, 1, "v"), (move, 3)]
        on_s = [
            (own, *a), (own, *b), (own_square, *a), (square, 0, 4, 8), (own_square, *b), (square, 1, 0, 4), (square, 1, 4, 8),
            (own, *c), (own, *d), (square, 0, 11, 14), (own_square, *c), (own_square, *d), (square, 1, 8, 12), (square, 1, 12, 14),
            (late_square, 0, 8), (late_square, 8, 12), (late_square, 12, 16), (sums_side, 0), (sums_count, 0),
            (sums_copy, 0, 0, "s"), (sums_plain_copy, 0), (sums_count, 1), (sums_side, 1), (sums_copy, 0, 1, "s"),
            (sums_plain_copy, 1)]
        on_p = [
            (steps,), (own_sub, *a), (own_sub, *b), (add, 0, 4, 8), (add, 0, 0, 4),
            (key_start, "K3", 2), (add, 1, 0, 4), (add, 1, 4, 8, True), (own_sub, *c), (own_sub, *d), (add, 0, 11, 14), (add, 0, 8, 11),
            (add, 1, 8, 12), (add, 1, 12, 14, True), (late_add, 0, 8), (late_add, 8, 12), (late_add, 12, 16),
            (sums_turn, 0, 0), (sums_turn, 0, 1), (sums_plain, 0), (sums_add, 0, 0), (sums_plain, 1),
            (sums_turn, 1, 0), (sums_turn, 1, 1), (sums_add, 0, 1), (sums_add, 1, 0), (sums_add, 1, 1)]
        _weave(ops, [on_v, on_s, on_p])
        Pt, LD, LH, DL = T["P%d" % t], T["LD%d" % t], T["LH%d" % t], T["DL%d" % t]
        ts(Pt[:], T.Z0[:, 0:4 * PW], -1.0, 32768.0, A.mult, A.add, [], ["P%d" % t], ["Z0"])

        peers = [c for c in mine if c != core]
        eng, on_chip = topo.engines(core, peers[0]), topo.engines(core, helpers[0])
        ne = len(eng)
        counts, r = NC[:, 4 * rank:4 * rank + 4], ["NC%d0" % t, "NC%d1" % t, "NCz"]
        write([e for e in on_chip if e not in eng], [(c, "cin%d" % t, counts, T["HC%d" % t][:]) for c in helpers], r)
        write(eng, [(c, "cin%d" % t, counts, T["HC%d" % t][:]) for c in plain], r)
        ext("cn%d" % t, 4 * ne, ["NCr%d" % t])
        write(on_chip, [(c, "hin%d" % t, Pt[:, 2 * i * PW:(2 * i + 2) * PW], T["HB%d" % t][:]) for i, c in enumerate(helpers)], ["P%d" % t])
        for steps_on in ((1, 2), (3,)):
            ks = [(me + i) % 4 for i in steps_on]
            write(eng, [(mine[k], "rd%d" % t, Pt[:, k * PW:(k + 1) * PW], LD[:, me * PW:(me + 1) * PW]) for k in ks], ["P%d" % t])
        ext("rd%d" % t, 2 * ne, ["LD%d" % t])
        ext("rh%d" % t, 2 * ne, ["LH%d" % t])

        if t == 0:
            tree_constants()

        def choose(step):
            if step == 0:
                op("v", lambda nc=NC: V.tensor_reduce(T.NT[:, 0:1], nc[:], X.X, A.add), ["NC%d0" % t, "NC%d1" % t, "NCz", "NCr%d" % t], ["NT"])
                mm("K3", T.K3[0:48, 0:1], T.BL[:], T.NT[:, 0:1], True, True, ["BL0", "BL1", "BL2", "NT"])
            elif step == 1:
                ts(T.UB[0:48, :], T.C260[0:48, :], T.K3[0:48, 0:1], None, A.is_gt, None, ["C260"], ["UB"], ["K3"])
                mm("K3", T.K3[:, 0:256], T.UB[0:48, :], T.EX[0:48, :], True, True, ["UB", "EX"])
            else:
                for s in range(2):
                    tt(T.SEL[:, 128 * s:128 * s + 128], T.K3[:, 128 * s:128 * s + 128], T.LEV[:], A.is_ge, ["LEV"], ["SEL%d" % s], ["K3"])

        mm("Z0", T.Z0[:, 0:32], T.ONES[0:64, 0:128], T.OC[0:64, :], True, False, ["ONES", "OCa", "OCb"])
        if not last:
            mm("Z1", T.Z1[:, 0:128], T.ONES[0:64, 0:128], T.M3[0:64, :], True, False, ["ONES", "M3"])
            mm("Z1", T.Z1[:, 0:128], T.ID[:], T.ATS[:], False, False, ["ID", "ATS0", "ATS1"])
            x192(t + 1)
            xrep(t + 1, range(XV, 16), "s")
            xrep_late(t + 1)
        else:
            mm("Z1", T.Z1[:, 0:128], T.ONES[0:64, 0:128], T.M192[0:64, :], True, False, ["ONES", "M192"])
            for c in range(8):
                mm("Z1", T.Z1[:, 16 * c:16 * c + 16], T.BD[:, c, :], T.J64[:], False, False, BDK[c // 4] + ["J64"])

        def last_states():
            ts(T.SJ[:], T.SI[:], 1023, None, A.bitwise_and, None, ["SI"], ["SJ"])
            cp(T.OUT[:, 48:64], T.SJ[:], ["SJ"], ["OUT3"])

        def store(blk):
            op("v", lambda blk=blk: V.transpose(T.OUTT[:, 32 * blk:32 * blk + 32], T.OUT[:, 32 * blk:32 * blk + 32]),
               ["OUT%d" % (2 * blk), "OUT%d" % (2 * blk + 1)], ["OUTT%d" % blk])
            for gp in range(8):
                p0, o = 32 * (gp // 2), 32 * blk + 16 * (gp % 2)
                if blk == 0:
                    dma("y", T.yw[gp:gp + 1, 0:512], T.OUTT[p0:p0 + 32, o:o + 16], "d_o0", ["OUTT0"], ["o0"] if gp == 7 else [], 128)
                else:
                    dma("y", T.yw[gp:gp + 1, 512:768], T.OUTT[p0:p0 + 16, o:o + 16], "d_o1", ["OUTT1"], [], 256)
                    dma("y", T.ys[gp:gp + 1, :], T.OUTT[p0 + 16:p0 + 32, o:o + 16], "d_o1", ["OUTT1"], ["o1"] if gp == 7 else [], 256)
        def near(ks):
            for k in ks:
                src = Pt if k == me else LD
                ts(T.LA[:, k::4], src[:, k * PW:(k + 1) * PW], -32768.0, 1.0 / 256, A.add, A.mult,
                   ["P%d" % t if k == me else "LD%d" % t], ["LA%d" % k])

        def add_up(name):
            scan(T[name + "S"][:], T.SS[:], T[name][:], A.mult, A.add, ["SS"] + [name + "%d" % k for k in range(4)], [name + "S"])

        def far():
            for k in range(4):
                ts(T.LB[:, k::4], LH[:, k * PW:(k + 1) * PW], -32768.0, 1.0 / 256, A.add, A.mult, ["LH%d" % t], ["LB%d" % k])

        others = [k for k in range(4) if k != me]
        if t == 0:
            candidates(0)
            candidates(1)
            early_list()
            heights()
            near([me] + others)
            add_up("LA")
            choose(0)
            choose(1)
            far()
            choose(2)
        else:
            near([me])
            choose(0)
            last_states() if last else candidates(0)
            choose(1)
            store(1) if last else candidates(1)
            choose(2)
            near(others)
            far()
            add_up("LA")
        add_up("LB")
        for name in ("LAS", "LBS"):
            for s in range(2):
                mm("Z0", T.Z0[:, 16 * s:16 * s + 16], T.SEL[:, 128 * s:128 * s + 128], T[name][:, 64 * s + 3:64 * s + 64:4],
                   False, name == "LBS" and s == 1, ["SEL%d" % s, name])
        own_d = DL[:, 32 * me:32 * me + 32]
        ts(own_d, T.Z0[:, 0:32], 190.0, 194.0, A.max, A.min, [], ["DLo%d" % t], ["Z0"])
        tr = [RemoteDMATransfer(dst_ids=[_dst(topo, c, core) for c in peers], dma_engine_mask=_mask(eng),
                                remote_sem=T.sem["ag%d" % t], srcs=[own_d], dsts=[own_d for c in peers])]
        sent[0] += ne
        op("g", lambda tr=tr: g.remote_dma_fused(tr, local_sem=T.sem.sent), ["DLo%d" % t])
        ext("ag%d" % t, 3 * ne, ["DLr%d" % t])
        if not last:
            for h in range(2):
                fill("EW%d" % h, 0, ["EW%d" % h])
            if t:
                early_list()
                store(0)
            turn_list()
            late_list()
            xrep(t + 1, range(0, XV), "v")
            bias_bank("Z2")
            bias_bank("K3")
            mm("Z1", T.Z1[:, 0:128], DL[:], T.ID64[:], False, True, ["DLo%d" % t, "DLr%d" % t, "ID64"])
            for k in range(2):
                half = slice(64 * k, 64 * k + 64)
                ts(T.ATS[:, half], T.Z1[:, half], -127.0 / 64, 127.0 / 64, A.max, A.min, [], ["ATS%d" % k], ["Z1"])
            expand((0,), 6)
            expand((1,), 8)
        else:
            mm("Z1", T.Z1[:, 0:128], DL[:], T.ID[:], False, True, ["DLo%d" % t, "DLr%d" % t, "ID"])
            ts(T.YA[:], T.Z1[:, 0:128], -127.0, 127.0, A.max, A.min, [], ["YA"], ["Z1"])
            dma("y", T.ya[:], T.YA[:], "d_ya", ["YA"], ["ya"])
    op("g", lambda: g.wait_ge(T.sem.sent, sent[0]), ["o0", "o1", "ya"])
    _emit(ops, g, T)
